import numpy as np
import ml_dtypes


def mxq(x, axis, fmt="e4m3"):
    dtype, down = {"e4m3": (ml_dtypes.float8_e4m3fn, 7), "e5m2": (ml_dtypes.float8_e5m2, 14)}[fmt]
    v = np.moveaxis(np.asarray(x, np.float32).astype(ml_dtypes.bfloat16).astype(np.float64), axis, -1)
    blocks = v.reshape(v.shape[:-1] + (-1, 32))
    amax = np.abs(blocks).max(-1, keepdims=True)
    byte = np.maximum(np.where(amax > 0, np.frexp(amax)[1] - 1 + 127, 0) - down, 1)
    scale = np.exp2(byte - 127.0)
    codes = (blocks / scale).astype(np.float32).astype(dtype).astype(np.float64)
    return np.moveaxis((codes * scale).reshape(v.shape), -1, axis)


WIDE = False


def mx_kscale(k):
    if not WIDE:
        return np.ones(k)
    levels = np.array([10, -10, 5, -5, 0])
    if k % 512:
        return np.exp2(np.random.permutation(np.resize(levels, k // 32))).repeat(32)
    a = np.empty((k // 512, 16))
    for p in range(k // 512):
        a[p, :8] = np.random.permutation(np.resize(levels, 8))
        for g in range(8):
            far = levels[np.abs(levels - a[p, g]) >= 10]
            a[p, g + 8] = far[np.random.randint(len(far))]
    return np.exp2(a.ravel()).repeat(32)


BF16 = ml_dtypes.bfloat16


def bf(x):
    return np.asarray(x, np.float32).astype(BF16)


def f64(x):
    return np.asarray(x).astype(np.float64)


E2M1 = np.array([0.0, 0.5, 1.0, 1.5, 2.0, 3.0, 4.0, 6.0, -0.0, -0.5, -1.0, -1.5, -2.0, -3.0, -4.0, -6.0])


def pack_weight(w, fmt):
    k, n = w.shape
    w = f64(bf(w)).reshape(k // 32, 32, n)
    amax = np.abs(w).max(1)
    if fmt == "e4m3":
        byte = np.frexp(amax)[1] - 1 + 127 - 7
    else:
        mant, ex = np.frexp(amax / 6.0)
        byte = np.where(mant > 0.5, ex, ex - 1) + 127
    byte = np.clip(np.where(amax > 0, byte, 1), 1, 254)
    scaled = (w * np.exp2(127.0 - byte)[:, None, :]).reshape(k, n).astype(np.float32)
    by_word = np.ascontiguousarray(scaled.reshape(k // 512, 128, 4, n).transpose(0, 1, 3, 2))
    if fmt == "e4m3":
        words = by_word.astype(ml_dtypes.float8_e4m3fn).view(np.uint8)
    else:
        c = by_word.astype(ml_dtypes.float4_e2m1fn).view(np.uint8) & 0xF
        words = c[..., 0::2] | (c[..., 1::2] << 4)
    return np.ascontiguousarray(words), np.ascontiguousarray(byte.astype(np.uint8).reshape(k // 512, 16, n))


def unpack_weight(words, scales, fmt):
    g, p, n, _ = words.shape
    if fmt == "e4m3":
        vals = np.ascontiguousarray(words).view(ml_dtypes.float8_e4m3fn).astype(np.float64)
    else:
        nib = np.empty((g, p, n, 4), np.uint8)
        nib[..., 0::2] = words & 0xF
        nib[..., 1::2] = words >> 4
        vals = E2M1[nib]
    vals = vals * np.repeat(np.exp2(scales.astype(np.float64) - 127.0), 8, axis=1)[..., None]
    return vals.transpose(0, 1, 3, 2).reshape(g * 512, n)
def pack4(w):
    words, scales = pack_weight(w, "e2m1")
    return words.reshape(words.shape[0], 128, -1), scales


def unpack4(words, scales):
    return unpack_weight(words.reshape(words.shape[0], 128, -1, 2), scales, "e2m1")


S, F, C, D = 2048, 1024, 512, 2048


def draw0():
    s, t = mx_kscale(F), mx_kscale(S)
    x = np.random.standard_normal((S, F)) * s
    w = 0.7 * np.random.standard_normal((F, C)) / np.sqrt(F) / s[:, None]
    base = 0.3 * np.random.standard_normal(C)
    ratio = np.exp(0.2 * np.random.standard_normal(S)) * t
    eps_words, eps_scales = pack4(np.random.standard_normal((S, D)) / np.sqrt(S) / t[:, None])
    return {"x": bf(x), "w": bf(w), "base": bf(base), "ratio": bf(ratio),
            "eps_words": eps_words, "eps_scales": eps_scales}


def core(x, w, base, ratio, eps_words, eps_scales):
    cost = mxq(f64(x), 1, "e4m3") @ mxq(f64(w), 0, "e4m3")
    weight = np.exp(f64(base) - cost) * f64(ratio)[:, None]
    eps = unpack4(eps_words, eps_scales)
    return mxq(weight, 0, "e4m3").T @ eps


def e4m3fn_bytes(y):
    return np.clip(np.asarray(y, np.float64), -448.0, 448.0).astype(np.float32).astype(ml_dtypes.float8_e4m3fn).view(np.uint8)


def e4m3fn_values(b):
    return np.asarray(b, np.uint8).view(ml_dtypes.float8_e4m3fn).astype(np.float64)


def setup_inputs():
    d = draw0()
    x0 = np.asarray(d['x']).astype(np.float64)
    s = (np.max(np.abs(x0), axis=(0,), keepdims=True) / 448.0).astype(np.float32)
    out = {}
    for k, v in d.items():
        if k == 'x':
            out['x_bytes'] = e4m3fn_bytes(x0 / s.astype(np.float64))
            out['x_scale'] = s
        else:
            out[k] = v
    return out


def reference(x_bytes, x_scale, w, base, ratio, eps_words, eps_scales):
    return core(e4m3fn_values(x_bytes) * x_scale.astype(np.float64), w, base, ratio, eps_words, eps_scales)

@@ -1,0 +1,359 @@
+from contextlib import ExitStack
+
+import concourse.mybir as mybir
+from concourse.masks import make_identity
+
+F32 = mybir.dt.float32
+BF16 = mybir.dt.bfloat16
+U32 = mybir.dt.uint32
+I32 = mybir.dt.int32
+U8 = mybir.dt.uint8
+FP8 = mybir.dt.float8_e4m3fn
+FP8X4 = mybir.dt.float8_e4m3fn_x4
+FP4X4 = mybir.dt.float4_e2m1fn_x4
+ALU = mybir.AluOpType
+ACT = mybir.ActivationFunctionType
+
+P = 128
+S, F, C, D = 2048, 1024, 512, 2048
+KP = 512
+NG = S // KP
+NQ = F // KP
+NT = 4
+NC = C // P
+NB = 512
+ND = D // NB
+
+POOLX = ((1, 3),)
+VMUL = ((2, 2), (2, 3), (3, 0), (3, 1), (3, 2), (3, 3))
+IW = ("pool", "scalar")
+FLOPS = 2 * S * F * C + 2 * C * S * D
+
+
+def tile_mppi_control_update_s13_kernel(tc, x_bytes, x_scale, w, base, ratio, eps_words, eps_scales, out):
+    nc = tc.nc
+    with ExitStack() as ctx:
+        sb = ctx.enter_context(tc.tile_pool(name="sb", bufs=1))
+        psum = ctx.enter_context(tc.psum_pool(name="psum", bufs=1))
+        ctx.enter_context(tc.manual_schedule())
+
+        def buf(tag, bufs, shape, dtype):
+            return sb.tile(shape, dtype, name=tag, tag=tag, bufs=bufs, align_bytes=64)
+
+        def bank(tag, shape):
+            return psum.tile(shape, F32, name=tag, tag=tag)
+
+        e_plane = buf("e_plane", 1, [P, NG, D], U8)
+        nc.vector.memset(e_plane[:].rearrange("p g n -> p (g n)").bitcast(I32), 0)
+        warm = buf("warm", 1, [P, 1], F32)
+        warm_out = buf("warm_out", 1, [P, 1], F32)
+        nc.vector.memset(warm[:], 0.0)
+
+        xs = buf("xs", 1, [P, NQ, 4], F32)
+        nc.scalar.dma_start(out=xs[:], in_=x_scale.rearrange("o (q p t) -> p (o q) t", p=P, t=4))
+        base_bf = buf("base_bf", 1, [P, NC], BF16)
+        nc.scalar.dma_start(out=base_bf[:], in_=base.rearrange("(p t) -> p t", t=NC))
+        nc.scalar.activation(out=warm_out[:], in_=warm[:], func=ACT.Exp)
+
+        ident = buf("ident", 1, [P, P], F32)
+        make_identity(nc, ident[:])
+
+        x_rows = x_bytes.rearrange("(g p t) k -> g p t k", p=P, t=NT)
+        xb = [buf("xb", NG, [P, NT, F], U8) for g in range(NG)]
+        w_rows = w.rearrange("(q p j) c -> q p j c", p=P, j=4)
+        w_raw = [buf("w_raw", NQ, [P, 4, C], BF16) for q in range(NQ)]
+        for h in (0, 2):
+            nc.sync.dma_start(out=xb[0][:, h : h + 2, :], in_=x_rows[0][:, h : h + 2, :])
+        xs_bc = buf("xs_bc", 1, [P, KP], F32)
+        nc.sync.dma_start(out=xs_bc[:], in_=x_scale.rearrange("o k -> (o k)")[KP:].partition_broadcast(P))
+        for q in range(NQ):
+            nc.sync.dma_start(out=w_raw[q][:], in_=w_rows[q])
+        for g in range(1, NG):
+            nc.sync.dma_start(out=xb[g][:], in_=x_rows[g])
+        ratio_bc = buf("ratio_bc", 1, [P, S], BF16)
+        nc.sync.dma_start(out=ratio_bc[:], in_=ratio.partition_broadcast(P))
+        e_rows = eps_scales.bitcast(I32).rearrange("g q n -> q g n")
+        for quad in range(4):
+            nc.sync.dma_start(
+                out=e_plane[32 * quad : 32 * quad + 4, :, :].bitcast(I32), in_=e_rows[4 * quad : 4 * quad + 4]
+            )
+        e_words = [buf("e_words", NG, [P, 2 * D], U8) for g in range(NG)]
+        for g in range(NG):
+            nc.sync.dma_start(out=e_words[g][:], in_=eps_words[g])
+
+        base_f = buf("base_f", 1, [P, NC], F32)
+        nc.vector.tensor_copy(out=base_f[:], in_=base_bf[:])
+
+        w_grouped, w_codes, w_scales = [], [], []
+        for q in range(NQ):
+            w_grouped.append(buf("w_grouped", NQ, [P, C, 4], BF16))
+            w_codes.append(buf("w_codes", NQ, [P, C], U32))
+            w_scales.append(buf("w_scales", NQ, [P, C], U8))
+
+        def interleave_w(q, cts):
+            engine = IW[q]
+            dst = w_grouped[q][:].rearrange("p (t m) j -> p t m j", t=NC)
+            src = w_raw[q][:].rearrange("p j (m t) -> p t m j", t=NC)
+            for ct in cts:
+                if engine == "pool":
+                    nc.gpsimd.tensor_scalar(
+                        out=dst[:, ct], in0=src[:, ct], scalar1=1.0, scalar2=0.0, op0=ALU.mult, op1=ALU.add
+                    )
+                elif engine == "scalar":
+                    nc.scalar.copy(out=dst[:, ct], in_=src[:, ct])
+                else:
+                    nc.vector.tensor_copy(out=dst[:, ct], in_=src[:, ct])
+
+        def quantise_w(q, half):
+            cols = slice(256 * half, 256 * (half + 1))
+            nc.vector.quantize_mx(
+                out=w_codes[q][:, cols].bitcast(FP8X4),
+                scales=w_scales[q][:, cols],
+                in_=w_grouped[q][:, cols, :].rearrange("p c j -> p (c j)"),
+            )
+
+        xp = {}
+        xf, xt, xg, x_codes, x_scales = {}, {}, {}, {}, {}
+        cost, ex, eb, wt, wg = {}, {}, {}, {}, {}
+        m_codes = buf("m_codes", 1, [P, NG, C], U32)
+        m_scales = buf("m_scales", 1, [P, NG, C], U8)
+
+        def cast(g, t, part=slice(0, F)):
+            if (g, t) not in xf:
+                xf[g, t] = buf("xf", 8, [P, F], BF16)
+            nc.scalar.copy(out=xf[g, t][:, part], in_=xb[g][:, t, part].bitcast(FP8))
+
+        def prescale_x(g, n, a):
+            if a == 0:
+                xp[g, n] = buf("xp", 3, [P, 2, 2, 2 * P], BF16)
+            if True:
+                nc.gpsimd.tensor_tensor(
+                    out=xp[g, n][:, a].rearrange("p u (i e) -> p u i e", e=2),
+                    in0=xf[g, n - 1 + a][:, KP:].rearrange("p (i u e) -> p u i e", u=2, e=2),
+                    in1=xs_bc[:].rearrange("p (i u e) -> p u i e", u=2, e=2),
+                    op=ALU.mult,
+                )
+
+        def turn_x(g, n):
+            h, q = divmod(n, NQ)
+            if n == 0:
+                for i in range(NQ):
+                    xg[g, i] = buf("xg", 2 * NQ, [P, KP, 4], BF16)
+            xt[g, n] = bank("xt%d" % (n % 2), [P, 2, 2 * P])
+            for a in range(2):
+                for u in range(2):
+                    if (g, n) in POOLX:
+                        src = xp[g, n][:, a, u].bitcast(F32)
+                    else:
+                        src = xf[g, 2 * h + a][:].bitcast(F32)[:, 256 * q + u : 256 * (q + 1) : 2]
+                    nc.tensor.transpose(xt[g, n][:, u, P * a : P * (a + 1)], src, ident[:])
+
+        def scale_x(g, n):
+            h, q = divmod(n, NQ)
+            rows = slice(2 * P * h, 2 * P * (h + 1))
+            if (g, n) in POOLX:
+                nc.scalar.copy(
+                    out=xg[g, q][:, rows, :].bitcast(F32), in_=xt[g, n][:].rearrange("p u r -> p r u")
+                )
+            else:
+                nc.vector.tensor_tensor(
+                    out=xg[g, q][:, rows, :].rearrange("p r (u e) -> p r u e", u=2),
+                    in0=xt[g, n][:].bitcast(BF16).rearrange("p u (r e) -> p r u e", e=2),
+                    in1=xs[:, q : q + 1, :].rearrange("p q (u e) -> p q u e", u=2).to_broadcast([P, 2 * P, 2, 2]),
+                    op=ALU.mult,
+                )
+
+        def quantise_x(g, q):
+            x_codes[g, q] = buf("x_codes", 2 * NQ, [P, KP], U32)
+            x_scales[g, q] = buf("x_scales", 2 * NQ, [P, KP], U8)
+            nc.vector.quantize_mx(
+                out=x_codes[g, q][:].bitcast(FP8X4),
+                scales=x_scales[g, q][:],
+                in_=xg[g, q][:].rearrange("p r j -> p (r j)"),
+            )
+
+        def product1(g, ct):
+            cost[g, ct] = bank("cost%d" % (ct % 2), [P, KP])
+            cols = slice(P * ct, P * (ct + 1))
+            for q in range(NQ):
+                nc.tensor.matmul_mx(
+                    out=cost[g, ct][:],
+                    lhsT=w_codes[q][:, cols].bitcast(FP8X4),
+                    lhsT_scale=w_scales[q][:, cols],
+                    rhs=x_codes[g, q][:].bitcast(FP8X4),
+                    rhs_scale=x_scales[g, q][:],
+                    start=(q == 0),
+                    stop=(q == NQ - 1),
+                )
+
+        def exponential(g, ct):
+            ex[g, ct] = buf("ex", 6, [P, KP], F32)
+            nc.scalar.activation(
+                out=ex[g, ct][:], in_=cost[g, ct][:], func=ACT.Exp, bias=base_f[:, ct : ct + 1], scale=-1.0
+            )
+
+        def times_ratio(g, ct):
+            engine = nc.vector if (g, ct) in VMUL else nc.gpsimd
+            eb[g, ct] = buf("eb", 8, [P, 2, 256], BF16)
+            engine.tensor_tensor(
+                out=eb[g, ct][:].rearrange("p u (i e) -> p u i e", e=2),
+                in0=ex[g, ct][:].rearrange("p (u e i) -> p u i e", u=2, e=2),
+                in1=ratio_bc[:, KP * g : KP * (g + 1)].rearrange("p (i u e) -> p u i e", u=2, e=2),
+                op=ALU.mult,
+            )
+
+        def turn_m(g, pair, tag):
+            wt[g, pair] = bank(tag, [P, 2, 2, P])
+            for a in range(2):
+                for u in range(2):
+                    nc.tensor.transpose(
+                        wt[g, pair][:, a, u, :], eb[g, 2 * pair + a][:, u, :].bitcast(F32), ident[:]
+                    )
+
+        def empty_m(g, pair):
+            if pair == 0:
+                wg[g] = buf("wg", 2, [P, C, 4], BF16)
+            nc.scalar.copy(
+                out=wg[g][:, 256 * pair : 256 * (pair + 1), :].bitcast(F32).rearrange("p (a c) u -> p a c u", a=2),
+                in_=wt[g, pair][:].rearrange("p a u c -> p a c u"),
+            )
+
+        def quantise_m(g, pair):
+            cols = slice(256 * pair, 256 * (pair + 1))
+            nc.vector.quantize_mx(
+                out=m_codes[:, g, cols].bitcast(FP8X4),
+                scales=m_scales[:, g, cols],
+                in_=wg[g][:, cols, :].rearrange("p c j -> p (c j)"),
+            )
+
+        acc = {}
+
+        def product2(o, g, tag):
+            ct, dt = divmod(o, ND)
+            if g == 0:
+                acc[o] = bank(tag, [P, NB])
+            cols = slice(P * ct, P * (ct + 1))
+            nc.tensor.matmul_mx(
+                out=acc[o][:],
+                lhsT=m_codes[:, g, cols].bitcast(FP8X4),
+                lhsT_scale=m_scales[:, g, cols],
+                rhs=e_words[g][:, 2 * NB * dt : 2 * NB * (dt + 1)].bitcast(FP4X4),
+                rhs_scale=e_plane[:, g, NB * dt : NB * (dt + 1)],
+                start=(g == 0),
+                stop=(g == NG - 1),
+            )
+
+        out_rows = out.rearrange("(p t) d -> t p d", t=NC)
+
+        def finish(o):
+            ct, dt = divmod(o, ND)
+            res = buf("res", 16, [P, NB], F32)
+            if o % 2 == 0:
+                nc.vector.tensor_copy(out=res[:], in_=acc[o][:])
+            else:
+                nc.scalar.copy(out=res[:], in_=acc[o][:])
+            nc.sync.dma_start(out=out_rows[ct][:, NB * dt : NB * (dt + 1)], in_=res[:])
+
+        HELD = {0: "acc0", 1: "acc1", 2: "acc2"}
+
+        def chain(g, ct):
+            product1(g, ct)
+            exponential(g, ct)
+
+        for t in range(NT):
+            cast(0, t)
+        interleave_w(0, (0, 1, 2, 3))
+        interleave_w(1, (0, 1, 2, 3))
+
+        for n in range(4):
+            turn_x(0, n)
+            scale_x(0, n)
+        for t in range(NT):
+            cast(1, t)
+        quantise_x(0, 0)
+        quantise_x(0, 1)
+        for s in range(1, NG):
+            for n in (1, 3):
+                if (s, n) in POOLX:
+                    prescale_x(s, n, 0)
+                    prescale_x(s, n, 1)
+            turn_x(s, 0)
+            turn_x(s, 1)
+            if s >= 2:
+                turn_m(s - 2, 0, "wt")
+            scale_x(s, 0)
+            if s == 1:
+                for q in range(NQ):
+                    quantise_w(q, 0)
+                    quantise_w(q, 1)
+            scale_x(s, 1)
+            chain(s - 1, 0)
+            if s >= 2:
+                empty_m(s - 2, 0)
+            chain(s - 1, 1)
+            times_ratio(s - 1, 0)
+            times_ratio(s - 1, 1)
+            if s + 1 < NG:
+                cast(s + 1, 0)
+                cast(s + 1, 1)
+            turn_x(s, 2)
+            turn_x(s, 3)
+            if s >= 2:
+                turn_m(s - 2, 1, "wt")
+                empty_m(s - 2, 1)
+            scale_x(s, 2)
+            scale_x(s, 3)
+            chain(s - 1, 2)
+            chain(s - 1, 3)
+            if s + 1 < NG:
+                cast(s + 1, 2)
+                cast(s + 1, 3)
+            times_ratio(s - 1, 2)
+            times_ratio(s - 1, 3)
+            if s >= 2:
+                quantise_m(s - 2, 0)
+            quantise_x(s, 0)
+            if s >= 2:
+                quantise_m(s - 2, 1)
+            quantise_x(s, 1)
+            if s >= 2:
+                for o in HELD:
+                    product2(o, s - 2, HELD[o])
+
+        last = NG - 1
+        chain(last, 0)
+        chain(last, 1)
+        turn_m(last - 1, 0, "xt0")
+        empty_m(last - 1, 0)
+        turn_m(last - 1, 1, "xt1")
+        empty_m(last - 1, 1)
+        times_ratio(last, 0)
+        chain(last, 2)
+        chain(last, 3)
+        times_ratio(last, 1)
+        quantise_m(last - 1, 0)
+        quantise_m(last - 1, 1)
+        times_ratio(last, 2)
+        times_ratio(last, 3)
+        tail = ("wt", "cost0", "cost1", "xt0", "xt1", "acc0", "acc1", "acc2", "wt", "cost0", "cost1", "xt0", "xt1")
+        product2(3, 0, "wt")
+        product2(3, 1, "wt")
+        for o in HELD:
+            product2(o, last - 1, HELD[o])
+        product2(3, last - 1, "wt")
+        turn_m(last, 0, "xt0")
+        empty_m(last, 0)
+        turn_m(last, 1, "xt1")
+        quantise_m(last, 0)
+        empty_m(last, 1)
+        quantise_m(last, 1)
+        for o in (4, 5):
+            for g in range(last):
+                product2(o, g, tail[o - 3])
+        for o in range(6):
+            product2(o, last, "")
+            finish(o)
+        for o in range(6, NC * ND):
+            for g in range(NG):
+                product2(o, g, tail[o - 3])
+            finish(o)

@@ -23,10 +23,8 @@ NT = 4
 NC = C // P
 NB = 512
 ND = D // NB
+HALF = KP // 2
 
-POOLX = ((1, 3),)
-VMUL = ((2, 2), (2, 3), (3, 0), (3, 1), (3, 2), (3, 3))
-IW = ("pool", "scalar")
 FLOPS = 2 * S * F * C + 2 * C * S * D
 
 
@@ -40,36 +38,30 @@ def tile_mppi_control_update_s13_kernel(tc, x_bytes, x_scale, w, base, ratio, ep
         def buf(tag, bufs, shape, dtype):
             return sb.tile(shape, dtype, name=tag, tag=tag, bufs=bufs, align_bytes=64)
 
-        def bank(tag, shape):
-            return psum.tile(shape, F32, name=tag, tag=tag)
-
-        e_plane = buf("e_plane", 1, [P, NG, D], U8)
-        nc.vector.memset(e_plane[:].rearrange("p g n -> p (g n)").bitcast(I32), 0)
-        warm = buf("warm", 1, [P, 1], F32)
-        warm_out = buf("warm_out", 1, [P, 1], F32)
-        nc.vector.memset(warm[:], 0.0)
+        def bank(number, shape):
+            return psum.tile(shape, F32, name="bank%d" % number, tag="bank%d" % number)
 
         xs = buf("xs", 1, [P, NQ, 4], F32)
-        nc.scalar.dma_start(out=xs[:], in_=x_scale.rearrange("o (q p t) -> p (o q) t", p=P, t=4))
+        nc.sync.dma_start(out=xs[:], in_=x_scale.rearrange("o (q p t) -> p (o q) t", p=P, t=4))
         base_bf = buf("base_bf", 1, [P, NC], BF16)
         nc.scalar.dma_start(out=base_bf[:], in_=base.rearrange("(p t) -> p t", t=NC))
-        nc.scalar.activation(out=warm_out[:], in_=warm[:], func=ACT.Exp)
 
         ident = buf("ident", 1, [P, P], F32)
         make_identity(nc, ident[:])
+        e_plane = buf("e_plane", 1, [P, NG, D], U8)
+        nc.vector.memset(e_plane[:].rearrange("p g n -> p (g n)").bitcast(I32), 0)
 
         x_rows = x_bytes.rearrange("(g p t) k -> g p t k", p=P, t=NT)
-        xb = [buf("xb", NG, [P, NT, F], U8) for g in range(NG)]
         w_rows = w.rearrange("(q p j) c -> q p j c", p=P, j=4)
+        x_first = [buf("x_first", NT, [P, F], U8) for t in range(NT)]
+        x_rest = [buf("x_rest", NG - 1, [P, NT, F], U8) for g in range(1, NG)]
         w_raw = [buf("w_raw", NQ, [P, 4, C], BF16) for q in range(NQ)]
-        for h in (0, 2):
-            nc.sync.dma_start(out=xb[0][:, h : h + 2, :], in_=x_rows[0][:, h : h + 2, :])
-        xs_bc = buf("xs_bc", 1, [P, KP], F32)
-        nc.sync.dma_start(out=xs_bc[:], in_=x_scale.rearrange("o k -> (o k)")[KP:].partition_broadcast(P))
         for q in range(NQ):
             nc.sync.dma_start(out=w_raw[q][:], in_=w_rows[q])
+            for t in (2 * q, 2 * q + 1):
+                nc.sync.dma_start(out=x_first[t][:], in_=x_rows[0][:, t, :])
         for g in range(1, NG):
-            nc.sync.dma_start(out=xb[g][:], in_=x_rows[g])
+            nc.sync.dma_start(out=x_rest[g - 1][:], in_=x_rows[g])
         ratio_bc = buf("ratio_bc", 1, [P, S], BF16)
         nc.sync.dma_start(out=ratio_bc[:], in_=ratio.partition_broadcast(P))
         e_rows = eps_scales.bitcast(I32).rearrange("g q n -> q g n")
@@ -81,99 +73,76 @@ def tile_mppi_control_update_s13_kernel(tc, x_bytes, x_scale, w, base, ratio, ep
         for g in range(NG):
             nc.sync.dma_start(out=e_words[g][:], in_=eps_words[g])
 
+        xs_all = buf("xs_all", 1, [P, F], F32)
+        for q in range(NQ):
+            spread = bank(4 + q, [P, 4, P])
+            for t in range(4):
+                nc.tensor.transpose(spread[:, t, :], xs[:, q, t : t + 1].to_broadcast([P, P]), ident[:])
+            dst = xs_all[:, KP * q : KP * (q + 1)].rearrange("m (p t) -> m p t", t=4)
+            src = spread[:].rearrange("m t p -> m p t")
+            nc.scalar.copy(out=dst, in_=src)
         base_f = buf("base_f", 1, [P, NC], F32)
         nc.vector.tensor_copy(out=base_f[:], in_=base_bf[:])
 
-        w_grouped, w_codes, w_scales = [], [], []
-        for q in range(NQ):
-            w_grouped.append(buf("w_grouped", NQ, [P, C, 4], BF16))
-            w_codes.append(buf("w_codes", NQ, [P, C], U32))
-            w_scales.append(buf("w_scales", NQ, [P, C], U8))
+        w_grouped = [buf("w_grouped", NQ, [P, C, 4], BF16) for q in range(NQ)]
+        w_codes = [buf("w_codes", NQ, [P, C], U32) for q in range(NQ)]
+        w_scales = [buf("w_scales", NQ, [P, C], U8) for q in range(NQ)]
 
-        def interleave_w(q, cts):
-            engine = IW[q]
+        def interleave_w(q, ct):
             dst = w_grouped[q][:].rearrange("p (t m) j -> p t m j", t=NC)
             src = w_raw[q][:].rearrange("p j (m t) -> p t m j", t=NC)
-            for ct in cts:
-                if engine == "pool":
-                    nc.gpsimd.tensor_scalar(
-                        out=dst[:, ct], in0=src[:, ct], scalar1=1.0, scalar2=0.0, op0=ALU.mult, op1=ALU.add
-                    )
-                elif engine == "scalar":
-                    nc.scalar.copy(out=dst[:, ct], in_=src[:, ct])
-                else:
-                    nc.vector.tensor_copy(out=dst[:, ct], in_=src[:, ct])
-
-        def quantise_w(q, half):
-            cols = slice(256 * half, 256 * (half + 1))
-            nc.vector.quantize_mx(
-                out=w_codes[q][:, cols].bitcast(FP8X4),
-                scales=w_scales[q][:, cols],
-                in_=w_grouped[q][:, cols, :].rearrange("p c j -> p (c j)"),
-            )
-
-        xp = {}
-        xf, xt, xg, x_codes, x_scales = {}, {}, {}, {}, {}
-        cost, ex, eb, wt, wg = {}, {}, {}, {}, {}
-        m_codes = buf("m_codes", 1, [P, NG, C], U32)
-        m_scales = buf("m_scales", 1, [P, NG, C], U8)
-
-        def cast(g, t, part=slice(0, F)):
-            if (g, t) not in xf:
-                xf[g, t] = buf("xf", 8, [P, F], BF16)
-            nc.scalar.copy(out=xf[g, t][:, part], in_=xb[g][:, t, part].bitcast(FP8))
-
-        def prescale_x(g, n, a):
-            if a == 0:
-                xp[g, n] = buf("xp", 3, [P, 2, 2, 2 * P], BF16)
-            if True:
-                nc.gpsimd.tensor_tensor(
-                    out=xp[g, n][:, a].rearrange("p u (i e) -> p u i e", e=2),
-                    in0=xf[g, n - 1 + a][:, KP:].rearrange("p (i u e) -> p u i e", u=2, e=2),
-                    in1=xs_bc[:].rearrange("p (i u e) -> p u i e", u=2, e=2),
-                    op=ALU.mult,
-                )
-
-        def turn_x(g, n):
-            h, q = divmod(n, NQ)
-            if n == 0:
-                for i in range(NQ):
-                    xg[g, i] = buf("xg", 2 * NQ, [P, KP, 4], BF16)
-            xt[g, n] = bank("xt%d" % (n % 2), [P, 2, 2 * P])
-            for a in range(2):
-                for u in range(2):
-                    if (g, n) in POOLX:
-                        src = xp[g, n][:, a, u].bitcast(F32)
-                    else:
-                        src = xf[g, 2 * h + a][:].bitcast(F32)[:, 256 * q + u : 256 * (q + 1) : 2]
-                    nc.tensor.transpose(xt[g, n][:, u, P * a : P * (a + 1)], src, ident[:])
-
-        def scale_x(g, n):
-            h, q = divmod(n, NQ)
-            rows = slice(2 * P * h, 2 * P * (h + 1))
-            if (g, n) in POOLX:
-                nc.scalar.copy(
-                    out=xg[g, q][:, rows, :].bitcast(F32), in_=xt[g, n][:].rearrange("p u r -> p r u")
-                )
+            if q == 0:
+                nc.vector.tensor_copy(out=dst[:, ct], in_=src[:, ct])
             else:
-                nc.vector.tensor_tensor(
-                    out=xg[g, q][:, rows, :].rearrange("p r (u e) -> p r u e", u=2),
-                    in0=xt[g, n][:].bitcast(BF16).rearrange("p u (r e) -> p r u e", e=2),
-                    in1=xs[:, q : q + 1, :].rearrange("p q (u e) -> p q u e", u=2).to_broadcast([P, 2 * P, 2, 2]),
-                    op=ALU.mult,
-                )
+                nc.scalar.copy(out=dst[:, ct], in_=src[:, ct])
 
-        def quantise_x(g, q):
-            x_codes[g, q] = buf("x_codes", 2 * NQ, [P, KP], U32)
-            x_scales[g, q] = buf("x_scales", 2 * NQ, [P, KP], U8)
+        def quantise_w(q):
             nc.vector.quantize_mx(
-                out=x_codes[g, q][:].bitcast(FP8X4),
-                scales=x_scales[g, q][:],
-                in_=xg[g, q][:].rearrange("p r j -> p (r j)"),
+                out=w_codes[q][:].bitcast(FP8X4),
+                scales=w_scales[q][:],
+                in_=w_grouped[q][:].rearrange("p c j -> p (c j)"),
             )
 
-        def product1(g, ct):
-            cost[g, ct] = bank("cost%d" % (ct % 2), [P, KP])
+        xf, xt, xg, x_codes, x_scales = {}, {}, {}, {}, {}
+        cost, ex, eb, wt, wg, acc = {}, {}, {}, {}, {}, {}
+        m_codes = [buf("m_codes", NC, [P, NG * P], U32) for ct in range(NC)]
+        m_scales = [buf("m_scales", NC, [P, NG * P], U8) for ct in range(NC)]
+
+        def scale_x(g, t):
+            xf[g, t] = buf("xf", 4, [P, F], BF16)
+            src = x_first[t][:] if g == 0 else x_rest[g - 1][:, t, :]
+            nc.vector.tensor_tensor(out=xf[g, t][:], in0=src.bitcast(FP8), in1=xs_all[:], op=ALU.mult)
+
+        def turn_x(g, t):
+            xt[g, t] = bank(t % 2, [P, NQ, 2, P])
+            words = xf[g, t][:].bitcast(F32)
+            for q in range(NQ):
+                for u in range(2):
+                    nc.tensor.transpose(xt[g, t][:, q, u, :], words[:, 256 * q + u : 256 * (q + 1) : 2], ident[:])
+
+        def empty_x(g, t):
+            h, a = divmod(t, 2)
+            if a == 0:
+                xg[g, h] = buf("xg", 3, [P, NQ, HALF, 4], BF16)
+            nc.scalar.copy(
+                out=xg[g, h][:, :, P * a : P * (a + 1), :].bitcast(F32),
+                in_=xt[g, t][:].rearrange("p q u r -> p q r u"),
+            )
+
+        def quantise_x(g, h):
+            cols = slice(HALF * h, HALF * (h + 1))
+            for q in range(NQ):
+                if h == 0:
+                    x_codes[g, q] = buf("x_codes", 2 * NQ, [P, KP], U32)
+                    x_scales[g, q] = buf("x_scales", 2 * NQ, [P, KP], U8)
+                nc.vector.quantize_mx(
+                    out=x_codes[g, q][:, cols].bitcast(FP8X4),
+                    scales=x_scales[g, q][:, cols],
+                    in_=xg[g, h][:, q].rearrange("p r j -> p (r j)"),
+                )
+
+        def product1(g, ct, number):
+            cost[g, ct] = bank(number, [P, KP])
             cols = slice(P * ct, P * (ct + 1))
             for q in range(NQ):
                 nc.tensor.matmul_mx(
@@ -185,58 +154,48 @@ def tile_mppi_control_update_s13_kernel(tc, x_bytes, x_scale, w, base, ratio, ep
                     start=(q == 0),
                     stop=(q == NQ - 1),
                 )
-
-        def exponential(g, ct):
-            ex[g, ct] = buf("ex", 6, [P, KP], F32)
+            ex[g, ct] = buf("ex", NG * NC, [P, KP], F32)
             nc.scalar.activation(
                 out=ex[g, ct][:], in_=cost[g, ct][:], func=ACT.Exp, bias=base_f[:, ct : ct + 1], scale=-1.0
             )
 
         def times_ratio(g, ct):
-            engine = nc.vector if (g, ct) in VMUL else nc.gpsimd
-            eb[g, ct] = buf("eb", 8, [P, 2, 256], BF16)
-            engine.tensor_tensor(
+            eb[g, ct] = buf("eb", 6, [P, 2, 256], BF16)
+            nc.vector.tensor_tensor(
                 out=eb[g, ct][:].rearrange("p u (i e) -> p u i e", e=2),
                 in0=ex[g, ct][:].rearrange("p (u e i) -> p u i e", u=2, e=2),
                 in1=ratio_bc[:, KP * g : KP * (g + 1)].rearrange("p (i u e) -> p u i e", u=2, e=2),
                 op=ALU.mult,
             )
 
-        def turn_m(g, pair, tag):
-            wt[g, pair] = bank(tag, [P, 2, 2, P])
-            for a in range(2):
+        def turn_m(gs, ct, number):
+            n = len(gs)
+            wt[gs, ct] = bank(number, [P, n, 2, P])
+            for a in range(n):
                 for u in range(2):
-                    nc.tensor.transpose(
-                        wt[g, pair][:, a, u, :], eb[g, 2 * pair + a][:, u, :].bitcast(F32), ident[:]
-                    )
-
-        def empty_m(g, pair):
-            if pair == 0:
-                wg[g] = buf("wg", 2, [P, C, 4], BF16)
+                    nc.tensor.transpose(wt[gs, ct][:, a, u, :], eb[gs[a], ct][:, u, :].bitcast(F32), ident[:])
+            wg[gs, ct] = buf("wg", 4, [P, n * P, 4], BF16)
             nc.scalar.copy(
-                out=wg[g][:, 256 * pair : 256 * (pair + 1), :].bitcast(F32).rearrange("p (a c) u -> p a c u", a=2),
-                in_=wt[g, pair][:].rearrange("p a u c -> p a c u"),
+                out=wg[gs, ct][:].bitcast(F32).rearrange("p (a c) u -> p a c u", a=n),
+                in_=wt[gs, ct][:].rearrange("p a u c -> p a c u"),
             )
 
-        def quantise_m(g, pair):
-            cols = slice(256 * pair, 256 * (pair + 1))
+        def quantise_m(gs, ct):
+            cols = slice(P * gs[0], P * (gs[-1] + 1))
             nc.vector.quantize_mx(
-                out=m_codes[:, g, cols].bitcast(FP8X4),
-                scales=m_scales[:, g, cols],
-                in_=wg[g][:, cols, :].rearrange("p c j -> p (c j)"),
+                out=m_codes[ct][:, cols].bitcast(FP8X4),
+                scales=m_scales[ct][:, cols],
+                in_=wg[gs, ct][:].rearrange("p c j -> p (c j)"),
             )
 
-        acc = {}
-
-        def product2(o, g, tag):
-            ct, dt = divmod(o, ND)
+        def product2(ct, dt, g, number):
             if g == 0:
-                acc[o] = bank(tag, [P, NB])
-            cols = slice(P * ct, P * (ct + 1))
+                acc[ct, dt] = bank(number, [P, NB])
+            cols = slice(P * g, P * (g + 1))
             nc.tensor.matmul_mx(
-                out=acc[o][:],
-                lhsT=m_codes[:, g, cols].bitcast(FP8X4),
-                lhsT_scale=m_scales[:, g, cols],
+                out=acc[ct, dt][:],
+                lhsT=m_codes[ct][:, cols].bitcast(FP8X4),
+                lhsT_scale=m_scales[ct][:, cols],
                 rhs=e_words[g][:, 2 * NB * dt : 2 * NB * (dt + 1)].bitcast(FP4X4),
                 rhs_scale=e_plane[:, g, NB * dt : NB * (dt + 1)],
                 start=(g == 0),
@@ -245,115 +204,94 @@ def tile_mppi_control_update_s13_kernel(tc, x_bytes, x_scale, w, base, ratio, ep
 
         out_rows = out.rearrange("(p t) d -> t p d", t=NC)
 
-        def finish(o):
-            ct, dt = divmod(o, ND)
-            res = buf("res", 16, [P, NB], F32)
-            if o % 2 == 0:
-                nc.vector.tensor_copy(out=res[:], in_=acc[o][:])
+        def finish(ct, dt):
+            res = buf("res", NC * ND, [P, NB], F32)
+            if ct >= 2 and dt % 2 == 0:
+                nc.vector.tensor_copy(out=res[:], in_=acc[ct, dt][:])
             else:
-                nc.scalar.copy(out=res[:], in_=acc[o][:])
+                nc.scalar.copy(out=res[:], in_=acc[ct, dt][:])
             nc.sync.dma_start(out=out_rows[ct][:, NB * dt : NB * (dt + 1)], in_=res[:])
 
-        HELD = {0: "acc0", 1: "acc1", 2: "acc2"}
+        def first_goals(g, dts):
+            for dt in dts:
+                product2(0, dt, g, 4 + dt)
 
-        def chain(g, ct):
-            product1(g, ct)
-            exponential(g, ct)
-
-        for t in range(NT):
-            cast(0, t)
-        interleave_w(0, (0, 1, 2, 3))
-        interleave_w(1, (0, 1, 2, 3))
-
-        for n in range(4):
-            turn_x(0, n)
-            scale_x(0, n)
-        for t in range(NT):
-            cast(1, t)
-        quantise_x(0, 0)
-        quantise_x(0, 1)
-        for s in range(1, NG):
-            for n in (1, 3):
-                if (s, n) in POOLX:
-                    prescale_x(s, n, 0)
-                    prescale_x(s, n, 1)
-            turn_x(s, 0)
-            turn_x(s, 1)
-            if s >= 2:
-                turn_m(s - 2, 0, "wt")
-            scale_x(s, 0)
-            if s == 1:
-                for q in range(NQ):
-                    quantise_w(q, 0)
-                    quantise_w(q, 1)
-            scale_x(s, 1)
-            chain(s - 1, 0)
-            if s >= 2:
-                empty_m(s - 2, 0)
-            chain(s - 1, 1)
-            times_ratio(s - 1, 0)
-            times_ratio(s - 1, 1)
-            if s + 1 < NG:
-                cast(s + 1, 0)
-                cast(s + 1, 1)
-            turn_x(s, 2)
-            turn_x(s, 3)
-            if s >= 2:
-                turn_m(s - 2, 1, "wt")
-                empty_m(s - 2, 1)
-            scale_x(s, 2)
-            scale_x(s, 3)
-            chain(s - 1, 2)
-            chain(s - 1, 3)
-            if s + 1 < NG:
-                cast(s + 1, 2)
-                cast(s + 1, 3)
-            times_ratio(s - 1, 2)
-            times_ratio(s - 1, 3)
-            if s >= 2:
-                quantise_m(s - 2, 0)
-            quantise_x(s, 0)
-            if s >= 2:
-                quantise_m(s - 2, 1)
-            quantise_x(s, 1)
-            if s >= 2:
-                for o in HELD:
-                    product2(o, s - 2, HELD[o])
+        def pair_x(g, h):
+            for t in (2 * h, 2 * h + 1):
+                turn_x(g, t)
+                empty_x(g, t)
+                if g == 0:
+                    interleave_w(1, t)
 
         last = NG - 1
-        chain(last, 0)
-        chain(last, 1)
-        turn_m(last - 1, 0, "xt0")
-        empty_m(last - 1, 0)
-        turn_m(last - 1, 1, "xt1")
-        empty_m(last - 1, 1)
+        for ct in range(NC):
+            interleave_w(0, ct)
+        for g in range(NG):
+            scale_x(g, 0)
+            scale_x(g, 1)
+            pair_x(g, 0)
+            if g == 1:
+                for q in range(NQ):
+                    quantise_w(q)
+            if g >= 1:
+                quantise_x(g - 1, 1)
+                product1(g - 1, 0, 3)
+            if g >= 2:
+                quantise_m((g - 2,), 0)
+                first_goals(g - 2, (0, 1))
+            if g >= 1:
+                product1(g - 1, 1, 2)
+            scale_x(g, 2)
+            scale_x(g, 3)
+            pair_x(g, 1)
+            if g >= 1:
+                times_ratio(g - 1, 0)
+                turn_m((g - 1,), 0, 3)
+            quantise_x(g, 0)
+            if g >= 1:
+                product1(g - 1, 2, 2)
+            if g >= 2:
+                first_goals(g - 2, (2, 3))
+            if g >= 1:
+                product1(g - 1, 3, 3)
+
+        early, late = (0, 1), (2, last)
+        times_ratio(0, 1)
+        times_ratio(1, 1)
+        quantise_x(last, 1)
+        quantise_m((last - 1,), 0)
+        product1(last, 0, 0)
+        product1(last, 1, 1)
+        first_goals(last - 1, range(ND))
+        times_ratio(2, 1)
         times_ratio(last, 0)
-        chain(last, 2)
-        chain(last, 3)
         times_ratio(last, 1)
-        quantise_m(last - 1, 0)
-        quantise_m(last - 1, 1)
-        times_ratio(last, 2)
-        times_ratio(last, 3)
-        tail = ("wt", "cost0", "cost1", "xt0", "xt1", "acc0", "acc1", "acc2", "wt", "cost0", "cost1", "xt0", "xt1")
-        product2(3, 0, "wt")
-        product2(3, 1, "wt")
-        for o in HELD:
-            product2(o, last - 1, HELD[o])
-        product2(3, last - 1, "wt")
-        turn_m(last, 0, "xt0")
-        empty_m(last, 0)
-        turn_m(last, 1, "xt1")
-        quantise_m(last, 0)
-        empty_m(last, 1)
-        quantise_m(last, 1)
-        for o in (4, 5):
-            for g in range(last):
-                product2(o, g, tail[o - 3])
-        for o in range(6):
-            product2(o, last, "")
-            finish(o)
-        for o in range(6, NC * ND):
-            for g in range(NG):
-                product2(o, g, tail[o - 3])
-            finish(o)
+        turn_m((last,), 0, 3)
+        turn_m(early, 1, 2)
+        product1(last, 2, 0)
+        product1(last, 3, 1)
+        quantise_m((last,), 0)
+        quantise_m(early, 1)
+        first_goals(last, range(ND))
+        turn_m(late, 1, 3)
+        for dt in range(ND):
+            finish(0, dt)
+        banks = (2, 0, 1, 4, 5, 6, 7, 0, 1, 4, 5, 6)
+        for ct in range(1, NC):
+            if ct == 1:
+                times_ratio(0, 2)
+                quantise_m(late, 1)
+                for g in range(1, NG):
+                    times_ratio(g, 2)
+            for dt in range(ND):
+                for g in range(NG):
+                    product2(ct, dt, g, banks[ND * (ct - 1) + dt])
+                if dt == 1 and ct + 1 < NC:
+                    turn_m(early, ct + 1, 3)
+                    turn_m(late, ct + 1, 2)
+                    quantise_m(early, ct + 1)
+                    quantise_m(late, ct + 1)
+                    if ct + 2 < NC:
+                        for g in range(NG):
+                            times_ratio(g, ct + 2)
+                finish(ct, dt)

@@ -38,16 +38,24 @@ def tile_mppi_control_update_s13_kernel(tc, x_bytes, x_scale, w, base, ratio, ep
         def buf(tag, bufs, shape, dtype):
             return sb.tile(shape, dtype, name=tag, tag=tag, bufs=bufs, align_bytes=64)
 
-        def bank(number, shape):
-            return psum.tile(shape, F32, name="bank%d" % number, tag="bank%d" % number)
+        def bank(number, shape, dtype=F32):
+            return psum.tile(shape, dtype, name="bank%d" % number, tag="bank%d" % number)
+
+        def copy_on(engine, dst, src):
+            if engine == "vector":
+                nc.vector.tensor_copy(out=dst, in_=src)
+            else:
+                nc.scalar.copy(out=dst, in_=src)
 
         xs = buf("xs", 1, [P, NQ, 4], F32)
         nc.sync.dma_start(out=xs[:], in_=x_scale.rearrange("o (q p t) -> p (o q) t", p=P, t=4))
-        base_bf = buf("base_bf", 1, [P, NC], BF16)
-        nc.scalar.dma_start(out=base_bf[:], in_=base.rearrange("(p t) -> p t", t=NC))
 
         ident = buf("ident", 1, [P, P], F32)
         make_identity(nc, ident[:])
+        ratio_row = buf("ratio_row", 1, [P, S], BF16)
+        nc.vector.memset(ratio_row[:].bitcast(I32), 0)
+        ones = buf("ones", 1, [P, P], BF16)
+        nc.vector.memset(ones[:], 1.0)
         e_plane = buf("e_plane", 1, [P, NG, D], U8)
         nc.vector.memset(e_plane[:].rearrange("p g n -> p (g n)").bitcast(I32), 0)
 
@@ -60,10 +68,12 @@ def tile_mppi_control_update_s13_kernel(tc, x_bytes, x_scale, w, base, ratio, ep
             nc.sync.dma_start(out=w_raw[q][:], in_=w_rows[q])
             for t in (2 * q, 2 * q + 1):
                 nc.sync.dma_start(out=x_first[t][:], in_=x_rows[0][:, t, :])
+            if q == 0:
+                nc.sync.dma_start(out=ratio_row[0:1, :], in_=ratio.rearrange("(o s) -> o s", o=1))
+        base_bf = buf("base_bf", 1, [P, NC], BF16)
+        nc.sync.dma_start(out=base_bf[:], in_=base.rearrange("(p t) -> p t", t=NC))
         for g in range(1, NG):
             nc.sync.dma_start(out=x_rest[g - 1][:], in_=x_rows[g])
-        ratio_bc = buf("ratio_bc", 1, [P, S], BF16)
-        nc.sync.dma_start(out=ratio_bc[:], in_=ratio.partition_broadcast(P))
         e_rows = eps_scales.bitcast(I32).rearrange("g q n -> q g n")
         for quad in range(4):
             nc.sync.dma_start(
@@ -80,21 +90,36 @@ def tile_mppi_control_update_s13_kernel(tc, x_bytes, x_scale, w, base, ratio, ep
                 nc.tensor.transpose(spread[:, t, :], xs[:, q, t : t + 1].to_broadcast([P, P]), ident[:])
             dst = xs_all[:, KP * q : KP * (q + 1)].rearrange("m (p t) -> m p t", t=4)
             src = spread[:].rearrange("m t p -> m p t")
-            nc.scalar.copy(out=dst, in_=src)
-        base_f = buf("base_f", 1, [P, NC], F32)
-        nc.vector.tensor_copy(out=base_f[:], in_=base_bf[:])
+            if q == 0:
+                nc.vector.tensor_copy(out=dst, in_=src)
+            else:
+                nc.scalar.activation(out=dst, in_=src, func=ACT.Copy)
+
+        ratio_all = buf("ratio_all", 1, [P, NG, KP], BF16)
+
+        def spread_ratio(pair):
+            spread = bank(6 + pair, [P, 2, KP], BF16)
+            for a in range(2):
+                g = 2 * pair + a
+                nc.tensor.matmul(
+                    spread[:, a, :], lhsT=ones[:], rhs=ratio_row[:, KP * g : KP * (g + 1)], start=True, stop=True
+                )
+            return spread
+
+        def empty_ratio(pair, spread):
+            nc.scalar.copy(
+                out=ratio_all[:, 2 * pair : 2 * pair + 2, :].bitcast(F32).rearrange("p a (u i) -> p a u i", u=2),
+                in_=spread[:].bitcast(F32).rearrange("p a (i u) -> p a u i", u=2),
+            )
 
         w_grouped = [buf("w_grouped", NQ, [P, C, 4], BF16) for q in range(NQ)]
         w_codes = [buf("w_codes", NQ, [P, C], U32) for q in range(NQ)]
         w_scales = [buf("w_scales", NQ, [P, C], U8) for q in range(NQ)]
 
-        def interleave_w(q, ct):
+        def interleave_w(q, ct, engine):
             dst = w_grouped[q][:].rearrange("p (t m) j -> p t m j", t=NC)
             src = w_raw[q][:].rearrange("p j (m t) -> p t m j", t=NC)
-            if q == 0:
-                nc.vector.tensor_copy(out=dst[:, ct], in_=src[:, ct])
-            else:
-                nc.scalar.copy(out=dst[:, ct], in_=src[:, ct])
+            copy_on(engine, dst[:, ct], src[:, ct])
 
         def quantise_w(q):
             nc.vector.quantize_mx(
@@ -108,63 +133,76 @@ def tile_mppi_control_update_s13_kernel(tc, x_bytes, x_scale, w, base, ratio, ep
         m_codes = [buf("m_codes", NC, [P, NG * P], U32) for ct in range(NC)]
         m_scales = [buf("m_scales", NC, [P, NG * P], U8) for ct in range(NC)]
 
-        def scale_x(g, t):
-            xf[g, t] = buf("xf", 4, [P, F], BF16)
+        def scale_x(j, a, parts=1):
+            g, t = divmod(2 * j + a, NT)
+            xf[j, a] = buf("xf", 4, [P, F], BF16)
             src = x_first[t][:] if g == 0 else x_rest[g - 1][:, t, :]
-            nc.vector.tensor_tensor(out=xf[g, t][:], in0=src.bitcast(FP8), in1=xs_all[:], op=ALU.mult)
+            for part in range(parts):
+                ks = slice(F // parts * part, F // parts * (part + 1))
+                nc.vector.tensor_tensor(
+                    out=xf[j, a][:, ks], in0=src[:, ks].bitcast(FP8), in1=xs_all[:, ks], op=ALU.mult
+                )
 
-        def turn_x(g, t):
-            xt[g, t] = bank(t % 2, [P, NQ, 2, P])
-            words = xf[g, t][:].bitcast(F32)
+        def turn_x(j, a):
+            xt[j, a] = bank(a, [P, NQ, 2, P])
+            words = xf[j, a][:].bitcast(F32)
             for q in range(NQ):
                 for u in range(2):
-                    nc.tensor.transpose(xt[g, t][:, q, u, :], words[:, 256 * q + u : 256 * (q + 1) : 2], ident[:])
+                    nc.tensor.transpose(xt[j, a][:, q, u, :], words[:, 256 * q + u : 256 * (q + 1) : 2], ident[:])
 
-        def empty_x(g, t):
-            h, a = divmod(t, 2)
+        def empty_x(j, a):
             if a == 0:
-                xg[g, h] = buf("xg", 3, [P, NQ, HALF, 4], BF16)
+                xg[j] = buf("xg", 3, [P, NQ, HALF, 4], BF16)
             nc.scalar.copy(
-                out=xg[g, h][:, :, P * a : P * (a + 1), :].bitcast(F32),
-                in_=xt[g, t][:].rearrange("p q u r -> p q r u"),
+                out=xg[j][:, :, P * a : P * (a + 1), :].bitcast(F32),
+                in_=xt[j, a][:].rearrange("p q u r -> p q r u"),
             )
 
-        def quantise_x(g, h):
-            cols = slice(HALF * h, HALF * (h + 1))
-            for q in range(NQ):
+        def quantise_x(j):
+            x_codes[j] = buf("x_codes", 3, [P, NQ * HALF], U32)
+            x_scales[j] = buf("x_scales", 3, [P, NQ * HALF], U8)
+            nc.vector.quantize_mx(
+                out=x_codes[j][:].bitcast(FP8X4),
+                scales=x_scales[j][:],
+                in_=xg[j][:].rearrange("p q r j -> p (q r j)"),
+            )
+
+        def product1(j, pair, number):
+            cost[j, pair] = bank(number, [P, 2, HALF])
+            for a in range(2):
+                cols = slice(P * (2 * pair + a), P * (2 * pair + a + 1))
+                for q in range(NQ):
+                    rows = slice(HALF * q, HALF * (q + 1))
+                    nc.tensor.matmul_mx(
+                        out=cost[j, pair][:, a, :],
+                        lhsT=w_codes[q][:, cols].bitcast(FP8X4),
+                        lhsT_scale=w_scales[q][:, cols],
+                        rhs=x_codes[j][:, rows].bitcast(FP8X4),
+                        rhs_scale=x_scales[j][:, rows],
+                        start=(q == 0),
+                        stop=(q == NQ - 1),
+                    )
+
+        def exponential(j, pair):
+            g, h = divmod(j, 2)
+            for a in range(2):
+                ct = 2 * pair + a
                 if h == 0:
-                    x_codes[g, q] = buf("x_codes", 2 * NQ, [P, KP], U32)
-                    x_scales[g, q] = buf("x_scales", 2 * NQ, [P, KP], U8)
-                nc.vector.quantize_mx(
-                    out=x_codes[g, q][:, cols].bitcast(FP8X4),
-                    scales=x_scales[g, q][:, cols],
-                    in_=xg[g, h][:, q].rearrange("p r j -> p (r j)"),
+                    ex[g, ct] = buf("ex", NG * NC, [P, KP], F32)
+                nc.scalar.activation(
+                    out=ex[g, ct][:, HALF * h : HALF * (h + 1)],
+                    in_=cost[j, pair][:, a, :],
+                    func=ACT.Exp,
+                    bias=base_bf[:, ct : ct + 1],
+                    scale=-1.0,
                 )
-
-        def product1(g, ct, number):
-            cost[g, ct] = bank(number, [P, KP])
-            cols = slice(P * ct, P * (ct + 1))
-            for q in range(NQ):
-                nc.tensor.matmul_mx(
-                    out=cost[g, ct][:],
-                    lhsT=w_codes[q][:, cols].bitcast(FP8X4),
-                    lhsT_scale=w_scales[q][:, cols],
-                    rhs=x_codes[g, q][:].bitcast(FP8X4),
-                    rhs_scale=x_scales[g, q][:],
-                    start=(q == 0),
-                    stop=(q == NQ - 1),
-                )
-            ex[g, ct] = buf("ex", NG * NC, [P, KP], F32)
-            nc.scalar.activation(
-                out=ex[g, ct][:], in_=cost[g, ct][:], func=ACT.Exp, bias=base_f[:, ct : ct + 1], scale=-1.0
-            )
 
         def times_ratio(g, ct):
-            eb[g, ct] = buf("eb", 6, [P, 2, 256], BF16)
+            eb[g, ct] = buf("eb", 8, [P, 2, 256], BF16)
             nc.vector.tensor_tensor(
                 out=eb[g, ct][:].rearrange("p u (i e) -> p u i e", e=2),
                 in0=ex[g, ct][:].rearrange("p (u e i) -> p u i e", u=2, e=2),
-                in1=ratio_bc[:, KP * g : KP * (g + 1)].rearrange("p (i u e) -> p u i e", u=2, e=2),
+                in1=ratio_all[:, g, :].rearrange("p (u i e) -> p u i e", u=2, e=2),
                 op=ALU.mult,
             )
 
@@ -174,10 +212,14 @@ def tile_mppi_control_update_s13_kernel(tc, x_bytes, x_scale, w, base, ratio, ep
             for a in range(n):
                 for u in range(2):
                     nc.tensor.transpose(wt[gs, ct][:, a, u, :], eb[gs[a], ct][:, u, :].bitcast(F32), ident[:])
+
+        def empty_m(gs, ct, engine):
+            n = len(gs)
             wg[gs, ct] = buf("wg", 4, [P, n * P, 4], BF16)
-            nc.scalar.copy(
-                out=wg[gs, ct][:].bitcast(F32).rearrange("p (a c) u -> p a c u", a=n),
-                in_=wt[gs, ct][:].rearrange("p a u c -> p a c u"),
+            copy_on(
+                engine,
+                wg[gs, ct][:].bitcast(F32).rearrange("p (a c) u -> p a c u", a=n),
+                wt[gs, ct][:].rearrange("p a u c -> p a c u"),
             )
 
         def quantise_m(gs, ct):
@@ -204,94 +246,113 @@ def tile_mppi_control_update_s13_kernel(tc, x_bytes, x_scale, w, base, ratio, ep
 
         out_rows = out.rearrange("(p t) d -> t p d", t=NC)
 
-        def finish(ct, dt):
+        def finish(ct, dt, engine):
             res = buf("res", NC * ND, [P, NB], F32)
-            if ct >= 2 and dt % 2 == 0:
-                nc.vector.tensor_copy(out=res[:], in_=acc[ct, dt][:])
-            else:
-                nc.scalar.copy(out=res[:], in_=acc[ct, dt][:])
+            copy_on(engine, res[:], acc[ct, dt][:])
             nc.sync.dma_start(out=out_rows[ct][:, NB * dt : NB * (dt + 1)], in_=res[:])
 
         def first_goals(g, dts):
             for dt in dts:
                 product2(0, dt, g, 4 + dt)
 
-        def pair_x(g, h):
-            for t in (2 * h, 2 * h + 1):
-                turn_x(g, t)
-                empty_x(g, t)
-                if g == 0:
-                    interleave_w(1, t)
+        def costs(j, pair, number):
+            product1(j, pair, number)
+            exponential(j, pair)
 
         last = NG - 1
-        for ct in range(NC):
-            interleave_w(0, ct)
-        for g in range(NG):
-            scale_x(g, 0)
-            scale_x(g, 1)
-            pair_x(g, 0)
-            if g == 1:
-                for q in range(NQ):
-                    quantise_w(q)
-            if g >= 1:
-                quantise_x(g - 1, 1)
-                product1(g - 1, 0, 3)
-            if g >= 2:
+        w_parts = [(q, ct) for q in range(NQ) for ct in range(NC)]
+        interleave_w(*w_parts[0], "vector")
+        for part in w_parts[1:4]:
+            interleave_w(*part, "scalar")
+        for j in range(2 * NG):
+            g, odd = divmod(j, 2)
+            scale_x(j, 0, NQ if j == 0 else 1)
+            if j == 1:
+                quantise_w(0)
+            if j == 2:
+                quantise_w(1)
+            if g >= 2 and not odd:
                 quantise_m((g - 2,), 0)
                 first_goals(g - 2, (0, 1))
-            if g >= 1:
-                product1(g - 1, 1, 2)
-            scale_x(g, 2)
-            scale_x(g, 3)
-            pair_x(g, 1)
-            if g >= 1:
+            scale_x(j, 1)
+            turn_x(j, 0)
+            if j == 0:
+                spread = [spread_ratio(0)]
+            empty_x(j, 0)
+            if j == 2:
+                costs(0, 0, 2)
+                costs(0, 1, 3)
+            if j == 0:
+                for part in w_parts[4:6]:
+                    interleave_w(*part, "scalar")
+            turn_x(j, 1)
+            if g >= 1 and odd:
                 times_ratio(g - 1, 0)
                 turn_m((g - 1,), 0, 3)
-            quantise_x(g, 0)
-            if g >= 1:
-                product1(g - 1, 2, 2)
-            if g >= 2:
-                first_goals(g - 2, (2, 3))
-            if g >= 1:
-                product1(g - 1, 3, 3)
+                empty_m((g - 1,), 0, "scalar")
+            empty_x(j, 1)
+            if j == 0:
+                for part in w_parts[6:]:
+                    interleave_w(*part, "scalar")
+            if j == 1:
+                spread.append(spread_ratio(1))
+                quantise_x(0)
+                empty_ratio(0, spread[0])
+            if j >= 2:
+                quantise_x(j - 1)
+                costs(j - 1, 0, 2)
+                if g >= 2 and not odd:
+                    first_goals(g - 2, (2, 3))
+                costs(j - 1, 1, 3)
+            if j == 3:
+                empty_ratio(1, spread[1])
 
         early, late = (0, 1), (2, last)
+        end = 2 * NG - 1
         times_ratio(0, 1)
         times_ratio(1, 1)
-        quantise_x(last, 1)
+        turn_m(early, 1, 0)
+        empty_m(early, 1, "scalar")
         quantise_m((last - 1,), 0)
-        product1(last, 0, 0)
-        product1(last, 1, 1)
-        first_goals(last - 1, range(ND))
+        quantise_x(end)
+        first_goals(last - 1, (0, 1))
+        costs(end, 0, 1)
+        costs(end, 1, 2)
+        first_goals(last - 1, (2, 3))
         times_ratio(2, 1)
+        times_ratio(0, 2)
+        quantise_m(early, 1)
+        times_ratio(1, 2)
         times_ratio(last, 0)
         times_ratio(last, 1)
-        turn_m((last,), 0, 3)
-        turn_m(early, 1, 2)
-        product1(last, 2, 0)
-        product1(last, 3, 1)
+        for g in early:
+            product2(1, 0, g, 0)
+        turn_m((last,), 0, 1)
+        turn_m(late, 1, 2)
+        empty_m((last,), 0, "scalar")
+        empty_m(late, 1, "scalar")
+        times_ratio(2, 2)
         quantise_m((last,), 0)
-        quantise_m(early, 1)
+        times_ratio(last, 2)
+        quantise_m(late, 1)
+        for g in early:
+            product2(1, 1, g, 3)
         first_goals(last, range(ND))
-        turn_m(late, 1, 3)
         for dt in range(ND):
-            finish(0, dt)
-        banks = (2, 0, 1, 4, 5, 6, 7, 0, 1, 4, 5, 6)
+            finish(0, dt, "scalar" if dt % 2 == 0 else "vector")
+        banks = (0, 3, 4, 5, 6, 7, 0, 3, 4, 5, 6, 7)
         for ct in range(1, NC):
-            if ct == 1:
-                times_ratio(0, 2)
-                quantise_m(late, 1)
-                for g in range(1, NG):
-                    times_ratio(g, 2)
             for dt in range(ND):
-                for g in range(NG):
+                for g in late if ct == 1 and dt < 2 else range(NG):
                     product2(ct, dt, g, banks[ND * (ct - 1) + dt])
                 if dt == 1 and ct + 1 < NC:
-                    turn_m(early, ct + 1, 3)
+                    turn_m(early, ct + 1, 1)
                     turn_m(late, ct + 1, 2)
+                    empty_m(early, ct + 1, "vector")
+                    empty_m(late, ct + 1, "scalar")
                     quantise_m(early, ct + 1)
                     quantise_m(late, ct + 1)
                     if ct + 2 < NC:
                         for g in range(NG):
                             times_ratio(g, ct + 2)
-                finish(ct, dt)
+                finish(ct, dt, "vector" if ct >= 2 and dt % 2 == 0 else "scalar")

@@ -56,6 +56,8 @@ def tile_mppi_control_update_s13_kernel(tc, x_bytes, x_scale, w, base, ratio, ep
         nc.vector.memset(ratio_row[:].bitcast(I32), 0)
         ones = buf("ones", 1, [P, P], BF16)
         nc.vector.memset(ones[:], 1.0)
+        ident_bf = buf("ident_bf", 1, [P, P], BF16)
+        nc.vector.tensor_copy(out=ident_bf[:], in_=ident[:])
         e_plane = buf("e_plane", 1, [P, NG, D], U8)
         nc.vector.memset(e_plane[:].rearrange("p g n -> p (g n)").bitcast(I32), 0)
 
@@ -68,8 +70,7 @@ def tile_mppi_control_update_s13_kernel(tc, x_bytes, x_scale, w, base, ratio, ep
             nc.sync.dma_start(out=w_raw[q][:], in_=w_rows[q])
             for t in (2 * q, 2 * q + 1):
                 nc.sync.dma_start(out=x_first[t][:], in_=x_rows[0][:, t, :])
-            if q == 0:
-                nc.sync.dma_start(out=ratio_row[0:1, :], in_=ratio.rearrange("(o s) -> o s", o=1))
+        nc.sync.dma_start(out=ratio_row[0:1, :], in_=ratio.rearrange("(o s) -> o s", o=1))
         base_bf = buf("base_bf", 1, [P, NC], BF16)
         nc.sync.dma_start(out=base_bf[:], in_=base.rearrange("(p t) -> p t", t=NC))
         for g in range(1, NG):
@@ -98,15 +99,12 @@ def tile_mppi_control_update_s13_kernel(tc, x_bytes, x_scale, w, base, ratio, ep
         ratio_all = buf("ratio_all", 1, [P, NG, KP], BF16)
 
         def spread_ratio(pair):
-            spread = bank(6 + pair, [P, 2, KP], BF16)
+            spread = bank(7, [P, 2, KP], BF16)
             for a in range(2):
                 g = 2 * pair + a
                 nc.tensor.matmul(
                     spread[:, a, :], lhsT=ones[:], rhs=ratio_row[:, KP * g : KP * (g + 1)], start=True, stop=True
                 )
-            return spread
-
-        def empty_ratio(pair, spread):
             nc.scalar.copy(
                 out=ratio_all[:, 2 * pair : 2 * pair + 2, :].bitcast(F32).rearrange("p a (u i) -> p a u i", u=2),
                 in_=spread[:].bitcast(F32).rearrange("p a (i u) -> p a u i", u=2),
@@ -116,16 +114,21 @@ def tile_mppi_control_update_s13_kernel(tc, x_bytes, x_scale, w, base, ratio, ep
         w_codes = [buf("w_codes", NQ, [P, C], U32) for q in range(NQ)]
         w_scales = [buf("w_scales", NQ, [P, C], U8) for q in range(NQ)]
 
-        def interleave_w(q, ct, engine):
-            dst = w_grouped[q][:].rearrange("p (t m) j -> p t m j", t=NC)
+        def interleave_w(q, pair, number):
             src = w_raw[q][:].rearrange("p j (m t) -> p t m j", t=NC)
-            copy_on(engine, dst[:, ct], src[:, ct])
+            mixed = bank(number, [P, 2, KP], BF16)
+            for a in range(2):
+                nc.tensor.matmul(mixed[:, a, :], lhsT=ident_bf[:], rhs=src[:, 2 * pair + a], start=True, stop=True)
+            nc.scalar.copy(
+                out=w_grouped[q][:, 2 * P * pair : 2 * P * (pair + 1), :].rearrange("p c j -> p (c j)"),
+                in_=mixed[:].rearrange("p a n -> p (a n)"),
+            )
 
-        def quantise_w(q):
+        def quantise_w(q, cols):
             nc.vector.quantize_mx(
-                out=w_codes[q][:].bitcast(FP8X4),
-                scales=w_scales[q][:],
-                in_=w_grouped[q][:].rearrange("p c j -> p (c j)"),
+                out=w_codes[q][:, cols].bitcast(FP8X4),
+                scales=w_scales[q][:, cols],
+                in_=w_grouped[q][:, cols, :].rearrange("p c j -> p (c j)"),
             )
 
         xf, xt, xg, x_codes, x_scales = {}, {}, {}, {}, {}
@@ -230,82 +233,75 @@ def tile_mppi_control_update_s13_kernel(tc, x_bytes, x_scale, w, base, ratio, ep
                 in_=wg[gs, ct][:].rearrange("p c j -> p (c j)"),
             )
 
-        def product2(ct, dt, g, number):
+        def product2(ct, ds, g, number):
             if g == 0:
-                acc[ct, dt] = bank(number, [P, NB])
+                acc[ct, ds.start] = bank(number, [P, ds.stop - ds.start])
             cols = slice(P * g, P * (g + 1))
             nc.tensor.matmul_mx(
-                out=acc[ct, dt][:],
+                out=acc[ct, ds.start][:],
                 lhsT=m_codes[ct][:, cols].bitcast(FP8X4),
                 lhsT_scale=m_scales[ct][:, cols],
-                rhs=e_words[g][:, 2 * NB * dt : 2 * NB * (dt + 1)].bitcast(FP4X4),
-                rhs_scale=e_plane[:, g, NB * dt : NB * (dt + 1)],
+                rhs=e_words[g][:, 2 * ds.start : 2 * ds.stop].bitcast(FP4X4),
+                rhs_scale=e_plane[:, g, ds],
                 start=(g == 0),
                 stop=(g == NG - 1),
             )
 
         out_rows = out.rearrange("(p t) d -> t p d", t=NC)
 
-        def finish(ct, dt, engine):
-            res = buf("res", NC * ND, [P, NB], F32)
-            copy_on(engine, res[:], acc[ct, dt][:])
-            nc.sync.dma_start(out=out_rows[ct][:, NB * dt : NB * (dt + 1)], in_=res[:])
+        def finish(ct, ds, engine):
+            res = buf("res", NC * ND + 3, [P, ds.stop - ds.start], F32)
+            copy_on(engine, res[:], acc[ct, ds.start][:])
+            nc.sync.dma_start(out=out_rows[ct][:, ds], in_=res[:])
+
+        wide = [slice(NB * dt, NB * (dt + 1)) for dt in range(ND)]
+        narrow = [slice(D - NB + P * n, D - NB + P * (n + 1)) for n in range(NB // P)]
 
         def first_goals(g, dts):
             for dt in dts:
-                product2(0, dt, g, 4 + dt)
+                product2(0, wide[dt], g, 4 + dt)
 
         def costs(j, pair, number):
             product1(j, pair, number)
             exponential(j, pair)
 
         last = NG - 1
-        w_parts = [(q, ct) for q in range(NQ) for ct in range(NC)]
-        interleave_w(*w_parts[0], "vector")
-        for part in w_parts[1:4]:
-            interleave_w(*part, "scalar")
+        for pair in range(2):
+            interleave_w(0, pair, 2 + pair)
         for j in range(2 * NG):
             g, odd = divmod(j, 2)
             scale_x(j, 0, NQ if j == 0 else 1)
             if j == 1:
-                quantise_w(0)
+                quantise_w(0, slice(0, C))
             if j == 2:
-                quantise_w(1)
+                quantise_w(1, slice(C // 2, C))
             if g >= 2 and not odd:
                 quantise_m((g - 2,), 0)
                 first_goals(g - 2, (0, 1))
             scale_x(j, 1)
             turn_x(j, 0)
-            if j == 0:
-                spread = [spread_ratio(0)]
             empty_x(j, 0)
-            if j == 2:
-                costs(0, 0, 2)
-                costs(0, 1, 3)
-            if j == 0:
-                for part in w_parts[4:6]:
-                    interleave_w(*part, "scalar")
+            if j < 2:
+                interleave_w(1, j, 4 + j)
+            if g == 1:
+                costs(j - 2, 1, 3)
             turn_x(j, 1)
             if g >= 1 and odd:
                 times_ratio(g - 1, 0)
-                turn_m((g - 1,), 0, 3)
+                turn_m((g - 1,), 0, 3 if g > 1 else 6)
                 empty_m((g - 1,), 0, "scalar")
             empty_x(j, 1)
-            if j == 0:
-                for part in w_parts[6:]:
-                    interleave_w(*part, "scalar")
             if j == 1:
-                spread.append(spread_ratio(1))
-                quantise_x(0)
-                empty_ratio(0, spread[0])
-            if j >= 2:
+                quantise_w(1, slice(0, C // 2))
+            if j >= 1:
                 quantise_x(j - 1)
                 costs(j - 1, 0, 2)
+                if j <= 2:
+                    spread_ratio(j - 1)
                 if g >= 2 and not odd:
                     first_goals(g - 2, (2, 3))
-                costs(j - 1, 1, 3)
-            if j == 3:
-                empty_ratio(1, spread[1])
+                if j >= 3:
+                    costs(j - 1, 1, 3)
 
         early, late = (0, 1), (2, last)
         end = 2 * NG - 1
@@ -326,7 +322,7 @@ def tile_mppi_control_update_s13_kernel(tc, x_bytes, x_scale, w, base, ratio, ep
         times_ratio(last, 0)
         times_ratio(last, 1)
         for g in early:
-            product2(1, 0, g, 0)
+            product2(1, wide[0], g, 0)
         turn_m((last,), 0, 1)
         turn_m(late, 1, 2)
         empty_m((last,), 0, "scalar")
@@ -336,15 +332,15 @@ def tile_mppi_control_update_s13_kernel(tc, x_bytes, x_scale, w, base, ratio, ep
         times_ratio(last, 2)
         quantise_m(late, 1)
         for g in early:
-            product2(1, 1, g, 3)
+            product2(1, wide[1], g, 3)
         first_goals(last, range(ND))
         for dt in range(ND):
-            finish(0, dt, "scalar" if dt % 2 == 0 else "vector")
-        banks = (0, 3, 4, 5, 6, 7, 0, 3, 4, 5, 6, 7)
+            finish(0, wide[dt], "scalar" if dt % 2 == 0 else "vector")
+        banks = (0, 3, 4, 5, 6, 7, 0, 3, 4, 5, 6)
         for ct in range(1, NC):
-            for dt in range(ND):
+            for dt in range(ND if ct + 1 < NC else ND - 1):
                 for g in late if ct == 1 and dt < 2 else range(NG):
-                    product2(ct, dt, g, banks[ND * (ct - 1) + dt])
+                    product2(ct, wide[dt], g, banks[ND * (ct - 1) + dt])
                 if dt == 1 and ct + 1 < NC:
                     turn_m(early, ct + 1, 1)
                     turn_m(late, ct + 1, 2)
@@ -355,4 +351,8 @@ def tile_mppi_control_update_s13_kernel(tc, x_bytes, x_scale, w, base, ratio, ep
                     if ct + 2 < NC:
                         for g in range(NG):
                             times_ratio(g, ct + 2)
-                finish(ct, dt, "vector" if ct >= 2 and dt % 2 == 0 else "scalar")
+                finish(ct, wide[dt], "vector" if ct >= 2 and dt % 2 == 0 else "scalar")
+        for n in range(NB // P):
+            for g in range(NG):
+                product2(NC - 1, narrow[n], g, n)
+            finish(NC - 1, narrow[n], "scalar" if n % 2 == 0 else "vector")

@@ -24,6 +24,7 @@ NC = C // P
 NB = 512
 ND = D // NB
 HALF = KP // 2
+XS_PARTS = 4
 
 FLOPS = 2 * S * F * C + 2 * C * S * D
 
@@ -47,8 +48,8 @@ def tile_mppi_control_update_s13_kernel(tc, x_bytes, x_scale, w, base, ratio, ep
             else:
                 nc.scalar.copy(out=dst, in_=src)
 
-        xs = buf("xs", 1, [P, NQ, 4], F32)
-        nc.sync.dma_start(out=xs[:], in_=x_scale.rearrange("o (q p t) -> p (o q) t", p=P, t=4))
+        xs = buf("xs", 1, [P, XS_PARTS, 2], F32)
+        nc.sync.dma_start(out=xs[:], in_=x_scale.rearrange("o (a p e) -> p (o a) e", p=P, e=2))
 
         ident = buf("ident", 1, [P, P], F32)
         make_identity(nc, ident[:])
@@ -66,13 +67,15 @@ def tile_mppi_control_update_s13_kernel(tc, x_bytes, x_scale, w, base, ratio, ep
         x_first = [buf("x_first", NT, [P, F], U8) for t in range(NT)]
         x_rest = [buf("x_rest", NG - 1, [P, NT, F], U8) for g in range(1, NG)]
         w_raw = [buf("w_raw", NQ, [P, 4, C], BF16) for q in range(NQ)]
-        for q in range(NQ):
-            nc.sync.dma_start(out=w_raw[q][:], in_=w_rows[q])
-            for t in (2 * q, 2 * q + 1):
-                nc.sync.dma_start(out=x_first[t][:], in_=x_rows[0][:, t, :])
+        for t in range(NT):
+            nc.sync.dma_start(out=x_first[t][:], in_=x_rows[0][:, t, :])
+            if t < NQ:
+                nc.sync.dma_start(out=w_raw[t][:], in_=w_rows[t])
         nc.sync.dma_start(out=ratio_row[0:1, :], in_=ratio.rearrange("(o s) -> o s", o=1))
         base_bf = buf("base_bf", 1, [P, NC], BF16)
-        nc.sync.dma_start(out=base_bf[:], in_=base.rearrange("(p t) -> p t", t=NC))
+        nc.sync.dma_start(
+            out=base_bf[:].rearrange("p (h e) -> p h e", e=2), in_=base.rearrange("(h p e) -> p h e", p=P, e=2)
+        )
         for g in range(1, NG):
             nc.sync.dma_start(out=x_rest[g - 1][:], in_=x_rows[g])
         e_rows = eps_scales.bitcast(I32).rearrange("g q n -> q g n")
@@ -85,13 +88,13 @@ def tile_mppi_control_update_s13_kernel(tc, x_bytes, x_scale, w, base, ratio, ep
             nc.sync.dma_start(out=e_words[g][:], in_=eps_words[g])
 
         xs_all = buf("xs_all", 1, [P, F], F32)
-        for q in range(NQ):
-            spread = bank(4 + q, [P, 4, P])
-            for t in range(4):
-                nc.tensor.transpose(spread[:, t, :], xs[:, q, t : t + 1].to_broadcast([P, P]), ident[:])
-            dst = xs_all[:, KP * q : KP * (q + 1)].rearrange("m (p t) -> m p t", t=4)
-            src = spread[:].rearrange("m t p -> m p t")
-            if q == 0:
+        for a in range(XS_PARTS):
+            spread = bank(4 + a, [P, 2, P])
+            for e in range(2):
+                nc.tensor.transpose(spread[:, e, :], xs[:, a, e : e + 1].to_broadcast([P, P]), ident[:])
+            dst = xs_all[:, 2 * P * a : 2 * P * (a + 1)].rearrange("m (p e) -> m p e", e=2)
+            src = spread[:].rearrange("m e p -> m p e")
+            if a == 0:
                 nc.vector.tensor_copy(out=dst, in_=src)
             else:
                 nc.scalar.activation(out=dst, in_=src, func=ACT.Copy)
@@ -115,14 +118,19 @@ def tile_mppi_control_update_s13_kernel(tc, x_bytes, x_scale, w, base, ratio, ep
         w_scales = [buf("w_scales", NQ, [P, C], U8) for q in range(NQ)]
 
         def interleave_w(q, pair, number):
-            src = w_raw[q][:].rearrange("p j (m t) -> p t m j", t=NC)
+            src = w_raw[q][:].rearrange("p j (h m e) -> p h e m j", m=P, e=2)
             mixed = bank(number, [P, 2, KP], BF16)
             for a in range(2):
-                nc.tensor.matmul(mixed[:, a, :], lhsT=ident_bf[:], rhs=src[:, 2 * pair + a], start=True, stop=True)
+                nc.tensor.matmul(mixed[:, a, :], lhsT=ident_bf[:], rhs=src[:, pair, a], start=True, stop=True)
             nc.scalar.copy(
                 out=w_grouped[q][:, 2 * P * pair : 2 * P * (pair + 1), :].rearrange("p c j -> p (c j)"),
                 in_=mixed[:].rearrange("p a n -> p (a n)"),
             )
+
+        def interleave_w_copy(q, pair):
+            src = w_raw[q][:].rearrange("p j (h m e) -> p h e m j", m=P, e=2)
+            dst = w_grouped[q][:].rearrange("p (h e m) j -> p h e m j", m=P, e=2)
+            nc.scalar.copy(out=dst[:, pair], in_=src[:, pair])
 
         def quantise_w(q, cols):
             nc.vector.quantize_mx(
@@ -201,7 +209,7 @@ def tile_mppi_control_update_s13_kernel(tc, x_bytes, x_scale, w, base, ratio, ep
                 )
 
         def times_ratio(g, ct):
-            eb[g, ct] = buf("eb", 8, [P, 2, 256], BF16)
+            eb[g, ct] = buf("eb", 10, [P, 2, 256], BF16)
             nc.vector.tensor_tensor(
                 out=eb[g, ct][:].rearrange("p u (i e) -> p u i e", e=2),
                 in0=ex[g, ct][:].rearrange("p (u e i) -> p u i e", u=2, e=2),
@@ -233,44 +241,44 @@ def tile_mppi_control_update_s13_kernel(tc, x_bytes, x_scale, w, base, ratio, ep
                 in_=wg[gs, ct][:].rearrange("p c j -> p (c j)"),
             )
 
-        def product2(ct, ds, g, number):
+        def product2(ct, dt, g, number):
             if g == 0:
-                acc[ct, ds.start] = bank(number, [P, ds.stop - ds.start])
+                acc[ct, dt] = bank(number, [P, NB])
             cols = slice(P * g, P * (g + 1))
             nc.tensor.matmul_mx(
-                out=acc[ct, ds.start][:],
+                out=acc[ct, dt][:],
                 lhsT=m_codes[ct][:, cols].bitcast(FP8X4),
                 lhsT_scale=m_scales[ct][:, cols],
-                rhs=e_words[g][:, 2 * ds.start : 2 * ds.stop].bitcast(FP4X4),
-                rhs_scale=e_plane[:, g, ds],
+                rhs=e_words[g][:, 2 * NB * dt : 2 * NB * (dt + 1)].bitcast(FP4X4),
+                rhs_scale=e_plane[:, g, NB * dt : NB * (dt + 1)],
                 start=(g == 0),
                 stop=(g == NG - 1),
             )
 
-        out_rows = out.rearrange("(p t) d -> t p d", t=NC)
+        out_rows = out.rearrange("(h p e) d -> h e p d", p=P, e=2)
 
-        def finish(ct, ds, engine):
-            res = buf("res", NC * ND + 3, [P, ds.stop - ds.start], F32)
-            copy_on(engine, res[:], acc[ct, ds.start][:])
-            nc.sync.dma_start(out=out_rows[ct][:, ds], in_=res[:])
-
-        wide = [slice(NB * dt, NB * (dt + 1)) for dt in range(ND)]
-        narrow = [slice(D - NB + P * n, D - NB + P * (n + 1)) for n in range(NB // P)]
+        def finish(ct, dt, engine, parts=1):
+            width = NB // parts
+            for part in range(parts):
+                res = buf("res", NC * ND + 3, [P, width], F32)
+                copy_on(engine, res[:], acc[ct, dt][:, width * part : width * (part + 1)])
+                first = NB * dt + width * part
+                nc.sync.dma_start(out=out_rows[ct // 2, ct % 2][:, first : first + width], in_=res[:])
 
         def first_goals(g, dts):
             for dt in dts:
-                product2(0, wide[dt], g, 4 + dt)
+                product2(0, dt, g, 4 + dt)
 
         def costs(j, pair, number):
             product1(j, pair, number)
             exponential(j, pair)
 
         last = NG - 1
-        for pair in range(2):
-            interleave_w(0, pair, 2 + pair)
+        interleave_w_copy(0, 1)
+        interleave_w(0, 0, 2)
         for j in range(2 * NG):
             g, odd = divmod(j, 2)
-            scale_x(j, 0, NQ if j == 0 else 1)
+            scale_x(j, 0, XS_PARTS if j == 0 else 1)
             if j == 1:
                 quantise_w(0, slice(0, C))
             if j == 2:
@@ -322,7 +330,7 @@ def tile_mppi_control_update_s13_kernel(tc, x_bytes, x_scale, w, base, ratio, ep
         times_ratio(last, 0)
         times_ratio(last, 1)
         for g in early:
-            product2(1, wide[0], g, 0)
+            product2(1, 0, g, 0)
         turn_m((last,), 0, 1)
         turn_m(late, 1, 2)
         empty_m((last,), 0, "scalar")
@@ -332,27 +340,23 @@ def tile_mppi_control_update_s13_kernel(tc, x_bytes, x_scale, w, base, ratio, ep
         times_ratio(last, 2)
         quantise_m(late, 1)
         for g in early:
-            product2(1, wide[1], g, 3)
+            product2(1, 1, g, 3)
         first_goals(last, range(ND))
         for dt in range(ND):
-            finish(0, wide[dt], "scalar" if dt % 2 == 0 else "vector")
-        banks = (0, 3, 4, 5, 6, 7, 0, 3, 4, 5, 6)
+            finish(0, dt, "scalar")
+        for g in range(NG):
+            times_ratio(g, 3)
+        banks = (0, 3, 4, 7, 0, 3, 4, 1, 2, 5, 6, 7)
         for ct in range(1, NC):
-            for dt in range(ND if ct + 1 < NC else ND - 1):
+            for dt in range(ND):
                 for g in late if ct == 1 and dt < 2 else range(NG):
-                    product2(ct, wide[dt], g, banks[ND * (ct - 1) + dt])
-                if dt == 1 and ct + 1 < NC:
-                    turn_m(early, ct + 1, 1)
-                    turn_m(late, ct + 1, 2)
-                    empty_m(early, ct + 1, "vector")
-                    empty_m(late, ct + 1, "scalar")
-                    quantise_m(early, ct + 1)
-                    quantise_m(late, ct + 1)
-                    if ct + 2 < NC:
-                        for g in range(NG):
-                            times_ratio(g, ct + 2)
-                finish(ct, wide[dt], "vector" if ct >= 2 and dt % 2 == 0 else "scalar")
-        for n in range(NB // P):
-            for g in range(NG):
-                product2(NC - 1, narrow[n], g, n)
-            finish(NC - 1, narrow[n], "scalar" if n % 2 == 0 else "vector")
+                    product2(ct, dt, g, banks[ND * (ct - 1) + dt])
+                if ct == 1 and dt == 2:
+                    rest = [(gs, c) for c in (2, 3) for gs in (early, late)]
+                    for n in range(4):
+                        turn_m(*rest[n], (1, 2, 5, 6)[n])
+                    for n in range(4):
+                        empty_m(*rest[n], "vector" if n == 0 else "scalar")
+                        quantise_m(*rest[n])
+                parts = 4 if (ct, dt) == (NC - 1, ND - 1) else 1
+                finish(ct, dt, "vector" if ct >= 2 and dt % 2 == 1 else "scalar", parts)

@@ -78,6 +78,10 @@ def tile_mppi_control_update_s13_kernel(tc, x_bytes, x_scale, w, base, ratio, ep
         )
         for g in range(1, NG):
             nc.sync.dma_start(out=x_rest[g - 1][:], in_=x_rows[g])
+        base_all = buf("base_all", 1, [P, C // 2], BF16)
+        nc.sync.dma_start(out=base_all[:], in_=base[C // 2 :].partition_broadcast(P))
+        ratio_own = buf("ratio_own", 1, [P, NG, NT], BF16)
+        nc.sync.dma_start(out=ratio_own[:], in_=ratio.rearrange("(g p t) -> p g t", p=P, t=NT))
         e_rows = eps_scales.bitcast(I32).rearrange("g q n -> q g n")
         for quad in range(4):
             nc.sync.dma_start(
@@ -140,7 +144,7 @@ def tile_mppi_control_update_s13_kernel(tc, x_bytes, x_scale, w, base, ratio, ep
             )
 
         xf, xt, xg, x_codes, x_scales = {}, {}, {}, {}, {}
-        cost, ex, eb, wt, wg, acc = {}, {}, {}, {}, {}, {}
+        cost, ex, kept, diff, eb, wt, wg, acc = {}, {}, {}, {}, {}, {}, {}, {}
         m_codes = [buf("m_codes", NC, [P, NG * P], U32) for ct in range(NC)]
         m_scales = [buf("m_scales", NC, [P, NG * P], U8) for ct in range(NC)]
 
@@ -181,35 +185,70 @@ def tile_mppi_control_update_s13_kernel(tc, x_bytes, x_scale, w, base, ratio, ep
         def product1(j, pair, number):
             cost[j, pair] = bank(number, [P, 2, HALF])
             for a in range(2):
-                cols = slice(P * (2 * pair + a), P * (2 * pair + a + 1))
                 for q in range(NQ):
-                    rows = slice(HALF * q, HALF * (q + 1))
+                    if pair == 0:
+                        goals, rows = slice(P * a, P * (a + 1)), slice(HALF * q, HALF * (q + 1))
+                        still = w_codes[q][:, goals], w_scales[q][:, goals]
+                        moving = x_codes[j][:, rows], x_scales[j][:, rows]
+                    else:
+                        goals, rows = slice(C // 2, C), slice(HALF * q + P * a, HALF * q + P * (a + 1))
+                        still = x_codes[j][:, rows], x_scales[j][:, rows]
+                        moving = w_codes[q][:, goals], w_scales[q][:, goals]
                     nc.tensor.matmul_mx(
                         out=cost[j, pair][:, a, :],
-                        lhsT=w_codes[q][:, cols].bitcast(FP8X4),
-                        lhsT_scale=w_scales[q][:, cols],
-                        rhs=x_codes[j][:, rows].bitcast(FP8X4),
-                        rhs_scale=x_scales[j][:, rows],
+                        lhsT=still[0].bitcast(FP8X4),
+                        lhsT_scale=still[1],
+                        rhs=moving[0].bitcast(FP8X4),
+                        rhs_scale=moving[1],
                         start=(q == 0),
                         stop=(q == NQ - 1),
                     )
 
         def exponential(j, pair):
             g, h = divmod(j, 2)
-            for a in range(2):
-                ct = 2 * pair + a
+            if pair == 1:
                 if h == 0:
-                    ex[g, ct] = buf("ex", NG * NC, [P, KP], F32)
+                    kept[g] = buf("kept", NG, [P, 2, C // 2, 2], F32)
+                nc.scalar.copy(out=kept[g][:, h], in_=cost[j, pair][:].rearrange("p a c -> p c a"))
+                return
+            for ct in range(2):
+                if h == 0:
+                    ex[g, ct] = buf("ex", 3 * NG, [P, KP], F32)
                 nc.scalar.activation(
                     out=ex[g, ct][:, HALF * h : HALF * (h + 1)],
-                    in_=cost[j, pair][:, a, :],
+                    in_=cost[j, pair][:, ct, :],
                     func=ACT.Exp,
                     bias=base_bf[:, ct : ct + 1],
                     scale=-1.0,
                 )
 
+        def late_difference(g, ct):
+            e = ct - 2
+            diff[g, ct] = buf("diff", 4, [P, 2, P, 2], F32)
+            nc.vector.tensor_tensor(
+                out=diff[g, ct][:],
+                in0=base_all[:].rearrange("p (h m e a) -> p e h m a", h=1, e=2, a=1)[:, e].to_broadcast([P, 2, P, 2]),
+                in1=kept[g][:, :, P * e : P * (e + 1), :],
+                op=ALU.subtract,
+            )
+
+        def late_exponential(g, ct):
+            ex[g, ct] = buf("ex", 3 * NG, [P, KP], F32)
+            nc.scalar.activation(out=ex[g, ct][:], in_=diff[g, ct][:].rearrange("p h m a -> p (h m a)"), func=ACT.Exp)
+
+        def late_ratio(gs, n, ct):
+            g = gs[n]
+            if n == 0:
+                wg[gs, ct] = buf("wg", 4, [P, 2 * P, 4], BF16)
+            nc.vector.tensor_tensor(
+                out=wg[gs, ct][:, P * n : P * (n + 1), :].rearrange("p m (h a) -> p m h a", a=2),
+                in0=ex[g, ct][:].rearrange("p (h m a) -> p m h a", h=2, a=2),
+                in1=ratio_own[:, g : g + 1, :].rearrange("p o (h a) -> p o h a", a=2).to_broadcast([P, P, 2, 2]),
+                op=ALU.mult,
+            )
+
         def times_ratio(g, ct):
-            eb[g, ct] = buf("eb", 10, [P, 2, 256], BF16)
+            eb[g, ct] = buf("eb", 6, [P, 2, 256], BF16)
             nc.vector.tensor_tensor(
                 out=eb[g, ct][:].rearrange("p u (i e) -> p u i e", e=2),
                 in0=ex[g, ct][:].rearrange("p (u e i) -> p u i e", u=2, e=2),
@@ -313,6 +352,15 @@ def tile_mppi_control_update_s13_kernel(tc, x_bytes, x_scale, w, base, ratio, ep
 
         early, late = (0, 1), (2, last)
         end = 2 * NG - 1
+
+        def late_weights(ct):
+            late_ratio(early, 0, ct)
+            late_ratio(early, 1, ct)
+            late_ratio(late, 0, ct)
+            quantise_m(early, ct)
+            late_ratio(late, 1, ct)
+            quantise_m(late, ct)
+
         times_ratio(0, 1)
         times_ratio(1, 1)
         turn_m(early, 1, 0)
@@ -324,39 +372,41 @@ def tile_mppi_control_update_s13_kernel(tc, x_bytes, x_scale, w, base, ratio, ep
         costs(end, 1, 2)
         first_goals(last - 1, (2, 3))
         times_ratio(2, 1)
-        times_ratio(0, 2)
+        late_difference(0, 2)
         quantise_m(early, 1)
-        times_ratio(1, 2)
+        late_difference(1, 2)
         times_ratio(last, 0)
         times_ratio(last, 1)
         for g in early:
             product2(1, 0, g, 0)
         turn_m((last,), 0, 1)
         turn_m(late, 1, 2)
+        late_exponential(0, 2)
         empty_m((last,), 0, "scalar")
         empty_m(late, 1, "scalar")
-        times_ratio(2, 2)
+        late_exponential(1, 2)
+        late_difference(2, 2)
         quantise_m((last,), 0)
-        times_ratio(last, 2)
+        late_difference(last, 2)
         quantise_m(late, 1)
+        for g in late:
+            late_exponential(g, 2)
         for g in early:
             product2(1, 1, g, 3)
         first_goals(last, range(ND))
         for dt in range(ND):
             finish(0, dt, "scalar")
+        late_weights(2)
         for g in range(NG):
-            times_ratio(g, 3)
-        banks = (0, 3, 4, 7, 0, 3, 4, 1, 2, 5, 6, 7)
+            late_difference(g, 3)
+        banks = (0, 3, 1, 2, 4, 5, 6, 7, 0, 3, 1, 2)
         for ct in range(1, NC):
             for dt in range(ND):
                 for g in late if ct == 1 and dt < 2 else range(NG):
                     product2(ct, dt, g, banks[ND * (ct - 1) + dt])
-                if ct == 1 and dt == 2:
-                    rest = [(gs, c) for c in (2, 3) for gs in (early, late)]
-                    for n in range(4):
-                        turn_m(*rest[n], (1, 2, 5, 6)[n])
-                    for n in range(4):
-                        empty_m(*rest[n], "vector" if n == 0 else "scalar")
-                        quantise_m(*rest[n])
+                if ct == 1 and dt == 1:
+                    for g in range(NG):
+                        late_exponential(g, 3)
+                    late_weights(3)
                 parts = 4 if (ct, dt) == (NC - 1, ND - 1) else 1
                 finish(ct, dt, "vector" if ct >= 2 and dt % 2 == 1 else "scalar", parts)

@@ -76,12 +76,8 @@ def tile_mppi_control_update_s13_kernel(tc, x_bytes, x_scale, w, base, ratio, ep
         nc.sync.dma_start(
             out=base_bf[:].rearrange("p (h e) -> p h e", e=2), in_=base.rearrange("(h p e) -> p h e", p=P, e=2)
         )
-        for g in range(1, NG):
+        for g in range(1, NG - 1):
             nc.sync.dma_start(out=x_rest[g - 1][:], in_=x_rows[g])
-        base_all = buf("base_all", 1, [P, C // 2], BF16)
-        nc.sync.dma_start(out=base_all[:], in_=base[C // 2 :].partition_broadcast(P))
-        ratio_own = buf("ratio_own", 1, [P, NG, NT], BF16)
-        nc.sync.dma_start(out=ratio_own[:], in_=ratio.rearrange("(g p t) -> p g t", p=P, t=NT))
         e_rows = eps_scales.bitcast(I32).rearrange("g q n -> q g n")
         for quad in range(4):
             nc.sync.dma_start(
@@ -90,6 +86,12 @@ def tile_mppi_control_update_s13_kernel(tc, x_bytes, x_scale, w, base, ratio, ep
         e_words = [buf("e_words", NG, [P, 2 * D], U8) for g in range(NG)]
         for g in range(NG):
             nc.sync.dma_start(out=e_words[g][:], in_=eps_words[g])
+            if g == 0:
+                nc.sync.dma_start(out=x_rest[NG - 2][:], in_=x_rows[NG - 1])
+        base_all = buf("base_all", 1, [P, C // 2], BF16)
+        nc.sync.dma_start(out=base_all[:], in_=base[C // 2 :].partition_broadcast(P))
+        ratio_own = buf("ratio_own", 1, [P, NG, NT], BF16)
+        nc.sync.dma_start(out=ratio_own[:], in_=ratio.rearrange("(g p t) -> p g t", p=P, t=NT))
 
         xs_all = buf("xs_all", 1, [P, F], F32)
         for a in range(XS_PARTS):
@@ -215,44 +217,56 @@ def tile_mppi_control_update_s13_kernel(tc, x_bytes, x_scale, w, base, ratio, ep
                 if h == 0:
                     ex[g, ct] = buf("ex", 3 * NG, [P, KP], F32)
                 nc.scalar.activation(
-                    out=ex[g, ct][:, HALF * h : HALF * (h + 1)],
-                    in_=cost[j, pair][:, ct, :],
+                    out=ex[g, ct][:, HALF * h : HALF * (h + 1)].rearrange("p (i a) -> p i a", a=2),
+                    in_=cost[j, pair][:, ct, :].rearrange("p (a i) -> p i a", a=2),
                     func=ACT.Exp,
                     bias=base_bf[:, ct : ct + 1],
                     scale=-1.0,
                 )
 
+        base_twice = buf("base_twice", 1, [P, 2, P, 2], F32)
+
+        def double_base():
+            nc.scalar.copy(
+                out=base_twice[:],
+                in_=base_all[:].rearrange("p (m e a) -> p e m a", e=2, a=1).to_broadcast([P, 2, P, 2]),
+            )
+
         def late_difference(g, ct):
             e = ct - 2
-            diff[g, ct] = buf("diff", 4, [P, 2, P, 2], F32)
+            diff[g, ct] = buf("diff", 6, [P, 2, P, 2], F32)
             nc.vector.tensor_tensor(
                 out=diff[g, ct][:],
-                in0=base_all[:].rearrange("p (h m e a) -> p e h m a", h=1, e=2, a=1)[:, e].to_broadcast([P, 2, P, 2]),
+                in0=base_twice[:, e : e + 1].to_broadcast([P, 2, P, 2]),
                 in1=kept[g][:, :, P * e : P * (e + 1), :],
                 op=ALU.subtract,
             )
 
         def late_exponential(g, ct):
             ex[g, ct] = buf("ex", 3 * NG, [P, KP], F32)
-            nc.scalar.activation(out=ex[g, ct][:], in_=diff[g, ct][:].rearrange("p h m a -> p (h m a)"), func=ACT.Exp)
+            nc.scalar.activation(
+                out=ex[g, ct][:].rearrange("p (m h a) -> p m h a", h=2, a=2),
+                in_=diff[g, ct][:].rearrange("p h m a -> p m h a"),
+                func=ACT.Exp,
+            )
 
         def late_ratio(gs, n, ct):
             g = gs[n]
             if n == 0:
                 wg[gs, ct] = buf("wg", 4, [P, 2 * P, 4], BF16)
             nc.vector.tensor_tensor(
-                out=wg[gs, ct][:, P * n : P * (n + 1), :].rearrange("p m (h a) -> p m h a", a=2),
-                in0=ex[g, ct][:].rearrange("p (h m a) -> p m h a", h=2, a=2),
-                in1=ratio_own[:, g : g + 1, :].rearrange("p o (h a) -> p o h a", a=2).to_broadcast([P, P, 2, 2]),
+                out=wg[gs, ct][:, P * n : P * (n + 1), :],
+                in0=ex[g, ct][:].rearrange("p (m t) -> p m t", t=NT),
+                in1=ratio_own[:, g : g + 1, :].to_broadcast([P, P, NT]),
                 op=ALU.mult,
             )
 
         def times_ratio(g, ct):
             eb[g, ct] = buf("eb", 6, [P, 2, 256], BF16)
             nc.vector.tensor_tensor(
-                out=eb[g, ct][:].rearrange("p u (i e) -> p u i e", e=2),
-                in0=ex[g, ct][:].rearrange("p (u e i) -> p u i e", u=2, e=2),
-                in1=ratio_all[:, g, :].rearrange("p (u i e) -> p u i e", u=2, e=2),
+                out=eb[g, ct][:].rearrange("p u n -> p (u n)"),
+                in0=ex[g, ct][:],
+                in1=ratio_all[:, g, :],
                 op=ALU.mult,
             )
 
@@ -349,18 +363,11 @@ def tile_mppi_control_update_s13_kernel(tc, x_bytes, x_scale, w, base, ratio, ep
                     first_goals(g - 2, (2, 3))
                 if j >= 3:
                     costs(j - 1, 1, 3)
+                if j == 5:
+                    double_base()
 
         early, late = (0, 1), (2, last)
         end = 2 * NG - 1
-
-        def late_weights(ct):
-            late_ratio(early, 0, ct)
-            late_ratio(early, 1, ct)
-            late_ratio(late, 0, ct)
-            quantise_m(early, ct)
-            late_ratio(late, 1, ct)
-            quantise_m(late, ct)
-
         times_ratio(0, 1)
         times_ratio(1, 1)
         turn_m(early, 1, 0)
@@ -389,24 +396,37 @@ def tile_mppi_control_update_s13_kernel(tc, x_bytes, x_scale, w, base, ratio, ep
         quantise_m((last,), 0)
         late_difference(last, 2)
         quantise_m(late, 1)
-        for g in late:
-            late_exponential(g, 2)
         for g in early:
             product2(1, 1, g, 3)
         first_goals(last, range(ND))
-        for dt in range(ND):
-            finish(0, dt, "scalar")
-        late_weights(2)
-        for g in range(NG):
+        for n in range(2):
+            late_ratio(early, n, 2)
+        late_difference(0, 3)
+        for n in range(2):
+            finish(0, n, "scalar")
+            late_exponential(late[n], 2)
+            late_ratio(late, n, 2)
+            if n == 0:
+                quantise_m(early, 2)
+        late_difference(1, 3)
+        quantise_m(late, 2)
+        for g in late:
             late_difference(g, 3)
+        for dt in range(2, ND):
+            finish(0, dt, "scalar")
         banks = (0, 3, 1, 2, 4, 5, 6, 7, 0, 3, 1, 2)
         for ct in range(1, NC):
+            if ct > 1:
+                for dt in range(2):
+                    for g in early:
+                        product2(ct, dt, g, banks[ND * (ct - 1) + dt])
             for dt in range(ND):
-                for g in late if ct == 1 and dt < 2 else range(NG):
+                for g in late if dt < 2 else range(NG):
                     product2(ct, dt, g, banks[ND * (ct - 1) + dt])
-                if ct == 1 and dt == 1:
-                    for g in range(NG):
-                        late_exponential(g, 3)
-                    late_weights(3)
+                if ct == 1:
+                    late_exponential(dt, 3)
+                    late_ratio((early, late)[dt // 2], dt % 2, 3)
+                    if dt >= 2:
+                        quantise_m((early, late)[dt - 2], 3)
                 parts = 4 if (ct, dt) == (NC - 1, ND - 1) else 1
                 finish(ct, dt, "vector" if ct >= 2 and dt % 2 == 1 else "scalar", parts)

@@ -72,10 +72,8 @@ def tile_mppi_control_update_s13_kernel(tc, x_bytes, x_scale, w, base, ratio, ep
             if t < NQ:
                 nc.sync.dma_start(out=w_raw[t][:], in_=w_rows[t])
         nc.sync.dma_start(out=ratio_row[0:1, :], in_=ratio.rearrange("(o s) -> o s", o=1))
-        base_bf = buf("base_bf", 1, [P, NC], BF16)
-        nc.sync.dma_start(
-            out=base_bf[:].rearrange("p (h e) -> p h e", e=2), in_=base.rearrange("(h p e) -> p h e", p=P, e=2)
-        )
+        base_bf = buf("base_bf", 1, [P, 2], BF16)
+        nc.sync.dma_start(out=base_bf[:], in_=base[: C // 2].rearrange("(p e) -> p e", e=2))
         for g in range(1, NG - 1):
             nc.sync.dma_start(out=x_rest[g - 1][:], in_=x_rows[g])
         e_rows = eps_scales.bitcast(I32).rearrange("g q n -> q g n")
@@ -294,33 +292,35 @@ def tile_mppi_control_update_s13_kernel(tc, x_bytes, x_scale, w, base, ratio, ep
                 in_=wg[gs, ct][:].rearrange("p c j -> p (c j)"),
             )
 
-        def product2(ct, dt, g, number):
+        def product2(ct, ds, g, number):
             if g == 0:
-                acc[ct, dt] = bank(number, [P, NB])
+                acc[ct, ds.start] = bank(number, [P, ds.stop - ds.start])
             cols = slice(P * g, P * (g + 1))
             nc.tensor.matmul_mx(
-                out=acc[ct, dt][:],
+                out=acc[ct, ds.start][:],
                 lhsT=m_codes[ct][:, cols].bitcast(FP8X4),
                 lhsT_scale=m_scales[ct][:, cols],
-                rhs=e_words[g][:, 2 * NB * dt : 2 * NB * (dt + 1)].bitcast(FP4X4),
-                rhs_scale=e_plane[:, g, NB * dt : NB * (dt + 1)],
+                rhs=e_words[g][:, 2 * ds.start : 2 * ds.stop].bitcast(FP4X4),
+                rhs_scale=e_plane[:, g, ds],
                 start=(g == 0),
                 stop=(g == NG - 1),
             )
 
+        wide = [slice(NB * dt, NB * (dt + 1)) for dt in range(ND)]
+        narrow = [slice(D - NB + P * n, D - NB + P * (n + 1)) for n in range(NB // P)]
         out_rows = out.rearrange("(h p e) d -> h e p d", p=P, e=2)
 
-        def finish(ct, dt, engine, parts=1):
-            width = NB // parts
+        def finish(ct, ds, engine, parts=1):
+            width = (ds.stop - ds.start) // parts
             for part in range(parts):
-                res = buf("res", NC * ND + 3, [P, width], F32)
-                copy_on(engine, res[:], acc[ct, dt][:, width * part : width * (part + 1)])
-                first = NB * dt + width * part
+                res = buf("res", NC * ND + 4, [P, width], F32)
+                copy_on(engine, res[:], acc[ct, ds.start][:, width * part : width * (part + 1)])
+                first = ds.start + width * part
                 nc.sync.dma_start(out=out_rows[ct // 2, ct % 2][:, first : first + width], in_=res[:])
 
         def first_goals(g, dts):
             for dt in dts:
-                product2(0, dt, g, 4 + dt)
+                product2(0, wide[dt], g, 4 + dt)
 
         def costs(j, pair, number):
             product1(j, pair, number)
@@ -385,7 +385,7 @@ def tile_mppi_control_update_s13_kernel(tc, x_bytes, x_scale, w, base, ratio, ep
         times_ratio(last, 0)
         times_ratio(last, 1)
         for g in early:
-            product2(1, 0, g, 0)
+            product2(1, wide[0], g, 0)
         turn_m((last,), 0, 1)
         turn_m(late, 1, 2)
         late_exponential(0, 2)
@@ -397,13 +397,13 @@ def tile_mppi_control_update_s13_kernel(tc, x_bytes, x_scale, w, base, ratio, ep
         late_difference(last, 2)
         quantise_m(late, 1)
         for g in early:
-            product2(1, 1, g, 3)
+            product2(1, wide[1], g, 3)
         first_goals(last, range(ND))
         for n in range(2):
             late_ratio(early, n, 2)
         late_difference(0, 3)
         for n in range(2):
-            finish(0, n, "scalar")
+            finish(0, wide[n], "scalar")
             late_exponential(late[n], 2)
             late_ratio(late, n, 2)
             if n == 0:
@@ -413,20 +413,43 @@ def tile_mppi_control_update_s13_kernel(tc, x_bytes, x_scale, w, base, ratio, ep
         for g in late:
             late_difference(g, 3)
         for dt in range(2, ND):
-            finish(0, dt, "scalar")
-        banks = (0, 3, 1, 2, 4, 5, 6, 7, 0, 3, 1, 2)
-        for ct in range(1, NC):
-            if ct > 1:
-                for dt in range(2):
-                    for g in early:
-                        product2(ct, dt, g, banks[ND * (ct - 1) + dt])
-            for dt in range(ND):
-                for g in late if dt < 2 else range(NG):
-                    product2(ct, dt, g, banks[ND * (ct - 1) + dt])
-                if ct == 1:
-                    late_exponential(dt, 3)
-                    late_ratio((early, late)[dt // 2], dt % 2, 3)
-                    if dt >= 2:
-                        quantise_m((early, late)[dt - 2], 3)
-                parts = 4 if (ct, dt) == (NC - 1, ND - 1) else 1
-                finish(ct, dt, "vector" if ct >= 2 and dt % 2 == 1 else "scalar", parts)
+            finish(0, wide[dt], "scalar")
+        banks = (0, 3, 1, 2, 4, 5, 6, 7, 0, 3, 1)
+
+        def passes(ct, dts, gs):
+            for dt in dts:
+                for g in gs:
+                    product2(ct, wide[dt], g, banks[ND * (ct - 1) + dt])
+
+        passes(1, (0, 1), late)
+        passes(1, (2, 3), range(NG))
+        passes(2, (0, 1), early)
+        passes(2, (0, 1), late)
+        for dt in range(3):
+            finish(1, wide[dt], "scalar")
+        for n in range(2):
+            late_exponential(early[n], 3)
+        finish(1, wide[3], "vector")
+        for n in range(2):
+            late_ratio(early, n, 3)
+        for n in range(2):
+            late_exponential(late[n], 3)
+        late_ratio(late, 0, 3)
+        quantise_m(early, 3)
+        late_ratio(late, 1, 3)
+        finish(2, wide[0], "scalar")
+        finish(2, wide[1], "scalar")
+        quantise_m(late, 3)
+        passes(2, (2, 3), range(NG))
+        passes(3, (0, 1), early)
+        passes(3, (0, 1), late)
+        finish(2, wide[2], "scalar")
+        finish(2, wide[3], "vector")
+        finish(3, wide[0], "vector")
+        finish(3, wide[1], "scalar")
+        passes(3, (2,), range(NG))
+        finish(3, wide[2], "scalar", 2)
+        for n in range(NB // P):
+            for g in range(NG):
+                product2(3, narrow[n], g, 4 + n)
+            finish(3, narrow[n], "vector" if n % 2 == 0 else "scalar")

@@ -81,15 +81,15 @@ def tile_mppi_control_update_s13_kernel(tc, x_bytes, x_scale, w, base, ratio, ep
             nc.sync.dma_start(
                 out=e_plane[32 * quad : 32 * quad + 4, :, :].bitcast(I32), in_=e_rows[4 * quad : 4 * quad + 4]
             )
+        ratio_own = buf("ratio_own", 1, [P, NG, NT], BF16)
         e_words = [buf("e_words", NG, [P, 2 * D], U8) for g in range(NG)]
         for g in range(NG):
             nc.sync.dma_start(out=e_words[g][:], in_=eps_words[g])
             if g == 0:
+                nc.sync.dma_start(out=ratio_own[:], in_=ratio.rearrange("(g p t) -> p g t", p=P, t=NT))
                 nc.sync.dma_start(out=x_rest[NG - 2][:], in_=x_rows[NG - 1])
         base_all = buf("base_all", 1, [P, C // 2], BF16)
         nc.sync.dma_start(out=base_all[:], in_=base[C // 2 :].partition_broadcast(P))
-        ratio_own = buf("ratio_own", 1, [P, NG, NT], BF16)
-        nc.sync.dma_start(out=ratio_own[:], in_=ratio.rearrange("(g p t) -> p g t", p=P, t=NT))
 
         xs_all = buf("xs_all", 1, [P, F], F32)
         for a in range(XS_PARTS):
@@ -230,6 +230,14 @@ def tile_mppi_control_update_s13_kernel(tc, x_bytes, x_scale, w, base, ratio, ep
                 in_=base_all[:].rearrange("p (m e a) -> p e m a", e=2, a=1).to_broadcast([P, 2, P, 2]),
             )
 
+        ratio_rows = buf("ratio_rows", 1, [P, NG, P, NT], BF16)
+
+        def repeat_ratio(g):
+            nc.scalar.copy(
+                out=ratio_rows[:, g].bitcast(F32),
+                in_=ratio_own[:, g : g + 1, :].bitcast(F32).to_broadcast([P, P, 2]),
+            )
+
         def late_difference(g, ct):
             e = ct - 2
             diff[g, ct] = buf("diff", 6, [P, 2, P, 2], F32)
@@ -253,9 +261,9 @@ def tile_mppi_control_update_s13_kernel(tc, x_bytes, x_scale, w, base, ratio, ep
             if n == 0:
                 wg[gs, ct] = buf("wg", 4, [P, 2 * P, 4], BF16)
             nc.vector.tensor_tensor(
-                out=wg[gs, ct][:, P * n : P * (n + 1), :],
-                in0=ex[g, ct][:].rearrange("p (m t) -> p m t", t=NT),
-                in1=ratio_own[:, g : g + 1, :].to_broadcast([P, P, NT]),
+                out=wg[gs, ct][:, P * n : P * (n + 1), :].rearrange("p m t -> p (m t)"),
+                in0=ex[g, ct][:],
+                in1=ratio_rows[:, g].rearrange("p m t -> p (m t)"),
                 op=ALU.mult,
             )
 
@@ -360,9 +368,12 @@ def tile_mppi_control_update_s13_kernel(tc, x_bytes, x_scale, w, base, ratio, ep
                 if j <= 2:
                     spread_ratio(j - 1)
                 if g >= 2 and not odd:
+                    repeat_ratio(g - 1)
                     first_goals(g - 2, (2, 3))
                 if j >= 3:
                     costs(j - 1, 1, 3)
+                if j == 3:
+                    repeat_ratio(0)
                 if j == 5:
                     double_base()
 
@@ -372,6 +383,7 @@ def tile_mppi_control_update_s13_kernel(tc, x_bytes, x_scale, w, base, ratio, ep
         times_ratio(1, 1)
         turn_m(early, 1, 0)
         empty_m(early, 1, "scalar")
+        repeat_ratio(last)
         quantise_m((last - 1,), 0)
         quantise_x(end)
         first_goals(last - 1, (0, 1))

@@ -222,7 +222,7 @@ def tile_mppi_control_update_s13_kernel(tc, x_bytes, x_scale, w, base, ratio, ep
                     scale=-1.0,
                 )
 
-        base_twice = buf("base_twice", 1, [P, 2, P, 2], F32)
+        base_twice = buf("base_twice", 1, [P, 2, P, 2], BF16)
 
         def double_base():
             nc.scalar.copy(
@@ -243,8 +243,8 @@ def tile_mppi_control_update_s13_kernel(tc, x_bytes, x_scale, w, base, ratio, ep
             diff[g, ct] = buf("diff", 6, [P, 2, P, 2], F32)
             nc.vector.tensor_tensor(
                 out=diff[g, ct][:],
-                in0=base_twice[:, e : e + 1].to_broadcast([P, 2, P, 2]),
-                in1=kept[g][:, :, P * e : P * (e + 1), :],
+                in0=kept[g][:, :, P * e : P * (e + 1), :],
+                in1=base_twice[:, e : e + 1].to_broadcast([P, 2, P, 2]),
                 op=ALU.subtract,
             )
 
@@ -254,6 +254,7 @@ def tile_mppi_control_update_s13_kernel(tc, x_bytes, x_scale, w, base, ratio, ep
                 out=ex[g, ct][:].rearrange("p (m h a) -> p m h a", h=2, a=2),
                 in_=diff[g, ct][:].rearrange("p h m a -> p m h a"),
                 func=ACT.Exp,
+                scale=-1.0,
             )
 
         def late_ratio(gs, n, ct):

@@ -37,7 +37,7 @@ def tile_mppi_control_update_s13_kernel(tc, x_bytes, x_scale, w, base, ratio, ep
         ctx.enter_context(tc.manual_schedule())
 
         def buf(tag, bufs, shape, dtype):
-            return sb.tile(shape, dtype, name=tag, tag=tag, bufs=bufs, align_bytes=64)
+            return sb.tile(shape, dtype, name=tag, tag=tag, bufs=bufs, align_bytes=256)
 
         def bank(number, shape, dtype=F32):
             return psum.tile(shape, dtype, name="bank%d" % number, tag="bank%d" % number)

@@ -23,8 +23,12 @@ NT = 4
 NC = C // P
 NB = 512
 ND = D // NB
-HALF = KP // 2
+UNIT = KP // 2
+PAIR = C // 2
 XS_PARTS = 4
+X_BANKS = (0, 1)
+COST_BANKS = (2, 3)
+HELD_BANK = 4
 
 FLOPS = 2 * S * F * C + 2 * C * S * D
 
@@ -59,8 +63,8 @@ def tile_mppi_control_update_s13_kernel(tc, x_bytes, x_scale, w, base, ratio, ep
         nc.vector.memset(ones[:], 1.0)
         ident_bf = buf("ident_bf", 1, [P, P], BF16)
         nc.vector.tensor_copy(out=ident_bf[:], in_=ident[:])
-        e_plane = buf("e_plane", 1, [P, NG, D], U8)
-        nc.vector.memset(e_plane[:].rearrange("p g n -> p (g n)").bitcast(I32), 0)
+        e_scales = buf("e_scales", 1, [P, NG, D], U8)
+        nc.vector.memset(e_scales[:].rearrange("p g n -> p (g n)").bitcast(I32), 0)
 
         x_rows = x_bytes.rearrange("(g p t) k -> g p t k", p=P, t=NT)
         w_rows = w.rearrange("(q p j) c -> q p j c", p=P, j=4)
@@ -72,14 +76,14 @@ def tile_mppi_control_update_s13_kernel(tc, x_bytes, x_scale, w, base, ratio, ep
             if t < NQ:
                 nc.sync.dma_start(out=w_raw[t][:], in_=w_rows[t])
         nc.sync.dma_start(out=ratio_row[0:1, :], in_=ratio.rearrange("(o s) -> o s", o=1))
-        base_bf = buf("base_bf", 1, [P, 2], BF16)
-        nc.sync.dma_start(out=base_bf[:], in_=base[: C // 2].rearrange("(p e) -> p e", e=2))
+        base_own = buf("base_own", 1, [P, 2], BF16)
+        nc.sync.dma_start(out=base_own[:], in_=base[:PAIR].rearrange("(p e) -> p e", e=2))
         for g in range(1, NG - 1):
             nc.sync.dma_start(out=x_rest[g - 1][:], in_=x_rows[g])
         e_rows = eps_scales.bitcast(I32).rearrange("g q n -> q g n")
         for quad in range(4):
             nc.sync.dma_start(
-                out=e_plane[32 * quad : 32 * quad + 4, :, :].bitcast(I32), in_=e_rows[4 * quad : 4 * quad + 4]
+                out=e_scales[32 * quad : 32 * quad + 4, :, :].bitcast(I32), in_=e_rows[4 * quad : 4 * quad + 4]
             )
         ratio_own = buf("ratio_own", 1, [P, NG, NT], BF16)
         e_words = [buf("e_words", NG, [P, 2 * D], U8) for g in range(NG)]
@@ -88,12 +92,12 @@ def tile_mppi_control_update_s13_kernel(tc, x_bytes, x_scale, w, base, ratio, ep
             if g == 0:
                 nc.sync.dma_start(out=ratio_own[:], in_=ratio.rearrange("(g p t) -> p g t", p=P, t=NT))
                 nc.sync.dma_start(out=x_rest[NG - 2][:], in_=x_rows[NG - 1])
-        base_all = buf("base_all", 1, [P, C // 2], BF16)
-        nc.sync.dma_start(out=base_all[:], in_=base[C // 2 :].partition_broadcast(P))
+        base_all = buf("base_all", 1, [P, PAIR], BF16)
+        nc.sync.dma_start(out=base_all[:], in_=base[PAIR:].partition_broadcast(P))
 
         xs_all = buf("xs_all", 1, [P, F], F32)
         for a in range(XS_PARTS):
-            spread = bank(4 + a, [P, 2, P])
+            spread = bank(HELD_BANK + a, [P, 2, P])
             for e in range(2):
                 nc.tensor.transpose(spread[:, e, :], xs[:, a, e : e + 1].to_broadcast([P, P]), ident[:])
             dst = xs_all[:, 2 * P * a : 2 * P * (a + 1)].rearrange("m (p e) -> m p e", e=2)
@@ -105,15 +109,15 @@ def tile_mppi_control_update_s13_kernel(tc, x_bytes, x_scale, w, base, ratio, ep
 
         ratio_all = buf("ratio_all", 1, [P, NG, KP], BF16)
 
-        def spread_ratio(pair):
-            spread = bank(7, [P, 2, KP], BF16)
+        def spread_ratio(half):
+            spread = bank(HELD_BANK + ND - 1, [P, 2, KP], BF16)
             for a in range(2):
-                g = 2 * pair + a
+                g = 2 * half + a
                 nc.tensor.matmul(
                     spread[:, a, :], lhsT=ones[:], rhs=ratio_row[:, KP * g : KP * (g + 1)], start=True, stop=True
                 )
             nc.scalar.copy(
-                out=ratio_all[:, 2 * pair : 2 * pair + 2, :].bitcast(F32).rearrange("p a (u i) -> p a u i", u=2),
+                out=ratio_all[:, 2 * half : 2 * half + 2, :].bitcast(F32).rearrange("p a (u i) -> p a u i", u=2),
                 in_=spread[:].bitcast(F32).rearrange("p a (i u) -> p a u i", u=2),
             )
 
@@ -121,20 +125,21 @@ def tile_mppi_control_update_s13_kernel(tc, x_bytes, x_scale, w, base, ratio, ep
         w_codes = [buf("w_codes", NQ, [P, C], U32) for q in range(NQ)]
         w_scales = [buf("w_scales", NQ, [P, C], U8) for q in range(NQ)]
 
-        def interleave_w(q, pair, number):
-            src = w_raw[q][:].rearrange("p j (h m e) -> p h e m j", m=P, e=2)
-            mixed = bank(number, [P, 2, KP], BF16)
-            for a in range(2):
-                nc.tensor.matmul(mixed[:, a, :], lhsT=ident_bf[:], rhs=src[:, pair, a], start=True, stop=True)
+        def w_by_tile(q):
+            return w_raw[q][:].rearrange("p j (h m e) -> p h e m j", m=P, e=2)
+
+        def group_w_on_tensor(q, pair, number):
+            grouped = bank(number, [P, 2, KP], BF16)
+            for e in range(2):
+                nc.tensor.matmul(grouped[:, e, :], lhsT=ident_bf[:], rhs=w_by_tile(q)[:, pair, e], start=True, stop=True)
             nc.scalar.copy(
-                out=w_grouped[q][:, 2 * P * pair : 2 * P * (pair + 1), :].rearrange("p c j -> p (c j)"),
-                in_=mixed[:].rearrange("p a n -> p (a n)"),
+                out=w_grouped[q][:, PAIR * pair : PAIR * (pair + 1), :].rearrange("p c j -> p (c j)"),
+                in_=grouped[:].rearrange("p e n -> p (e n)"),
             )
 
-        def interleave_w_copy(q, pair):
-            src = w_raw[q][:].rearrange("p j (h m e) -> p h e m j", m=P, e=2)
+        def group_w_on_scalar(q, pair):
             dst = w_grouped[q][:].rearrange("p (h e m) j -> p h e m j", m=P, e=2)
-            nc.scalar.copy(out=dst[:, pair], in_=src[:, pair])
+            nc.scalar.copy(out=dst[:, pair], in_=w_by_tile(q)[:, pair])
 
         def quantise_w(q, cols):
             nc.vector.quantize_mx(
@@ -143,86 +148,117 @@ def tile_mppi_control_update_s13_kernel(tc, x_bytes, x_scale, w, base, ratio, ep
                 in_=w_grouped[q][:, cols, :].rearrange("p c j -> p (c j)"),
             )
 
-        xf, xt, xg, x_codes, x_scales = {}, {}, {}, {}, {}
-        cost, ex, kept, diff, eb, wt, wg, acc = {}, {}, {}, {}, {}, {}, {}, {}
-        m_codes = [buf("m_codes", NC, [P, NG * P], U32) for ct in range(NC)]
-        m_scales = [buf("m_scales", NC, [P, NG * P], U8) for ct in range(NC)]
+        x_scaled, x_turned, x_grouped, x_codes, x_scales = {}, {}, {}, {}, {}
 
         def scale_x(j, a, parts=1):
             g, t = divmod(2 * j + a, NT)
-            xf[j, a] = buf("xf", 4, [P, F], BF16)
+            x_scaled[j, a] = buf("x_scaled", 4, [P, F], BF16)
             src = x_first[t][:] if g == 0 else x_rest[g - 1][:, t, :]
             for part in range(parts):
                 ks = slice(F // parts * part, F // parts * (part + 1))
                 nc.vector.tensor_tensor(
-                    out=xf[j, a][:, ks], in0=src[:, ks].bitcast(FP8), in1=xs_all[:, ks], op=ALU.mult
+                    out=x_scaled[j, a][:, ks], in0=src[:, ks].bitcast(FP8), in1=xs_all[:, ks], op=ALU.mult
                 )
 
         def turn_x(j, a):
-            xt[j, a] = bank(a, [P, NQ, 2, P])
-            words = xf[j, a][:].bitcast(F32)
+            x_turned[j, a] = bank(X_BANKS[a], [P, NQ, 2, P])
+            words = x_scaled[j, a][:].bitcast(F32)
             for q in range(NQ):
                 for u in range(2):
-                    nc.tensor.transpose(xt[j, a][:, q, u, :], words[:, 256 * q + u : 256 * (q + 1) : 2], ident[:])
+                    nc.tensor.transpose(x_turned[j, a][:, q, u, :], words[:, 256 * q + u : 256 * (q + 1) : 2], ident[:])
 
         def empty_x(j, a):
             if a == 0:
-                xg[j] = buf("xg", 3, [P, NQ, HALF, 4], BF16)
+                x_grouped[j] = buf("x_grouped", 3, [P, NQ, UNIT, 4], BF16)
             nc.scalar.copy(
-                out=xg[j][:, :, P * a : P * (a + 1), :].bitcast(F32),
-                in_=xt[j, a][:].rearrange("p q u r -> p q r u"),
+                out=x_grouped[j][:, :, P * a : P * (a + 1), :].bitcast(F32),
+                in_=x_turned[j, a][:].rearrange("p q u r -> p q r u"),
             )
 
         def quantise_x(j):
-            x_codes[j] = buf("x_codes", 3, [P, NQ * HALF], U32)
-            x_scales[j] = buf("x_scales", 3, [P, NQ * HALF], U8)
+            x_codes[j] = buf("x_codes", 3, [P, NQ * UNIT], U32)
+            x_scales[j] = buf("x_scales", 3, [P, NQ * UNIT], U8)
             nc.vector.quantize_mx(
                 out=x_codes[j][:].bitcast(FP8X4),
                 scales=x_scales[j][:],
-                in_=xg[j][:].rearrange("p q r j -> p (q r j)"),
+                in_=x_grouped[j][:].rearrange("p q r j -> p (q r j)"),
             )
 
-        def product1(j, pair, number):
-            cost[j, pair] = bank(number, [P, 2, HALF])
-            for a in range(2):
-                for q in range(NQ):
-                    if pair == 0:
-                        goals, rows = slice(P * a, P * (a + 1)), slice(HALF * q, HALF * (q + 1))
-                        still = w_codes[q][:, goals], w_scales[q][:, goals]
-                        moving = x_codes[j][:, rows], x_scales[j][:, rows]
-                    else:
-                        goals, rows = slice(C // 2, C), slice(HALF * q + P * a, HALF * q + P * (a + 1))
-                        still = x_codes[j][:, rows], x_scales[j][:, rows]
-                        moving = w_codes[q][:, goals], w_scales[q][:, goals]
-                    nc.tensor.matmul_mx(
-                        out=cost[j, pair][:, a, :],
-                        lhsT=still[0].bitcast(FP8X4),
-                        lhsT_scale=still[1],
-                        rhs=moving[0].bitcast(FP8X4),
-                        rhs_scale=moving[1],
-                        start=(q == 0),
-                        stop=(q == NQ - 1),
-                    )
+        expo, kept, diff, scaled, turned, grouped_m = {}, {}, {}, {}, {}, {}
+        m_codes = [buf("m_codes", NC, [P, NG * P], U32) for ct in range(NC)]
+        m_scales = [buf("m_scales", NC, [P, NG * P], U8) for ct in range(NC)]
 
-        def exponential(j, pair):
+        def cost_group(dst, still, moving):
+            for q in range(NQ):
+                nc.tensor.matmul_mx(
+                    out=dst,
+                    lhsT=still(q)[0].bitcast(FP8X4),
+                    lhsT_scale=still(q)[1],
+                    rhs=moving(q)[0].bitcast(FP8X4),
+                    rhs_scale=moving(q)[1],
+                    start=(q == 0),
+                    stop=(q == NQ - 1),
+                )
+
+        def w_cols(first, n):
+            return lambda q: (w_codes[q][:, first : first + n], w_scales[q][:, first : first + n])
+
+        def x_cols(j, first, n):
+            def cols(q):
+                rows = slice(UNIT * q + first, UNIT * q + first + n)
+                return x_codes[j][:, rows], x_scales[j][:, rows]
+
+            return cols
+
+        def costs_by_goal(j, number):
             g, h = divmod(j, 2)
-            if pair == 1:
-                if h == 0:
-                    kept[g] = buf("kept", NG, [P, 2, C // 2, 2], F32)
-                nc.scalar.copy(out=kept[g][:, h], in_=cost[j, pair][:].rearrange("p a c -> p c a"))
-                return
+            cost = bank(number, [P, 2, UNIT])
+            for ct in range(2):
+                cost_group(cost[:, ct, :], w_cols(P * ct, P), x_cols(j, 0, UNIT))
             for ct in range(2):
                 if h == 0:
-                    ex[g, ct] = buf("ex", 3 * NG, [P, KP], F32)
+                    expo[g, ct] = buf("expo", 3 * NG, [P, KP], F32)
                 nc.scalar.activation(
-                    out=ex[g, ct][:, HALF * h : HALF * (h + 1)].rearrange("p (i a) -> p i a", a=2),
-                    in_=cost[j, pair][:, ct, :].rearrange("p (a i) -> p i a", a=2),
+                    out=expo[g, ct][:, UNIT * h : UNIT * (h + 1)].rearrange("p (r a) -> p r a", a=2),
+                    in_=cost[:, ct, :].rearrange("p (a r) -> p r a", a=2),
                     func=ACT.Exp,
-                    bias=base_bf[:, ct : ct + 1],
+                    bias=base_own[:, ct : ct + 1],
                     scale=-1.0,
                 )
 
+        def costs_by_rollout(j, number):
+            g, h = divmod(j, 2)
+            cost = bank(number, [P, 2, PAIR])
+            for a in range(2):
+                cost_group(cost[:, a, :], x_cols(j, P * a, P), w_cols(PAIR, PAIR))
+            if h == 0:
+                kept[g] = buf("kept", NG, [P, 2, PAIR, 2], F32)
+            nc.scalar.copy(out=kept[g][:, h], in_=cost[:].rearrange("p a c -> p c a"))
+
+        def times_ratio(g, ct):
+            scaled[g, ct] = buf("scaled", 6, [P, 2, UNIT], BF16)
+            nc.vector.tensor_tensor(
+                out=scaled[g, ct][:].rearrange("p u n -> p (u n)"),
+                in0=expo[g, ct][:],
+                in1=ratio_all[:, g, :],
+                op=ALU.mult,
+            )
+
+        def turn_m(gs, ct, number):
+            turned[gs, ct] = bank(number, [P, len(gs), 2, P])
+            for n in range(len(gs)):
+                for u in range(2):
+                    nc.tensor.transpose(turned[gs, ct][:, n, u, :], scaled[gs[n], ct][:, u, :].bitcast(F32), ident[:])
+
+        def empty_m(gs, ct):
+            grouped_m[gs, ct] = buf("grouped_m", 4, [P, len(gs) * P, 4], BF16)
+            nc.scalar.copy(
+                out=grouped_m[gs, ct][:].bitcast(F32).rearrange("p (n m) u -> p n m u", n=len(gs)),
+                in_=turned[gs, ct][:].rearrange("p n u m -> p n m u"),
+            )
+
         base_twice = buf("base_twice", 1, [P, 2, P, 2], BF16)
+        ratio_rows = buf("ratio_rows", 1, [P, NG, P, NT], BF16)
 
         def double_base():
             nc.scalar.copy(
@@ -230,15 +266,13 @@ def tile_mppi_control_update_s13_kernel(tc, x_bytes, x_scale, w, base, ratio, ep
                 in_=base_all[:].rearrange("p (m e a) -> p e m a", e=2, a=1).to_broadcast([P, 2, P, 2]),
             )
 
-        ratio_rows = buf("ratio_rows", 1, [P, NG, P, NT], BF16)
-
         def repeat_ratio(g):
             nc.scalar.copy(
                 out=ratio_rows[:, g].bitcast(F32),
                 in_=ratio_own[:, g : g + 1, :].bitcast(F32).to_broadcast([P, P, 2]),
             )
 
-        def late_difference(g, ct):
+        def minus_base(g, ct):
             e = ct - 2
             diff[g, ct] = buf("diff", 6, [P, 2, P, 2], F32)
             nc.vector.tensor_tensor(
@@ -249,48 +283,22 @@ def tile_mppi_control_update_s13_kernel(tc, x_bytes, x_scale, w, base, ratio, ep
             )
 
         def late_exponential(g, ct):
-            ex[g, ct] = buf("ex", 3 * NG, [P, KP], F32)
+            expo[g, ct] = buf("expo", 3 * NG, [P, KP], F32)
             nc.scalar.activation(
-                out=ex[g, ct][:].rearrange("p (m h a) -> p m h a", h=2, a=2),
+                out=expo[g, ct][:].rearrange("p (m h a) -> p m h a", h=2, a=2),
                 in_=diff[g, ct][:].rearrange("p h m a -> p m h a"),
                 func=ACT.Exp,
                 scale=-1.0,
             )
 
         def late_ratio(gs, n, ct):
-            g = gs[n]
             if n == 0:
-                wg[gs, ct] = buf("wg", 4, [P, 2 * P, 4], BF16)
+                grouped_m[gs, ct] = buf("grouped_m", 4, [P, 2 * P, 4], BF16)
             nc.vector.tensor_tensor(
-                out=wg[gs, ct][:, P * n : P * (n + 1), :].rearrange("p m t -> p (m t)"),
-                in0=ex[g, ct][:],
-                in1=ratio_rows[:, g].rearrange("p m t -> p (m t)"),
+                out=grouped_m[gs, ct][:, P * n : P * (n + 1), :].rearrange("p m t -> p (m t)"),
+                in0=expo[gs[n], ct][:],
+                in1=ratio_rows[:, gs[n]].rearrange("p m t -> p (m t)"),
                 op=ALU.mult,
-            )
-
-        def times_ratio(g, ct):
-            eb[g, ct] = buf("eb", 6, [P, 2, 256], BF16)
-            nc.vector.tensor_tensor(
-                out=eb[g, ct][:].rearrange("p u n -> p (u n)"),
-                in0=ex[g, ct][:],
-                in1=ratio_all[:, g, :],
-                op=ALU.mult,
-            )
-
-        def turn_m(gs, ct, number):
-            n = len(gs)
-            wt[gs, ct] = bank(number, [P, n, 2, P])
-            for a in range(n):
-                for u in range(2):
-                    nc.tensor.transpose(wt[gs, ct][:, a, u, :], eb[gs[a], ct][:, u, :].bitcast(F32), ident[:])
-
-        def empty_m(gs, ct, engine):
-            n = len(gs)
-            wg[gs, ct] = buf("wg", 4, [P, n * P, 4], BF16)
-            copy_on(
-                engine,
-                wg[gs, ct][:].bitcast(F32).rearrange("p (a c) u -> p a c u", a=n),
-                wt[gs, ct][:].rearrange("p a u c -> p a c u"),
             )
 
         def quantise_m(gs, ct):
@@ -298,8 +306,13 @@ def tile_mppi_control_update_s13_kernel(tc, x_bytes, x_scale, w, base, ratio, ep
             nc.vector.quantize_mx(
                 out=m_codes[ct][:, cols].bitcast(FP8X4),
                 scales=m_scales[ct][:, cols],
-                in_=wg[gs, ct][:].rearrange("p c j -> p (c j)"),
+                in_=grouped_m[gs, ct][:].rearrange("p c j -> p (c j)"),
             )
+
+        acc = {}
+        wide = [slice(NB * dt, NB * (dt + 1)) for dt in range(ND)]
+        narrow = [slice(D - NB + P * n, D - NB + P * (n + 1)) for n in range(NB // P)]
+        out_rows = out.rearrange("(h p e) d -> h e p d", p=P, e=2)
 
         def product2(ct, ds, g, number):
             if g == 0:
@@ -310,14 +323,10 @@ def tile_mppi_control_update_s13_kernel(tc, x_bytes, x_scale, w, base, ratio, ep
                 lhsT=m_codes[ct][:, cols].bitcast(FP8X4),
                 lhsT_scale=m_scales[ct][:, cols],
                 rhs=e_words[g][:, 2 * ds.start : 2 * ds.stop].bitcast(FP4X4),
-                rhs_scale=e_plane[:, g, ds],
+                rhs_scale=e_scales[:, g, ds],
                 start=(g == 0),
                 stop=(g == NG - 1),
             )
-
-        wide = [slice(NB * dt, NB * (dt + 1)) for dt in range(ND)]
-        narrow = [slice(D - NB + P * n, D - NB + P * (n + 1)) for n in range(NB // P)]
-        out_rows = out.rearrange("(h p e) d -> h e p d", p=P, e=2)
 
         def finish(ct, ds, engine, parts=1):
             width = (ds.stop - ds.start) // parts
@@ -327,52 +336,48 @@ def tile_mppi_control_update_s13_kernel(tc, x_bytes, x_scale, w, base, ratio, ep
                 first = ds.start + width * part
                 nc.sync.dma_start(out=out_rows[ct // 2, ct % 2][:, first : first + width], in_=res[:])
 
-        def first_goals(g, dts):
+        def held_passes(g, dts):
             for dt in dts:
-                product2(0, wide[dt], g, 4 + dt)
-
-        def costs(j, pair, number):
-            product1(j, pair, number)
-            exponential(j, pair)
+                product2(0, wide[dt], g, HELD_BANK + dt)
 
         last = NG - 1
-        interleave_w_copy(0, 1)
-        interleave_w(0, 0, 2)
+        group_w_on_scalar(0, 1)
+        group_w_on_tensor(0, 0, COST_BANKS[0])
         for j in range(2 * NG):
             g, odd = divmod(j, 2)
             scale_x(j, 0, XS_PARTS if j == 0 else 1)
             if j == 1:
                 quantise_w(0, slice(0, C))
             if j == 2:
-                quantise_w(1, slice(C // 2, C))
+                quantise_w(1, slice(PAIR, C))
             if g >= 2 and not odd:
                 quantise_m((g - 2,), 0)
-                first_goals(g - 2, (0, 1))
+                held_passes(g - 2, (0, 1))
             scale_x(j, 1)
             turn_x(j, 0)
             empty_x(j, 0)
-            if j < 2:
-                interleave_w(1, j, 4 + j)
+            if g == 0:
+                group_w_on_tensor(1, j, HELD_BANK + j)
             if g == 1:
-                costs(j - 2, 1, 3)
+                costs_by_rollout(j - 2, COST_BANKS[1])
             turn_x(j, 1)
             if g >= 1 and odd:
                 times_ratio(g - 1, 0)
-                turn_m((g - 1,), 0, 3 if g > 1 else 6)
-                empty_m((g - 1,), 0, "scalar")
+                turn_m((g - 1,), 0, COST_BANKS[1] if g > 1 else HELD_BANK + 2)
+                empty_m((g - 1,), 0)
             empty_x(j, 1)
             if j == 1:
-                quantise_w(1, slice(0, C // 2))
+                quantise_w(1, slice(0, PAIR))
             if j >= 1:
                 quantise_x(j - 1)
-                costs(j - 1, 0, 2)
+                costs_by_goal(j - 1, COST_BANKS[0])
                 if j <= 2:
                     spread_ratio(j - 1)
                 if g >= 2 and not odd:
                     repeat_ratio(g - 1)
-                    first_goals(g - 2, (2, 3))
+                    held_passes(g - 2, (2, 3))
                 if j >= 3:
-                    costs(j - 1, 1, 3)
+                    costs_by_rollout(j - 1, COST_BANKS[1])
                 if j == 3:
                     repeat_ratio(0)
                 if j == 5:
@@ -383,50 +388,21 @@ def tile_mppi_control_update_s13_kernel(tc, x_bytes, x_scale, w, base, ratio, ep
         times_ratio(0, 1)
         times_ratio(1, 1)
         turn_m(early, 1, 0)
-        empty_m(early, 1, "scalar")
+        empty_m(early, 1)
         repeat_ratio(last)
         quantise_m((last - 1,), 0)
         quantise_x(end)
-        first_goals(last - 1, (0, 1))
-        costs(end, 0, 1)
-        costs(end, 1, 2)
-        first_goals(last - 1, (2, 3))
+        held_passes(last - 1, (0, 1))
+        costs_by_goal(end, 1)
+        costs_by_rollout(end, 2)
+        held_passes(last - 1, (2, 3))
         times_ratio(2, 1)
-        late_difference(0, 2)
+        minus_base(0, 2)
         quantise_m(early, 1)
-        late_difference(1, 2)
+        minus_base(1, 2)
         times_ratio(last, 0)
         times_ratio(last, 1)
-        for g in early:
-            product2(1, wide[0], g, 0)
-        turn_m((last,), 0, 1)
-        turn_m(late, 1, 2)
-        late_exponential(0, 2)
-        empty_m((last,), 0, "scalar")
-        empty_m(late, 1, "scalar")
-        late_exponential(1, 2)
-        late_difference(2, 2)
-        quantise_m((last,), 0)
-        late_difference(last, 2)
-        quantise_m(late, 1)
-        for g in early:
-            product2(1, wide[1], g, 3)
-        first_goals(last, range(ND))
-        for n in range(2):
-            late_ratio(early, n, 2)
-        late_difference(0, 3)
-        for n in range(2):
-            finish(0, wide[n], "scalar")
-            late_exponential(late[n], 2)
-            late_ratio(late, n, 2)
-            if n == 0:
-                quantise_m(early, 2)
-        late_difference(1, 3)
-        quantise_m(late, 2)
-        for g in late:
-            late_difference(g, 3)
-        for dt in range(2, ND):
-            finish(0, wide[dt], "scalar")
+
         banks = (0, 3, 1, 2, 4, 5, 6, 7, 0, 3, 1)
 
         def passes(ct, dts, gs):
@@ -434,25 +410,53 @@ def tile_mppi_control_update_s13_kernel(tc, x_bytes, x_scale, w, base, ratio, ep
                 for g in gs:
                     product2(ct, wide[dt], g, banks[ND * (ct - 1) + dt])
 
+        passes(1, (0,), early)
+        turn_m((last,), 0, 1)
+        turn_m(late, 1, 2)
+        late_exponential(0, 2)
+        empty_m((last,), 0)
+        empty_m(late, 1)
+        late_exponential(1, 2)
+        minus_base(2, 2)
+        quantise_m((last,), 0)
+        minus_base(last, 2)
+        quantise_m(late, 1)
+        passes(1, (1,), early)
+        held_passes(last, range(ND))
+
+        for n in range(2):
+            late_ratio(early, n, 2)
+        minus_base(0, 3)
+        for n in range(2):
+            finish(0, wide[n], "scalar")
+            late_exponential(late[n], 2)
+            late_ratio(late, n, 2)
+            if n == 0:
+                quantise_m(early, 2)
+        minus_base(1, 3)
+        quantise_m(late, 2)
+        for g in late:
+            minus_base(g, 3)
+        for dt in range(2, ND):
+            finish(0, wide[dt], "scalar")
         passes(1, (0, 1), late)
         passes(1, (2, 3), range(NG))
         passes(2, (0, 1), early)
         passes(2, (0, 1), late)
-        for dt in range(3):
+        for dt in range(ND - 1):
             finish(1, wide[dt], "scalar")
         for n in range(2):
             late_exponential(early[n], 3)
-        finish(1, wide[3], "vector")
-        for n in range(2):
             late_ratio(early, n, 3)
         for n in range(2):
             late_exponential(late[n], 3)
-        late_ratio(late, 0, 3)
-        quantise_m(early, 3)
-        late_ratio(late, 1, 3)
-        finish(2, wide[0], "scalar")
-        finish(2, wide[1], "scalar")
+            late_ratio(late, n, 3)
+            if n == 0:
+                quantise_m(early, 3)
+                finish(1, wide[ND - 1], "scalar")
         quantise_m(late, 3)
+        for dt in range(2):
+            finish(2, wide[dt], "scalar")
         passes(2, (2, 3), range(NG))
         passes(3, (0, 1), early)
         passes(3, (0, 1), late)
@@ -464,5 +468,5 @@ def tile_mppi_control_update_s13_kernel(tc, x_bytes, x_scale, w, base, ratio, ep
         finish(3, wide[2], "scalar", 2)
         for n in range(NB // P):
             for g in range(NG):
-                product2(3, narrow[n], g, 4 + n)
+                product2(3, narrow[n], g, HELD_BANK + n)
             finish(3, narrow[n], "vector" if n % 2 == 0 else "scalar")

@@ -26,6 +26,7 @@ ND = D // NB
 UNIT = KP // 2
 PAIR = C // 2
 XS_PARTS = 4
+REP = 16
 X_BANKS = (0, 1)
 COST_BANKS = (2, 3)
 HELD_BANK = 4
@@ -57,10 +58,6 @@ def tile_mppi_control_update_s13_kernel(tc, x_bytes, x_scale, w, base, ratio, ep
 
         ident = buf("ident", 1, [P, P], F32)
         make_identity(nc, ident[:])
-        ratio_row = buf("ratio_row", 1, [P, S], BF16)
-        nc.vector.memset(ratio_row[:].bitcast(I32), 0)
-        ones = buf("ones", 1, [P, P], BF16)
-        nc.vector.memset(ones[:], 1.0)
         ident_bf = buf("ident_bf", 1, [P, P], BF16)
         nc.vector.tensor_copy(out=ident_bf[:], in_=ident[:])
         e_scales = buf("e_scales", 1, [P, NG, D], U8)
@@ -75,11 +72,17 @@ def tile_mppi_control_update_s13_kernel(tc, x_bytes, x_scale, w, base, ratio, ep
             nc.sync.dma_start(out=x_first[t][:], in_=x_rows[0][:, t, :])
             if t < NQ:
                 nc.sync.dma_start(out=w_raw[t][:], in_=w_rows[t])
-        nc.sync.dma_start(out=ratio_row[0:1, :], in_=ratio.rearrange("(o s) -> o s", o=1))
         base_own = buf("base_own", 1, [P, 2], BF16)
         nc.sync.dma_start(out=base_own[:], in_=base[:PAIR].rearrange("(p e) -> p e", e=2))
+        ratio_all = [buf("ratio_all", 2, [P, 2 * KP], BF16) for half in range(2)]
+
+        def spread_ratio(half):
+            nc.sync.dma_start(out=ratio_all[half][:], in_=ratio[2 * KP * half : 2 * KP * (half + 1)].partition_broadcast(P))
+
         for g in range(1, NG - 1):
             nc.sync.dma_start(out=x_rest[g - 1][:], in_=x_rows[g])
+            if g == 1:
+                spread_ratio(0)
         e_rows = eps_scales.bitcast(I32).rearrange("g q n -> q g n")
         for quad in range(4):
             nc.sync.dma_start(
@@ -90,8 +93,10 @@ def tile_mppi_control_update_s13_kernel(tc, x_bytes, x_scale, w, base, ratio, ep
         for g in range(NG):
             nc.sync.dma_start(out=e_words[g][:], in_=eps_words[g])
             if g == 0:
-                nc.sync.dma_start(out=ratio_own[:], in_=ratio.rearrange("(g p t) -> p g t", p=P, t=NT))
                 nc.sync.dma_start(out=x_rest[NG - 2][:], in_=x_rows[NG - 1])
+            if g == 1:
+                spread_ratio(1)
+        nc.sync.dma_start(out=ratio_own[:], in_=ratio.rearrange("(g p t) -> p g t", p=P, t=NT))
         base_all = buf("base_all", 1, [P, PAIR], BF16)
         nc.sync.dma_start(out=base_all[:], in_=base[PAIR:].partition_broadcast(P))
 
@@ -106,20 +111,6 @@ def tile_mppi_control_update_s13_kernel(tc, x_bytes, x_scale, w, base, ratio, ep
                 nc.vector.tensor_copy(out=dst, in_=src)
             else:
                 nc.scalar.activation(out=dst, in_=src, func=ACT.Copy)
-
-        ratio_all = buf("ratio_all", 1, [P, NG, KP], BF16)
-
-        def spread_ratio(half):
-            spread = bank(HELD_BANK + ND - 1, [P, 2, KP], BF16)
-            for a in range(2):
-                g = 2 * half + a
-                nc.tensor.matmul(
-                    spread[:, a, :], lhsT=ones[:], rhs=ratio_row[:, KP * g : KP * (g + 1)], start=True, stop=True
-                )
-            nc.scalar.copy(
-                out=ratio_all[:, 2 * half : 2 * half + 2, :].bitcast(F32).rearrange("p a (u i) -> p a u i", u=2),
-                in_=spread[:].bitcast(F32).rearrange("p a (i u) -> p a u i", u=2),
-            )
 
         w_grouped = [buf("w_grouped", NQ, [P, C, 4], BF16) for q in range(NQ)]
         w_codes = [buf("w_codes", NQ, [P, C], U32) for q in range(NQ)]
@@ -160,31 +151,33 @@ def tile_mppi_control_update_s13_kernel(tc, x_bytes, x_scale, w, base, ratio, ep
                     out=x_scaled[j, a][:, ks], in0=src[:, ks].bitcast(FP8), in1=xs_all[:, ks], op=ALU.mult
                 )
 
-        def turn_x(j, a):
-            x_turned[j, a] = bank(X_BANKS[a], [P, NQ, 2, P])
+        def turn_x(j, a, qs=(0, 1), number=None):
+            x_turned[j, a, qs] = bank(X_BANKS[a] if number is None else number, [P, len(qs), 2, P])
             words = x_scaled[j, a][:].bitcast(F32)
-            for q in range(NQ):
+            for n in range(len(qs)):
                 for u in range(2):
-                    nc.tensor.transpose(x_turned[j, a][:, q, u, :], words[:, 256 * q + u : 256 * (q + 1) : 2], ident[:])
+                    first = 256 * qs[n]
+                    nc.tensor.transpose(x_turned[j, a, qs][:, n, u, :], words[:, first + u : first + 256 : 2], ident[:])
 
-        def empty_x(j, a):
+        def empty_x(j, a, qs=(0, 1)):
             if a == 0:
                 x_grouped[j] = buf("x_grouped", 3, [P, NQ, UNIT, 4], BF16)
             nc.scalar.copy(
-                out=x_grouped[j][:, :, P * a : P * (a + 1), :].bitcast(F32),
-                in_=x_turned[j, a][:].rearrange("p q u r -> p q r u"),
+                out=x_grouped[j][:, qs[0] : qs[-1] + 1, P * a : P * (a + 1), :].bitcast(F32),
+                in_=x_turned[j, a, qs][:].rearrange("p q u r -> p q r u"),
             )
 
-        def quantise_x(j):
-            x_codes[j] = buf("x_codes", 3, [P, NQ * UNIT], U32)
-            x_scales[j] = buf("x_scales", 3, [P, NQ * UNIT], U8)
+        def quantise_x(j, first=0, count=NQ * UNIT):
+            if first == 0:
+                x_codes[j] = buf("x_codes", 3, [P, NQ * UNIT], U32)
+                x_scales[j] = buf("x_scales", 3, [P, NQ * UNIT], U8)
             nc.vector.quantize_mx(
-                out=x_codes[j][:].bitcast(FP8X4),
-                scales=x_scales[j][:],
-                in_=x_grouped[j][:].rearrange("p q r j -> p (q r j)"),
+                out=x_codes[j][:, first : first + count].bitcast(FP8X4),
+                scales=x_scales[j][:, first : first + count],
+                in_=x_grouped[j][:].rearrange("p q r j -> p (q r j)")[:, 4 * first : 4 * (first + count)],
             )
 
-        expo, kept, diff, scaled, turned, grouped_m = {}, {}, {}, {}, {}, {}
+        by_goal, by_rollout, expo, kept, diff, scaled, turned, grouped_m = {}, {}, {}, {}, {}, {}, {}, {}
         m_codes = [buf("m_codes", NC, [P, NG * P], U32) for ct in range(NC)]
         m_scales = [buf("m_scales", NC, [P, NG * P], U8) for ct in range(NC)]
 
@@ -211,10 +204,13 @@ def tile_mppi_control_update_s13_kernel(tc, x_bytes, x_scale, w, base, ratio, ep
             return cols
 
         def costs_by_goal(j, number):
-            g, h = divmod(j, 2)
-            cost = bank(number, [P, 2, UNIT])
+            by_goal[j] = bank(number, [P, 2, UNIT])
             for ct in range(2):
-                cost_group(cost[:, ct, :], w_cols(P * ct, P), x_cols(j, 0, UNIT))
+                cost_group(by_goal[j][:, ct, :], w_cols(P * ct, P), x_cols(j, 0, UNIT))
+
+        def exponentials(j):
+            g, h = divmod(j, 2)
+            cost = by_goal[j]
             for ct in range(2):
                 if h == 0:
                     expo[g, ct] = buf("expo", 3 * NG, [P, KP], F32)
@@ -227,10 +223,13 @@ def tile_mppi_control_update_s13_kernel(tc, x_bytes, x_scale, w, base, ratio, ep
                 )
 
         def costs_by_rollout(j, number):
-            g, h = divmod(j, 2)
-            cost = bank(number, [P, 2, PAIR])
+            by_rollout[j] = bank(number, [P, 2, PAIR])
             for a in range(2):
-                cost_group(cost[:, a, :], x_cols(j, P * a, P), w_cols(PAIR, PAIR))
+                cost_group(by_rollout[j][:, a, :], x_cols(j, P * a, P), w_cols(PAIR, PAIR))
+
+        def keep_costs(j):
+            g, h = divmod(j, 2)
+            cost = by_rollout[j]
             if h == 0:
                 kept[g] = buf("kept", NG, [P, 2, PAIR, 2], F32)
             nc.scalar.copy(out=kept[g][:, h], in_=cost[:].rearrange("p a c -> p c a"))
@@ -238,9 +237,9 @@ def tile_mppi_control_update_s13_kernel(tc, x_bytes, x_scale, w, base, ratio, ep
         def times_ratio(g, ct):
             scaled[g, ct] = buf("scaled", 6, [P, 2, UNIT], BF16)
             nc.vector.tensor_tensor(
-                out=scaled[g, ct][:].rearrange("p u n -> p (u n)"),
-                in0=expo[g, ct][:],
-                in1=ratio_all[:, g, :],
+                out=scaled[g, ct][:].rearrange("p u (i e) -> p u i e", e=2),
+                in0=expo[g, ct][:].rearrange("p (u i e) -> p u i e", u=2, e=2),
+                in1=ratio_all[g // 2][:, KP * (g % 2) : KP * (g % 2 + 1)].rearrange("p (i u e) -> p u i e", u=2, e=2),
                 op=ALU.mult,
             )
 
@@ -258,7 +257,7 @@ def tile_mppi_control_update_s13_kernel(tc, x_bytes, x_scale, w, base, ratio, ep
             )
 
         base_twice = buf("base_twice", 1, [P, 2, P, 2], BF16)
-        ratio_rows = buf("ratio_rows", 1, [P, NG, P, NT], BF16)
+        ratio_rep = buf("ratio_rep", 1, [P, NG, REP, NT], BF16)
 
         def double_base():
             nc.scalar.copy(
@@ -266,10 +265,9 @@ def tile_mppi_control_update_s13_kernel(tc, x_bytes, x_scale, w, base, ratio, ep
                 in_=base_all[:].rearrange("p (m e a) -> p e m a", e=2, a=1).to_broadcast([P, 2, P, 2]),
             )
 
-        def repeat_ratio(g):
+        def repeat_ratio():
             nc.scalar.copy(
-                out=ratio_rows[:, g].bitcast(F32),
-                in_=ratio_own[:, g : g + 1, :].bitcast(F32).to_broadcast([P, P, 2]),
+                out=ratio_rep[:].bitcast(F32), in_=ratio_own[:].bitcast(F32).unsqueeze(2).to_broadcast([P, NG, REP, 2])
             )
 
         def minus_base(g, ct):
@@ -295,18 +293,19 @@ def tile_mppi_control_update_s13_kernel(tc, x_bytes, x_scale, w, base, ratio, ep
             if n == 0:
                 grouped_m[gs, ct] = buf("grouped_m", 4, [P, 2 * P, 4], BF16)
             nc.vector.tensor_tensor(
-                out=grouped_m[gs, ct][:, P * n : P * (n + 1), :].rearrange("p m t -> p (m t)"),
-                in0=expo[gs[n], ct][:],
-                in1=ratio_rows[:, gs[n]].rearrange("p m t -> p (m t)"),
+                out=grouped_m[gs, ct][:, P * n : P * (n + 1), :].rearrange("p (h m) t -> p h (m t)", m=REP),
+                in0=expo[gs[n], ct][:].rearrange("p (h x) -> p h x", x=REP * NT),
+                in1=ratio_rep[:, gs[n] : gs[n] + 1].rearrange("p o m t -> p o (m t)").to_broadcast([P, P // REP, REP * NT]),
                 op=ALU.mult,
             )
 
-        def quantise_m(gs, ct):
-            cols = slice(P * gs[0], P * (gs[-1] + 1))
+        def quantise_m(gs, ct, only=None):
+            first, count = (0, len(gs)) if only is None else (only, 1)
+            cols = slice(P * gs[first], P * (gs[first] + count))
             nc.vector.quantize_mx(
                 out=m_codes[ct][:, cols].bitcast(FP8X4),
                 scales=m_scales[ct][:, cols],
-                in_=grouped_m[gs, ct][:].rearrange("p c j -> p (c j)"),
+                in_=grouped_m[gs, ct][:, P * first : P * (first + count), :].rearrange("p c j -> p (c j)"),
             )
 
         acc = {}
@@ -353,117 +352,126 @@ def tile_mppi_control_update_s13_kernel(tc, x_bytes, x_scale, w, base, ratio, ep
             if g >= 2 and not odd:
                 quantise_m((g - 2,), 0)
                 held_passes(g - 2, (0, 1))
-            scale_x(j, 1)
+            scale_x(j, 1, NQ if j == 2 * NG - 1 else 1)
             turn_x(j, 0)
             empty_x(j, 0)
             if g == 0:
                 group_w_on_tensor(1, j, HELD_BANK + j)
             if g == 1:
                 costs_by_rollout(j - 2, COST_BANKS[1])
-            turn_x(j, 1)
+                keep_costs(j - 2)
+            if j < 2 * NG - 1:
+                turn_x(j, 1)
+            else:
+                for q in range(NQ):
+                    turn_x(j, 1, (q,), 1 + q)
+                    empty_x(j, 1, (q,))
             if g >= 1 and odd:
                 times_ratio(g - 1, 0)
                 turn_m((g - 1,), 0, COST_BANKS[1] if g > 1 else HELD_BANK + 2)
                 empty_m((g - 1,), 0)
-            empty_x(j, 1)
+            if j < 2 * NG - 1:
+                empty_x(j, 1)
             if j == 1:
                 quantise_w(1, slice(0, PAIR))
             if j >= 1:
                 quantise_x(j - 1)
-                costs_by_goal(j - 1, COST_BANKS[0])
-                if j <= 2:
-                    spread_ratio(j - 1)
+                if g >= 2 and odd:
+                    held_passes(g - 2, (3,))
+                costs_by_goal(j - 1, COST_BANKS[0] if j < 2 * NG - 1 else 0)
+                exponentials(j - 1)
                 if g >= 2 and not odd:
-                    repeat_ratio(g - 1)
-                    held_passes(g - 2, (2, 3))
+                    held_passes(g - 2, (2,))
                 if j >= 3:
-                    costs_by_rollout(j - 1, COST_BANKS[1])
-                if j == 3:
-                    repeat_ratio(0)
+                    costs_by_rollout(j - 1, COST_BANKS[1] if j < 2 * NG - 1 else 1)
+                    keep_costs(j - 1)
                 if j == 5:
                     double_base()
+                if j == 4:
+                    repeat_ratio()
 
         early, late = (0, 1), (2, last)
         end = 2 * NG - 1
         times_ratio(0, 1)
+        quantise_x(end, 0, UNIT)
+        quantise_x(end, UNIT, UNIT)
+        quantise_m((last - 1,), 0)
         times_ratio(1, 1)
+        times_ratio(2, 1)
+        costs_by_goal(end, 2)
+        exponentials(end)
+        costs_by_rollout(end, 3)
         turn_m(early, 1, 0)
         empty_m(early, 1)
-        repeat_ratio(last)
-        quantise_m((last - 1,), 0)
-        quantise_x(end)
-        held_passes(last - 1, (0, 1))
-        costs_by_goal(end, 1)
-        costs_by_rollout(end, 2)
-        held_passes(last - 1, (2, 3))
-        times_ratio(2, 1)
+        keep_costs(end)
+        held_passes(last - 1, range(ND))
         minus_base(0, 2)
-        quantise_m(early, 1)
-        minus_base(1, 2)
         times_ratio(last, 0)
         times_ratio(last, 1)
+        quantise_m(early, 1)
+        minus_base(1, 2)
 
-        banks = (0, 3, 1, 2, 4, 5, 6, 7, 0, 3, 1)
+        banks = (3, 0, 1, 2, 4, 5, 6, 7, 3, 0, 1)
 
         def passes(ct, dts, gs):
             for dt in dts:
                 for g in gs:
                     product2(ct, wide[dt], g, banks[ND * (ct - 1) + dt])
 
-        passes(1, (0,), early)
         turn_m((last,), 0, 1)
         turn_m(late, 1, 2)
         late_exponential(0, 2)
         empty_m((last,), 0)
         empty_m(late, 1)
-        late_exponential(1, 2)
-        minus_base(2, 2)
+        passes(1, (0, 1), early)
         quantise_m((last,), 0)
-        minus_base(last, 2)
+        minus_base(2, 2)
         quantise_m(late, 1)
-        passes(1, (1,), early)
+        minus_base(last, 2)
+        late_exponential(1, 2)
         held_passes(last, range(ND))
+        passes(1, (0, 1), late)
+        passes(1, (2, 3), range(NG))
 
-        for n in range(2):
-            late_ratio(early, n, 2)
-        minus_base(0, 3)
         for n in range(2):
             finish(0, wide[n], "scalar")
             late_exponential(late[n], 2)
-            late_ratio(late, n, 2)
-            if n == 0:
-                quantise_m(early, 2)
-        minus_base(1, 3)
+        for n in range(2):
+            late_ratio(early, n, 2)
+        late_ratio(late, 0, 2)
+        quantise_m(early, 2)
+        late_ratio(late, 1, 2)
+        minus_base(0, 3)
         quantise_m(late, 2)
-        for g in late:
+        for g in range(1, NG):
             minus_base(g, 3)
         for dt in range(2, ND):
             finish(0, wide[dt], "scalar")
-        passes(1, (0, 1), late)
-        passes(1, (2, 3), range(NG))
+        for dt in range(2):
+            finish(1, wide[dt], "scalar")
+        for g in early:
+            late_exponential(g, 3)
+        finish(1, wide[2], "scalar")
+        for g in late:
+            late_exponential(g, 3)
+        finish(1, wide[3], "scalar")
         passes(2, (0, 1), early)
         passes(2, (0, 1), late)
-        for dt in range(ND - 1):
-            finish(1, wide[dt], "scalar")
-        for n in range(2):
-            late_exponential(early[n], 3)
-            late_ratio(early, n, 3)
-        for n in range(2):
-            late_exponential(late[n], 3)
-            late_ratio(late, n, 3)
-            if n == 0:
-                quantise_m(early, 3)
-                finish(1, wide[ND - 1], "scalar")
-        quantise_m(late, 3)
-        for dt in range(2):
-            finish(2, wide[dt], "scalar")
         passes(2, (2, 3), range(NG))
+        for n in range(2):
+            late_ratio(early, n, 3)
+        late_ratio(late, 0, 3)
+        quantise_m(early, 3)
+        late_ratio(late, 1, 3)
+        for n in range(2):
+            quantise_m(late, 3, n)
+        for dt in range(ND):
+            finish(2, wide[dt], "scalar" if dt < ND - 1 else "vector")
         passes(3, (0, 1), early)
-        passes(3, (0, 1), late)
-        finish(2, wide[2], "scalar")
-        finish(2, wide[3], "vector")
-        finish(3, wide[0], "vector")
-        finish(3, wide[1], "scalar")
+        for g in late:
+            passes(3, (0, 1), (g,))
+        finish(3, wide[0], "scalar")
+        finish(3, wide[1], "vector")
         passes(3, (2,), range(NG))
         finish(3, wide[2], "scalar", 2)
         for n in range(NB // P):

@@ -160,7 +160,7 @@ def tile_mppi_control_update_s13_kernel(tc, x_bytes, x_scale, w, base, ratio, ep
                     nc.tensor.transpose(x_turned[j, a, qs][:, n, u, :], words[:, first + u : first + 256 : 2], ident[:])
 
         def empty_x(j, a, qs=(0, 1)):
-            if a == 0:
+            if j not in x_grouped:
                 x_grouped[j] = buf("x_grouped", 3, [P, NQ, UNIT, 4], BF16)
             nc.scalar.copy(
                 out=x_grouped[j][:, qs[0] : qs[-1] + 1, P * a : P * (a + 1), :].bitcast(F32),
@@ -245,7 +245,7 @@ def tile_mppi_control_update_s13_kernel(tc, x_bytes, x_scale, w, base, ratio, ep
 
         def turn_m(gs, ct, number):
             turned[gs, ct] = bank(number, [P, len(gs), 2, P])
-            for n in range(len(gs)):
+            for n in reversed(range(len(gs))):
                 for u in range(2):
                     nc.tensor.transpose(turned[gs, ct][:, n, u, :], scaled[gs[n], ct][:, u, :].bitcast(F32), ident[:])
 
@@ -308,14 +308,16 @@ def tile_mppi_control_update_s13_kernel(tc, x_bytes, x_scale, w, base, ratio, ep
                 in_=grouped_m[gs, ct][:, P * first : P * (first + count), :].rearrange("p c j -> p (c j)"),
             )
 
-        acc = {}
+        acc, done = {}, {}
         wide = [slice(NB * dt, NB * (dt + 1)) for dt in range(ND)]
         narrow = [slice(D - NB + P * n, D - NB + P * (n + 1)) for n in range(NB // P)]
         out_rows = out.rearrange("(h p e) d -> h e p d", p=P, e=2)
 
         def product2(ct, ds, g, number):
-            if g == 0:
-                acc[ct, ds.start] = bank(number, [P, ds.stop - ds.start])
+            key = (ct, ds.start)
+            done[key] = done.get(key, 0) + 1
+            if done[key] == 1:
+                acc[key] = bank(number, [P, ds.stop - ds.start])
             cols = slice(P * g, P * (g + 1))
             nc.tensor.matmul_mx(
                 out=acc[ct, ds.start][:],
@@ -323,8 +325,8 @@ def tile_mppi_control_update_s13_kernel(tc, x_bytes, x_scale, w, base, ratio, ep
                 lhsT_scale=m_scales[ct][:, cols],
                 rhs=e_words[g][:, 2 * ds.start : 2 * ds.stop].bitcast(FP4X4),
                 rhs_scale=e_scales[:, g, ds],
-                start=(g == 0),
-                stop=(g == NG - 1),
+                start=(done[key] == 1),
+                stop=(done[key] == NG),
             )
 
         def finish(ct, ds, engine, parts=1):
@@ -340,113 +342,129 @@ def tile_mppi_control_update_s13_kernel(tc, x_bytes, x_scale, w, base, ratio, ep
                 product2(0, wide[dt], g, HELD_BANK + dt)
 
         last = NG - 1
+        end = 2 * NG - 1
         group_w_on_scalar(0, 1)
         group_w_on_tensor(0, 0, COST_BANKS[0])
-        for j in range(2 * NG):
-            g, odd = divmod(j, 2)
+        for j in range(2):
             scale_x(j, 0, XS_PARTS if j == 0 else 1)
             if j == 1:
                 quantise_w(0, slice(0, C))
-            if j == 2:
-                quantise_w(1, slice(PAIR, C))
-            if g >= 2 and not odd:
-                quantise_m((g - 2,), 0)
-                held_passes(g - 2, (0, 1))
-            scale_x(j, 1, NQ if j == 2 * NG - 1 else 1)
+            scale_x(j, 1)
             turn_x(j, 0)
             empty_x(j, 0)
-            if g == 0:
-                group_w_on_tensor(1, j, HELD_BANK + j)
-            if g == 1:
-                costs_by_rollout(j - 2, COST_BANKS[1])
-                keep_costs(j - 2)
-            if j < 2 * NG - 1:
-                turn_x(j, 1)
-            else:
-                for q in range(NQ):
-                    turn_x(j, 1, (q,), 1 + q)
-                    empty_x(j, 1, (q,))
-            if g >= 1 and odd:
+            group_w_on_tensor(1, j, HELD_BANK + j)
+            turn_x(j, 1)
+            empty_x(j, 1)
+        quantise_w(1, slice(0, PAIR))
+        quantise_x(0)
+        costs_by_goal(0, 2)
+        exponentials(0)
+        for j in range(2, end):
+            g, odd = divmod(j, 2)
+            scale_x(j, 0)
+            if j == 2:
+                quantise_w(1, slice(PAIR, C))
+                costs_by_rollout(0, 3)
+                keep_costs(0)
+            if j >= 4 and not odd:
+                quantise_m((g - 2,), 0)
+                held_passes(g - 2, (0, 1))
+            scale_x(j, 1)
+            turn_x(j, 0)
+            turn_x(j, 1)
+            empty_x(j, 0)
+            if odd:
                 times_ratio(g - 1, 0)
-                turn_m((g - 1,), 0, COST_BANKS[1] if g > 1 else HELD_BANK + 2)
-                empty_m((g - 1,), 0)
-            if j < 2 * NG - 1:
-                empty_x(j, 1)
-            if j == 1:
-                quantise_w(1, slice(0, PAIR))
-            if j >= 1:
                 quantise_x(j - 1)
-                if g >= 2 and odd:
+                turn_m((g - 1,), 0, 3)
+                empty_m((g - 1,), 0)
+                empty_x(j, 1)
+                if g >= 2:
                     held_passes(g - 2, (3,))
-                costs_by_goal(j - 1, COST_BANKS[0] if j < 2 * NG - 1 else 0)
+                costs_by_goal(j - 1, 2)
                 exponentials(j - 1)
-                if g >= 2 and not odd:
+                costs_by_rollout(j - 1, 3)
+                keep_costs(j - 1)
+            else:
+                quantise_x(j - 1)
+                empty_x(j, 1)
+                costs_by_goal(j - 1, 3)
+                exponentials(j - 1)
+                costs_by_rollout(j - 1, 2)
+                keep_costs(j - 1)
+                if g >= 2:
                     held_passes(g - 2, (2,))
-                if j >= 3:
-                    costs_by_rollout(j - 1, COST_BANKS[1] if j < 2 * NG - 1 else 1)
-                    keep_costs(j - 1)
-                if j == 5:
-                    double_base()
-                if j == 4:
-                    repeat_ratio()
+            if j == 5:
+                double_base()
+                repeat_ratio()
 
         early, late = (0, 1), (2, last)
-        end = 2 * NG - 1
+        scale_x(end, 0)
+        scale_x(end, 1)
+        turn_x(end, 0)
+        turn_x(end, 1)
+        empty_x(end, 0)
+        empty_x(end, 1)
+        times_ratio(2, 0)
+        quantise_x(end - 1)
+        turn_m((2,), 0, 2)
+        empty_m((2,), 0)
+        held_passes(1, (3,))
+        costs_by_goal(end - 1, 3)
+        exponentials(end - 1)
+        costs_by_rollout(end - 1, 0)
+        keep_costs(end - 1)
         times_ratio(0, 1)
-        quantise_x(end, 0, UNIT)
-        quantise_x(end, UNIT, UNIT)
-        quantise_m((last - 1,), 0)
+        quantise_x(end)
+        quantise_m((2,), 0)
         times_ratio(1, 1)
         times_ratio(2, 1)
-        costs_by_goal(end, 2)
+        costs_by_goal(end, 1)
         exponentials(end)
-        costs_by_rollout(end, 3)
-        turn_m(early, 1, 0)
-        empty_m(early, 1)
+        held_passes(2, (0,))
+        costs_by_rollout(end, 2)
         keep_costs(end)
-        held_passes(last - 1, range(ND))
+        turn_m(early, 1, 3)
+        empty_m(early, 1)
+        held_passes(2, (1, 2, 3))
         minus_base(0, 2)
         times_ratio(last, 0)
         times_ratio(last, 1)
-        quantise_m(early, 1)
         minus_base(1, 2)
+        quantise_m(early, 1)
 
-        banks = (3, 0, 1, 2, 4, 5, 6, 7, 3, 0, 1)
+        banks = {1: (3, 2, 0, 1), 2: (7, 6, 5, 4), 3: (3, 2, 0)}
 
         def passes(ct, dts, gs):
             for dt in dts:
                 for g in gs:
-                    product2(ct, wide[dt], g, banks[ND * (ct - 1) + dt])
+                    product2(ct, wide[dt], g, banks[ct][dt])
 
-        turn_m((last,), 0, 1)
-        turn_m(late, 1, 2)
+        turn_m(late, 1, 1)
+        turn_m((last,), 0, 0)
         late_exponential(0, 2)
         empty_m((last,), 0)
         empty_m(late, 1)
         passes(1, (0, 1), early)
-        quantise_m((last,), 0)
         minus_base(2, 2)
-        quantise_m(late, 1)
+        quantise_m((last,), 0)
         minus_base(last, 2)
-        late_exponential(1, 2)
+        quantise_m(late, 1)
         held_passes(last, range(ND))
         passes(1, (0, 1), late)
         passes(1, (2, 3), range(NG))
 
-        for n in range(2):
-            finish(0, wide[n], "scalar")
-            late_exponential(late[n], 2)
-        for n in range(2):
-            late_ratio(early, n, 2)
-        late_ratio(late, 0, 2)
-        quantise_m(early, 2)
-        late_ratio(late, 1, 2)
-        minus_base(0, 3)
-        quantise_m(late, 2)
         for g in range(1, NG):
-            minus_base(g, 3)
-        for dt in range(2, ND):
+            late_exponential(g, 2)
+        for dt in range(ND):
             finish(0, wide[dt], "scalar")
+        for pair in (early, late):
+            for n in range(2):
+                late_ratio(pair, n, 2)
+        quantise_m(early, 2)
+        quantise_m(late, 2)
+        for g in range(NG):
+            minus_base(g, 3)
         for dt in range(2):
             finish(1, wide[dt], "scalar")
         for g in early:
@@ -455,26 +473,23 @@ def tile_mppi_control_update_s13_kernel(tc, x_bytes, x_scale, w, base, ratio, ep
         for g in late:
             late_exponential(g, 3)
         finish(1, wide[3], "scalar")
-        passes(2, (0, 1), early)
-        passes(2, (0, 1), late)
-        passes(2, (2, 3), range(NG))
+        for dt in range(ND):
+            passes(2, (dt,), late + early if dt == 0 else range(NG))
         for n in range(2):
             late_ratio(early, n, 3)
         late_ratio(late, 0, 3)
         quantise_m(early, 3)
         late_ratio(late, 1, 3)
-        for n in range(2):
-            quantise_m(late, 3, n)
+        quantise_m(late, 3)
         for dt in range(ND):
-            finish(2, wide[dt], "scalar" if dt < ND - 1 else "vector")
+            finish(2, wide[dt], "scalar")
         passes(3, (0, 1), early)
-        for g in late:
-            passes(3, (0, 1), (g,))
-        finish(3, wide[0], "scalar")
-        finish(3, wide[1], "vector")
+        passes(3, (0, 1), late)
+        finish(3, wide[0], "vector")
+        finish(3, wide[1], "scalar")
         passes(3, (2,), range(NG))
-        finish(3, wide[2], "scalar", 2)
+        finish(3, wide[2], "vector", 2)
         for n in range(NB // P):
             for g in range(NG):
                 product2(3, narrow[n], g, HELD_BANK + n)
-            finish(3, narrow[n], "vector" if n % 2 == 0 else "scalar")
+            finish(3, narrow[n], "scalar" if n % 2 == 0 else "vector")

@@ -74,6 +74,8 @@ def tile_mppi_control_update_s13_kernel(tc, x_bytes, x_scale, w, base, ratio, ep
                 nc.sync.dma_start(out=w_raw[t][:], in_=w_rows[t])
         base_own = buf("base_own", 1, [P, 2], BF16)
         nc.sync.dma_start(out=base_own[:], in_=base[:PAIR].rearrange("(p e) -> p e", e=2))
+        ratio_own = buf("ratio_own", 1, [P, NG, NT], BF16)
+        base_all = buf("base_all", 1, [P, PAIR], BF16)
         ratio_all = [buf("ratio_all", 2, [P, 2 * KP], BF16) for half in range(2)]
 
         def spread_ratio(half):
@@ -83,12 +85,13 @@ def tile_mppi_control_update_s13_kernel(tc, x_bytes, x_scale, w, base, ratio, ep
             nc.sync.dma_start(out=x_rest[g - 1][:], in_=x_rows[g])
             if g == 1:
                 spread_ratio(0)
+        nc.sync.dma_start(out=ratio_own[:], in_=ratio.rearrange("(g p t) -> p g t", p=P, t=NT))
+        nc.sync.dma_start(out=base_all[:], in_=base[PAIR:].partition_broadcast(P))
         e_rows = eps_scales.bitcast(I32).rearrange("g q n -> q g n")
         for quad in range(4):
             nc.sync.dma_start(
                 out=e_scales[32 * quad : 32 * quad + 4, :, :].bitcast(I32), in_=e_rows[4 * quad : 4 * quad + 4]
             )
-        ratio_own = buf("ratio_own", 1, [P, NG, NT], BF16)
         e_words = [buf("e_words", NG, [P, 2 * D], U8) for g in range(NG)]
         for g in range(NG):
             nc.sync.dma_start(out=e_words[g][:], in_=eps_words[g])
@@ -96,9 +99,6 @@ def tile_mppi_control_update_s13_kernel(tc, x_bytes, x_scale, w, base, ratio, ep
                 nc.sync.dma_start(out=x_rest[NG - 2][:], in_=x_rows[NG - 1])
             if g == 1:
                 spread_ratio(1)
-        nc.sync.dma_start(out=ratio_own[:], in_=ratio.rearrange("(g p t) -> p g t", p=P, t=NT))
-        base_all = buf("base_all", 1, [P, PAIR], BF16)
-        nc.sync.dma_start(out=base_all[:], in_=base[PAIR:].partition_broadcast(P))
 
         xs_all = buf("xs_all", 1, [P, F], F32)
         for a in range(XS_PARTS):
@@ -157,7 +157,19 @@ def tile_mppi_control_update_s13_kernel(tc, x_bytes, x_scale, w, base, ratio, ep
             for n in range(len(qs)):
                 for u in range(2):
                     first = 256 * qs[n]
-                    nc.tensor.transpose(x_turned[j, a, qs][:, n, u, :], words[:, first + u : first + 256 : 2], ident[:])
+                    if (j, a) in x_ordered:
+                        src = x_ordered[j, a][:, qs[n], u, :]
+                    else:
+                        src = words[:, first + u : first + 256 : 2]
+                    nc.tensor.transpose(x_turned[j, a, qs][:, n, u, :], src, ident[:])
+
+        x_ordered = {}
+
+        def order_x(j, a):
+            x_ordered[j, a] = buf("x_ordered", 2, [P, NQ, 2, P], F32)
+            nc.scalar.copy(
+                out=x_ordered[j, a][:], in_=x_scaled[j, a][:].bitcast(F32).rearrange("p (q i u) -> p q u i", q=NQ, u=2)
+            )
 
         def empty_x(j, a, qs=(0, 1)):
             if j not in x_grouped:
@@ -208,10 +220,10 @@ def tile_mppi_control_update_s13_kernel(tc, x_bytes, x_scale, w, base, ratio, ep
             for ct in range(2):
                 cost_group(by_goal[j][:, ct, :], w_cols(P * ct, P), x_cols(j, 0, UNIT))
 
-        def exponentials(j):
+        def exponentials(j, cts=(0, 1)):
             g, h = divmod(j, 2)
             cost = by_goal[j]
-            for ct in range(2):
+            for ct in cts:
                 if h == 0:
                     expo[g, ct] = buf("expo", 3 * NG, [P, KP], F32)
                 nc.scalar.activation(
@@ -243,9 +255,9 @@ def tile_mppi_control_update_s13_kernel(tc, x_bytes, x_scale, w, base, ratio, ep
                 op=ALU.mult,
             )
 
-        def turn_m(gs, ct, number):
+        def turn_m(gs, ct, number, newest_first=True):
             turned[gs, ct] = bank(number, [P, len(gs), 2, P])
-            for n in reversed(range(len(gs))):
+            for n in reversed(range(len(gs))) if newest_first else range(len(gs)):
                 for u in range(2):
                     nc.tensor.transpose(turned[gs, ct][:, n, u, :], scaled[gs[n], ct][:, u, :].bitcast(F32), ident[:])
 
@@ -359,112 +371,115 @@ def tile_mppi_control_update_s13_kernel(tc, x_bytes, x_scale, w, base, ratio, ep
         quantise_x(0)
         costs_by_goal(0, 2)
         exponentials(0)
+        scale_x(2, 0)
+        quantise_w(1, slice(PAIR, C))
+        double_base()
+        costs_by_rollout(0, 3)
+        keep_costs(0)
+        repeat_ratio()
         for j in range(2, end):
             g, odd = divmod(j, 2)
-            scale_x(j, 0)
-            if j == 2:
-                quantise_w(1, slice(PAIR, C))
-                costs_by_rollout(0, 3)
-                keep_costs(0)
-            if j >= 4 and not odd:
-                quantise_m((g - 2,), 0)
-                held_passes(g - 2, (0, 1))
             scale_x(j, 1)
             turn_x(j, 0)
             turn_x(j, 1)
             empty_x(j, 0)
             if odd:
                 times_ratio(g - 1, 0)
-                quantise_x(j - 1)
                 turn_m((g - 1,), 0, 3)
                 empty_m((g - 1,), 0)
-                empty_x(j, 1)
+            quantise_x(j - 1)
+            empty_x(j, 1)
+            scale_x(j + 1, 0)
+            if odd:
+                quantise_m((g - 1,), 0)
                 if g >= 2:
                     held_passes(g - 2, (3,))
-                costs_by_goal(j - 1, 2)
-                exponentials(j - 1)
-                costs_by_rollout(j - 1, 3)
-                keep_costs(j - 1)
-            else:
-                quantise_x(j - 1)
-                empty_x(j, 1)
-                costs_by_goal(j - 1, 3)
-                exponentials(j - 1)
-                costs_by_rollout(j - 1, 2)
-                keep_costs(j - 1)
-                if g >= 2:
-                    held_passes(g - 2, (2,))
-            if j == 5:
-                double_base()
-                repeat_ratio()
+            costs_by_goal(j - 1, 2 if odd else 3)
+            if j + 1 in (4, 6) and odd:
+                order_x(j + 1, 0)
+            exponentials(j - 1, (0,))
+            if j + 1 in (4, 6) and not odd:
+                order_x(j + 1, 0)
+            exponentials(j - 1, (1,))
+            costs_by_rollout(j - 1, 3 if odd else 2)
+            keep_costs(j - 1)
+            if odd:
+                held_passes(g - 1, (0, 1))
+            elif g >= 2:
+                held_passes(g - 2, (2,))
 
         early, late = (0, 1), (2, last)
-        scale_x(end, 0)
-        scale_x(end, 1)
+        scale_x(end, 1, NQ)
         turn_x(end, 0)
-        turn_x(end, 1)
         empty_x(end, 0)
-        empty_x(end, 1)
+        for q in range(NQ):
+            turn_x(end, 1, (q,), 1 + 2 * q)
+            empty_x(end, 1, (q,))
         times_ratio(2, 0)
         quantise_x(end - 1)
         turn_m((2,), 0, 2)
         empty_m((2,), 0)
         held_passes(1, (3,))
-        costs_by_goal(end - 1, 3)
+        costs_by_goal(end - 1, 0)
         exponentials(end - 1)
-        costs_by_rollout(end - 1, 0)
-        keep_costs(end - 1)
+        costs_by_rollout(end - 1, 1)
         times_ratio(0, 1)
-        quantise_x(end)
+        for q in range(NQ):
+            quantise_x(end, UNIT * q, UNIT)
         quantise_m((2,), 0)
         times_ratio(1, 1)
         times_ratio(2, 1)
-        costs_by_goal(end, 1)
+        costs_by_goal(end, 3)
         exponentials(end)
-        held_passes(2, (0,))
+        keep_costs(end - 1)
         costs_by_rollout(end, 2)
         keep_costs(end)
-        turn_m(early, 1, 3)
-        empty_m(early, 1)
-        held_passes(2, (1, 2, 3))
-        minus_base(0, 2)
+        held_passes(2, (0, 1))
         times_ratio(last, 0)
         times_ratio(last, 1)
-        minus_base(1, 2)
+        turn_m(early, 1, 0)
+        empty_m(early, 1)
+        turn_m((last,), 0, 3)
+        empty_m((last,), 0)
+        turn_m(late, 1, 1, False)
+        empty_m(late, 1)
+        held_passes(2, (2, 3))
+        minus_base(0, 2)
         quantise_m(early, 1)
+        quantise_m((last,), 0)
+        minus_base(1, 2)
+        quantise_m(late, 1)
+        minus_base(2, 2)
+        minus_base(last, 2)
+        late_exponential(0, 2)
+        late_exponential(1, 2)
 
-        banks = {1: (3, 2, 0, 1), 2: (7, 6, 5, 4), 3: (3, 2, 0)}
+        banks = {1: (2, 0, 3, 1), 2: (4, 5, 6, 7), 3: (2, 0, 3)}
 
         def passes(ct, dts, gs):
             for dt in dts:
                 for g in gs:
                     product2(ct, wide[dt], g, banks[ct][dt])
 
-        turn_m(late, 1, 1)
-        turn_m((last,), 0, 0)
-        late_exponential(0, 2)
-        empty_m((last,), 0)
-        empty_m(late, 1)
         passes(1, (0, 1), early)
-        minus_base(2, 2)
-        quantise_m((last,), 0)
-        minus_base(last, 2)
-        quantise_m(late, 1)
         held_passes(last, range(ND))
         passes(1, (0, 1), late)
         passes(1, (2, 3), range(NG))
 
-        for g in range(1, NG):
-            late_exponential(g, 2)
-        for dt in range(ND):
-            finish(0, wide[dt], "scalar")
-        for pair in (early, late):
-            for n in range(2):
-                late_ratio(pair, n, 2)
+        for n in range(2):
+            finish(0, wide[n], "scalar")
+            late_exponential(late[n], 2)
+        for n in range(2):
+            late_ratio(early, n, 2)
+        late_ratio(late, 0, 2)
         quantise_m(early, 2)
+        late_ratio(late, 1, 2)
+        minus_base(0, 3)
         quantise_m(late, 2)
-        for g in range(NG):
+        for g in range(1, NG):
             minus_base(g, 3)
+        for dt in range(2, ND):
+            finish(0, wide[dt], "scalar")
         for dt in range(2):
             finish(1, wide[dt], "scalar")
         for g in early:
@@ -473,23 +488,26 @@ def tile_mppi_control_update_s13_kernel(tc, x_bytes, x_scale, w, base, ratio, ep
         for g in late:
             late_exponential(g, 3)
         finish(1, wide[3], "scalar")
-        for dt in range(ND):
-            passes(2, (dt,), late + early if dt == 0 else range(NG))
+        passes(2, (0, 1), early)
+        passes(2, (0, 1), late)
+        passes(2, (2, 3), range(NG))
         for n in range(2):
             late_ratio(early, n, 3)
         late_ratio(late, 0, 3)
         quantise_m(early, 3)
         late_ratio(late, 1, 3)
-        quantise_m(late, 3)
+        for n in range(2):
+            quantise_m(late, 3, n)
         for dt in range(ND):
-            finish(2, wide[dt], "scalar")
+            finish(2, wide[dt], "scalar" if dt < ND - 1 else "vector")
         passes(3, (0, 1), early)
-        passes(3, (0, 1), late)
-        finish(3, wide[0], "vector")
-        finish(3, wide[1], "scalar")
+        for g in late:
+            passes(3, (0, 1), (g,))
+        finish(3, wide[0], "scalar")
+        finish(3, wide[1], "vector")
         passes(3, (2,), range(NG))
-        finish(3, wide[2], "vector", 2)
+        finish(3, wide[2], "scalar", 2)
         for n in range(NB // P):
             for g in range(NG):
                 product2(3, narrow[n], g, HELD_BANK + n)
-            finish(3, narrow[n], "scalar" if n % 2 == 0 else "vector")
+            finish(3, narrow[n], "vector" if n % 2 == 0 else "scalar")

@@ -26,7 +26,6 @@ ND = D // NB
 UNIT = KP // 2
 PAIR = C // 2
 XS_PARTS = 4
-REP = 16
 X_BANKS = (0, 1)
 COST_BANKS = (2, 3)
 HELD_BANK = 4
@@ -81,24 +80,28 @@ def tile_mppi_control_update_s13_kernel(tc, x_bytes, x_scale, w, base, ratio, ep
         def spread_ratio(half):
             nc.sync.dma_start(out=ratio_all[half][:], in_=ratio[2 * KP * half : 2 * KP * (half + 1)].partition_broadcast(P))
 
-        for g in range(1, NG - 1):
-            nc.sync.dma_start(out=x_rest[g - 1][:], in_=x_rows[g])
-            if g == 1:
-                spread_ratio(0)
+        e_rows = eps_scales.bitcast(I32).rearrange("g q n -> q g n")
+        e_words = [buf("e_words", NG, [P, 2 * D], U8) for g in range(NG)]
+
+        def load_e_scales(gs):
+            for quad in range(4):
+                nc.sync.dma_start(
+                    out=e_scales[32 * quad : 32 * quad + 4, gs, :].bitcast(I32), in_=e_rows[4 * quad : 4 * quad + 4, gs]
+                )
+
+        nc.sync.dma_start(out=x_rest[0][:], in_=x_rows[1])
+        spread_ratio(0)
+        nc.sync.dma_start(out=x_rest[1][:], in_=x_rows[2])
+        load_e_scales(slice(0, 1))
+        nc.sync.dma_start(out=e_words[0][:], in_=eps_words[0])
+        nc.sync.dma_start(out=x_rest[2][:], in_=x_rows[3])
+        load_e_scales(slice(1, NG))
+        nc.sync.dma_start(out=e_words[1][:], in_=eps_words[1])
         nc.sync.dma_start(out=ratio_own[:], in_=ratio.rearrange("(g p t) -> p g t", p=P, t=NT))
         nc.sync.dma_start(out=base_all[:], in_=base[PAIR:].partition_broadcast(P))
-        e_rows = eps_scales.bitcast(I32).rearrange("g q n -> q g n")
-        for quad in range(4):
-            nc.sync.dma_start(
-                out=e_scales[32 * quad : 32 * quad + 4, :, :].bitcast(I32), in_=e_rows[4 * quad : 4 * quad + 4]
-            )
-        e_words = [buf("e_words", NG, [P, 2 * D], U8) for g in range(NG)]
-        for g in range(NG):
+        spread_ratio(1)
+        for g in range(2, NG):
             nc.sync.dma_start(out=e_words[g][:], in_=eps_words[g])
-            if g == 0:
-                nc.sync.dma_start(out=x_rest[NG - 2][:], in_=x_rows[NG - 1])
-            if g == 1:
-                spread_ratio(1)
 
         xs_all = buf("xs_all", 1, [P, F], F32)
         for a in range(XS_PARTS):
@@ -268,27 +271,13 @@ def tile_mppi_control_update_s13_kernel(tc, x_bytes, x_scale, w, base, ratio, ep
                 in_=turned[gs, ct][:].rearrange("p n u m -> p n m u"),
             )
 
-        base_twice = buf("base_twice", 1, [P, 2, P, 2], BF16)
-        ratio_rep = buf("ratio_rep", 1, [P, NG, REP, NT], BF16)
-
-        def double_base():
-            nc.scalar.copy(
-                out=base_twice[:],
-                in_=base_all[:].rearrange("p (m e a) -> p e m a", e=2, a=1).to_broadcast([P, 2, P, 2]),
-            )
-
-        def repeat_ratio():
-            nc.scalar.copy(
-                out=ratio_rep[:].bitcast(F32), in_=ratio_own[:].bitcast(F32).unsqueeze(2).to_broadcast([P, NG, REP, 2])
-            )
-
         def minus_base(g, ct):
             e = ct - 2
             diff[g, ct] = buf("diff", 6, [P, 2, P, 2], F32)
             nc.vector.tensor_tensor(
                 out=diff[g, ct][:],
                 in0=kept[g][:, :, P * e : P * (e + 1), :],
-                in1=base_twice[:, e : e + 1].to_broadcast([P, 2, P, 2]),
+                in1=base_all[:].rearrange("p (m e a) -> p e m a", e=2, a=1)[:, e : e + 1].to_broadcast([P, 2, P, 2]),
                 op=ALU.subtract,
             )
 
@@ -305,9 +294,9 @@ def tile_mppi_control_update_s13_kernel(tc, x_bytes, x_scale, w, base, ratio, ep
             if n == 0:
                 grouped_m[gs, ct] = buf("grouped_m", 4, [P, 2 * P, 4], BF16)
             nc.vector.tensor_tensor(
-                out=grouped_m[gs, ct][:, P * n : P * (n + 1), :].rearrange("p (h m) t -> p h (m t)", m=REP),
-                in0=expo[gs[n], ct][:].rearrange("p (h x) -> p h x", x=REP * NT),
-                in1=ratio_rep[:, gs[n] : gs[n] + 1].rearrange("p o m t -> p o (m t)").to_broadcast([P, P // REP, REP * NT]),
+                out=grouped_m[gs, ct][:, P * n : P * (n + 1), :],
+                in0=expo[gs[n], ct][:].rearrange("p (m t) -> p m t", t=NT),
+                in1=ratio_own[:, gs[n] : gs[n] + 1, :].to_broadcast([P, P, NT]),
                 op=ALU.mult,
             )
 
@@ -373,10 +362,8 @@ def tile_mppi_control_update_s13_kernel(tc, x_bytes, x_scale, w, base, ratio, ep
         exponentials(0)
         scale_x(2, 0)
         quantise_w(1, slice(PAIR, C))
-        double_base()
         costs_by_rollout(0, 3)
         keep_costs(0)
-        repeat_ratio()
         for j in range(2, end):
             g, odd = divmod(j, 2)
             scale_x(j, 1)

@@ -52,8 +52,9 @@ def tile_mppi_control_update_s13_kernel(tc, x_bytes, x_scale, w, base, ratio, ep
             else:
                 nc.scalar.copy(out=dst, in_=src)
 
-        xs = buf("xs", 1, [P, XS_PARTS, 2], F32)
-        nc.sync.dma_start(out=xs[:], in_=x_scale.rearrange("o (a p e) -> p (o a) e", p=P, e=2))
+        xs_parts = x_scale.rearrange("o (a p e) -> p (o a) e", p=P, e=2)
+        xs = [buf("xs", 2, [P, XS_PARTS // 2, 2], F32) for half in range(2)]
+        nc.sync.dma_start(out=xs[0][:], in_=xs_parts[:, : XS_PARTS // 2])
 
         ident = buf("ident", 1, [P, P], F32)
         make_identity(nc, ident[:])
@@ -69,8 +70,10 @@ def tile_mppi_control_update_s13_kernel(tc, x_bytes, x_scale, w, base, ratio, ep
         w_raw = [buf("w_raw", NQ, [P, 4, C], BF16) for q in range(NQ)]
         for t in range(NT):
             nc.sync.dma_start(out=x_first[t][:], in_=x_rows[0][:, t, :])
-            if t < NQ:
-                nc.sync.dma_start(out=w_raw[t][:], in_=w_rows[t])
+            if t == 0:
+                nc.sync.dma_start(out=xs[1][:], in_=xs_parts[:, XS_PARTS // 2 :])
+            if t % 2 == 0:
+                nc.sync.dma_start(out=w_raw[t // 2][:], in_=w_rows[t // 2])
         base_own = buf("base_own", 1, [P, 2], BF16)
         nc.sync.dma_start(out=base_own[:], in_=base[:PAIR].rearrange("(p e) -> p e", e=2))
         ratio_own = buf("ratio_own", 1, [P, NG, NT], BF16)
@@ -90,16 +93,16 @@ def tile_mppi_control_update_s13_kernel(tc, x_bytes, x_scale, w, base, ratio, ep
                 )
 
         nc.sync.dma_start(out=x_rest[0][:], in_=x_rows[1])
-        spread_ratio(0)
+        nc.sync.dma_start(out=ratio_own[:], in_=ratio.rearrange("(g p t) -> p g t", p=P, t=NT))
         nc.sync.dma_start(out=x_rest[1][:], in_=x_rows[2])
         load_e_scales(slice(0, 1))
         nc.sync.dma_start(out=e_words[0][:], in_=eps_words[0])
         nc.sync.dma_start(out=x_rest[2][:], in_=x_rows[3])
+        spread_ratio(0)
         load_e_scales(slice(1, NG))
         nc.sync.dma_start(out=e_words[1][:], in_=eps_words[1])
-        nc.sync.dma_start(out=ratio_own[:], in_=ratio.rearrange("(g p t) -> p g t", p=P, t=NT))
-        nc.sync.dma_start(out=base_all[:], in_=base[PAIR:].partition_broadcast(P))
         spread_ratio(1)
+        nc.sync.dma_start(out=base_all[:], in_=base[PAIR:].partition_broadcast(P))
         for g in range(2, NG):
             nc.sync.dma_start(out=e_words[g][:], in_=eps_words[g])
 
@@ -107,10 +110,10 @@ def tile_mppi_control_update_s13_kernel(tc, x_bytes, x_scale, w, base, ratio, ep
         for a in range(XS_PARTS):
             spread = bank(HELD_BANK + a, [P, 2, P])
             for e in range(2):
-                nc.tensor.transpose(spread[:, e, :], xs[:, a, e : e + 1].to_broadcast([P, P]), ident[:])
+                nc.tensor.transpose(spread[:, e, :], xs[a // 2][:, a % 2, e : e + 1].to_broadcast([P, P]), ident[:])
             dst = xs_all[:, 2 * P * a : 2 * P * (a + 1)].rearrange("m (p e) -> m p e", e=2)
             src = spread[:].rearrange("m e p -> m p e")
-            if a == 0:
+            if a < 2:
                 nc.vector.tensor_copy(out=dst, in_=src)
             else:
                 nc.scalar.activation(out=dst, in_=src, func=ACT.Copy)
@@ -229,9 +232,12 @@ def tile_mppi_control_update_s13_kernel(tc, x_bytes, x_scale, w, base, ratio, ep
             for ct in cts:
                 if h == 0:
                     expo[g, ct] = buf("expo", 3 * NG, [P, KP], F32)
+                dst, src = expo[g, ct][:, UNIT * h : UNIT * (h + 1)], cost[:, ct, :]
+                if ct or g:
+                    dst, src = dst.rearrange("p (r a) -> p r a", a=2), src.rearrange("p (a r) -> p r a", a=2)
                 nc.scalar.activation(
-                    out=expo[g, ct][:, UNIT * h : UNIT * (h + 1)].rearrange("p (r a) -> p r a", a=2),
-                    in_=cost[:, ct, :].rearrange("p (a r) -> p r a", a=2),
+                    out=dst,
+                    in_=src,
                     func=ACT.Exp,
                     bias=base_own[:, ct : ct + 1],
                     scale=-1.0,
@@ -270,6 +276,22 @@ def tile_mppi_control_update_s13_kernel(tc, x_bytes, x_scale, w, base, ratio, ep
                 out=grouped_m[gs, ct][:].bitcast(F32).rearrange("p (n m) u -> p n m u", n=len(gs)),
                 in_=turned[gs, ct][:].rearrange("p n u m -> p n m u"),
             )
+
+        def turn_expo(number):
+            turned[0] = bank(number, [P, NT, P])
+            for t in range(NT):
+                nc.tensor.transpose(turned[0][:, t, :], expo[0, 0][:, P * t : P * (t + 1)], ident[:])
+
+        def ratio_on_scalar():
+            scaled[0, 0] = buf("planes", 1, [P, NT, P], BF16)
+            for t in range(NT):
+                nc.scalar.activation(
+                    out=scaled[0, 0][:, t, :], in_=turned[0][:, t, :], func=ACT.Copy, scale=ratio_f32[:, t : t + 1]
+                )
+
+        def group_on_scalar():
+            grouped_m[(0,), 0] = buf("grouped_m", 4, [P, P, 4], BF16)
+            nc.scalar.copy(out=grouped_m[(0,), 0][:], in_=scaled[0, 0][:].rearrange("p t m -> p m t"))
 
         def minus_base(g, ct):
             e = ct - 2
@@ -348,14 +370,13 @@ def tile_mppi_control_update_s13_kernel(tc, x_bytes, x_scale, w, base, ratio, ep
         group_w_on_tensor(0, 0, COST_BANKS[0])
         for j in range(2):
             scale_x(j, 0, XS_PARTS if j == 0 else 1)
-            if j == 1:
-                quantise_w(0, slice(0, C))
             scale_x(j, 1)
             turn_x(j, 0)
             empty_x(j, 0)
             group_w_on_tensor(1, j, HELD_BANK + j)
             turn_x(j, 1)
             empty_x(j, 1)
+        quantise_w(0, slice(0, C))
         quantise_w(1, slice(0, PAIR))
         quantise_x(0)
         costs_by_goal(0, 2)
@@ -364,38 +385,49 @@ def tile_mppi_control_update_s13_kernel(tc, x_bytes, x_scale, w, base, ratio, ep
         quantise_w(1, slice(PAIR, C))
         costs_by_rollout(0, 3)
         keep_costs(0)
+        ratio_f32 = buf("ratio_f32", 1, [P, NT], F32)
+        nc.scalar.copy(out=ratio_f32[:], in_=ratio_own[:, 0, :])
         for j in range(2, end):
             g, odd = divmod(j, 2)
             scale_x(j, 1)
+            if j == 3:
+                turn_expo(HELD_BANK + 3)
+                ratio_on_scalar()
             turn_x(j, 0)
             turn_x(j, 1)
             empty_x(j, 0)
-            if odd:
+            if j == 3:
+                group_on_scalar()
+            if odd and j > 3:
                 times_ratio(g - 1, 0)
                 turn_m((g - 1,), 0, 3)
                 empty_m((g - 1,), 0)
+            if j in (4,):
+                quantise_m((g - 2,), 0)
+                held_passes(g - 2, (0, 1))
             quantise_x(j - 1)
             empty_x(j, 1)
             scale_x(j + 1, 0)
             if odd:
-                quantise_m((g - 1,), 0)
+                if j + 1 not in (4,):
+                    quantise_m((g - 1,), 0)
                 if g >= 2:
                     held_passes(g - 2, (3,))
             costs_by_goal(j - 1, 2 if odd else 3)
-            if j + 1 in (4, 6) and odd:
+            if j + 1 in () and False:
                 order_x(j + 1, 0)
             exponentials(j - 1, (0,))
-            if j + 1 in (4, 6) and not odd:
+            if j + 1 in () and True:
                 order_x(j + 1, 0)
             exponentials(j - 1, (1,))
             costs_by_rollout(j - 1, 3 if odd else 2)
             keep_costs(j - 1)
             if odd:
-                held_passes(g - 1, (0, 1))
+                if j + 1 not in (4,):
+                    held_passes(g - 1, (0, 1))
             elif g >= 2:
                 held_passes(g - 2, (2,))
 
-        early, late = (0, 1), (2, last)
         scale_x(end, 1, NQ)
         turn_x(end, 0)
         empty_x(end, 0)
@@ -403,52 +435,53 @@ def tile_mppi_control_update_s13_kernel(tc, x_bytes, x_scale, w, base, ratio, ep
             turn_x(end, 1, (q,), 1 + 2 * q)
             empty_x(end, 1, (q,))
         times_ratio(2, 0)
-        quantise_x(end - 1)
         turn_m((2,), 0, 2)
         empty_m((2,), 0)
+        quantise_x(end - 1)
         held_passes(1, (3,))
         costs_by_goal(end - 1, 0)
         exponentials(end - 1)
         costs_by_rollout(end - 1, 1)
+        keep_costs(end - 1)
+        early, late = (0, 1), (2, last)
+        end = 2 * NG - 1
         times_ratio(0, 1)
-        for q in range(NQ):
-            quantise_x(end, UNIT * q, UNIT)
-        quantise_m((2,), 0)
+        quantise_x(end, 0, UNIT)
+        quantise_x(end, UNIT, UNIT)
+        quantise_m((last - 1,), 0)
         times_ratio(1, 1)
         times_ratio(2, 1)
         costs_by_goal(end, 3)
         exponentials(end)
-        keep_costs(end - 1)
         costs_by_rollout(end, 2)
-        keep_costs(end)
-        held_passes(2, (0, 1))
-        times_ratio(last, 0)
-        times_ratio(last, 1)
         turn_m(early, 1, 0)
         empty_m(early, 1)
-        turn_m((last,), 0, 3)
-        empty_m((last,), 0)
-        turn_m(late, 1, 1, False)
-        empty_m(late, 1)
-        held_passes(2, (2, 3))
+        keep_costs(end)
+        held_passes(last - 1, range(ND))
         minus_base(0, 2)
+        times_ratio(last, 0)
+        times_ratio(last, 1)
         quantise_m(early, 1)
-        quantise_m((last,), 0)
         minus_base(1, 2)
-        quantise_m(late, 1)
-        minus_base(2, 2)
-        minus_base(last, 2)
-        late_exponential(0, 2)
-        late_exponential(1, 2)
 
-        banks = {1: (2, 0, 3, 1), 2: (4, 5, 6, 7), 3: (2, 0, 3)}
+        banks = (2, 0, 1, 3, 4, 5, 6, 7, 2, 0, 1)
 
         def passes(ct, dts, gs):
             for dt in dts:
                 for g in gs:
-                    product2(ct, wide[dt], g, banks[ct][dt])
+                    product2(ct, wide[dt], g, banks[ND * (ct - 1) + dt])
 
+        turn_m((last,), 0, 1)
+        turn_m(late, 1, 3)
+        late_exponential(0, 2)
+        empty_m((last,), 0)
+        empty_m(late, 1)
         passes(1, (0, 1), early)
+        quantise_m((last,), 0)
+        minus_base(2, 2)
+        quantise_m(late, 1)
+        minus_base(last, 2)
+        late_exponential(1, 2)
         held_passes(last, range(ND))
         passes(1, (0, 1), late)
         passes(1, (2, 3), range(NG))

@@ -414,12 +414,9 @@ def tile_mppi_control_update_s13_kernel(tc, x_bytes, x_scale, w, base, ratio, ep
                 if g >= 2:
                     held_passes(g - 2, (3,))
             costs_by_goal(j - 1, 2 if odd else 3)
-            if j + 1 in () and False:
-                order_x(j + 1, 0)
-            exponentials(j - 1, (0,))
-            if j + 1 in () and True:
-                order_x(j + 1, 0)
-            exponentials(j - 1, (1,))
+            if j == 5:
+                order_x(6, 0)
+            exponentials(j - 1)
             costs_by_rollout(j - 1, 3 if odd else 2)
             keep_costs(j - 1)
             if odd:
@@ -464,7 +461,7 @@ def tile_mppi_control_update_s13_kernel(tc, x_bytes, x_scale, w, base, ratio, ep
         quantise_m(early, 1)
         minus_base(1, 2)
 
-        banks = (2, 0, 1, 3, 4, 5, 6, 7, 2, 0, 1)
+        banks = (2, 0, 1, 3, 5, 4, 7, 6, 2, 0, 1)
 
         def passes(ct, dts, gs):
             for dt in dts:
@@ -486,9 +483,10 @@ def tile_mppi_control_update_s13_kernel(tc, x_bytes, x_scale, w, base, ratio, ep
         passes(1, (0, 1), late)
         passes(1, (2, 3), range(NG))
 
-        for n in range(2):
-            finish(0, wide[n], "scalar")
-            late_exponential(late[n], 2)
+        finish(0, wide[0], "scalar")
+        late_exponential(2, 2)
+        finish(0, wide[1], "scalar")
+        late_exponential(last, 2)
         for n in range(2):
             late_ratio(early, n, 2)
         late_ratio(late, 0, 2)

@@ -29,6 +29,8 @@ XS_PARTS = 4
 X_BANKS = (0, 1)
 COST_BANKS = (2, 3)
 HELD_BANK = 4
+M_SCALES_START, E_WORDS_START, E_SCALES_START = 64, 128, 192
+ORDERED_UNIT = 6
 
 FLOPS = 2 * S * F * C + 2 * C * S * D
 
@@ -42,6 +44,9 @@ def tile_mppi_control_update_s13_kernel(tc, x_bytes, x_scale, w, base, ratio, ep
 
         def buf(tag, bufs, shape, dtype):
             return sb.tile(shape, dtype, name=tag, tag=tag, bufs=bufs, align_bytes=256)
+
+        def shifted(tag, bufs, width, start):
+            return buf(tag, bufs, [P, start + width], U8)[:, start:]
 
         def bank(number, shape, dtype=F32):
             return psum.tile(shape, dtype, name="bank%d" % number, tag="bank%d" % number)
@@ -60,8 +65,9 @@ def tile_mppi_control_update_s13_kernel(tc, x_bytes, x_scale, w, base, ratio, ep
         make_identity(nc, ident[:])
         ident_bf = buf("ident_bf", 1, [P, P], BF16)
         nc.vector.tensor_copy(out=ident_bf[:], in_=ident[:])
-        e_scales = buf("e_scales", 1, [P, NG, D], U8)
-        nc.vector.memset(e_scales[:].rearrange("p g n -> p (g n)").bitcast(I32), 0)
+        e_plane = shifted("e_scales", 1, NG * D, E_SCALES_START)
+        nc.vector.memset(e_plane.bitcast(I32), 0)
+        e_scales = e_plane.rearrange("p (g n) -> p g n", g=NG)
 
         x_rows = x_bytes.rearrange("(g p t) k -> g p t k", p=P, t=NT)
         w_rows = w.rearrange("(q p j) c -> q p j c", p=P, j=4)
@@ -84,7 +90,7 @@ def tile_mppi_control_update_s13_kernel(tc, x_bytes, x_scale, w, base, ratio, ep
             nc.sync.dma_start(out=ratio_all[half][:], in_=ratio[2 * KP * half : 2 * KP * (half + 1)].partition_broadcast(P))
 
         e_rows = eps_scales.bitcast(I32).rearrange("g q n -> q g n")
-        e_words = [buf("e_words", NG, [P, 2 * D], U8) for g in range(NG)]
+        e_words = [shifted("e_words", NG, 2 * D, E_WORDS_START) for g in range(NG)]
 
         def load_e_scales(gs):
             for quad in range(4):
@@ -96,15 +102,15 @@ def tile_mppi_control_update_s13_kernel(tc, x_bytes, x_scale, w, base, ratio, ep
         nc.sync.dma_start(out=ratio_own[:], in_=ratio.rearrange("(g p t) -> p g t", p=P, t=NT))
         nc.sync.dma_start(out=x_rest[1][:], in_=x_rows[2])
         load_e_scales(slice(0, 1))
-        nc.sync.dma_start(out=e_words[0][:], in_=eps_words[0])
+        nc.sync.dma_start(out=e_words[0], in_=eps_words[0])
         nc.sync.dma_start(out=x_rest[2][:], in_=x_rows[3])
         spread_ratio(0)
         load_e_scales(slice(1, NG))
-        nc.sync.dma_start(out=e_words[1][:], in_=eps_words[1])
+        nc.sync.dma_start(out=e_words[1], in_=eps_words[1])
         spread_ratio(1)
         nc.sync.dma_start(out=base_all[:], in_=base[PAIR:].partition_broadcast(P))
         for g in range(2, NG):
-            nc.sync.dma_start(out=e_words[g][:], in_=eps_words[g])
+            nc.sync.dma_start(out=e_words[g], in_=eps_words[g])
 
         xs_all = buf("xs_all", 1, [P, F], F32)
         for a in range(XS_PARTS):
@@ -113,7 +119,7 @@ def tile_mppi_control_update_s13_kernel(tc, x_bytes, x_scale, w, base, ratio, ep
                 nc.tensor.transpose(spread[:, e, :], xs[a // 2][:, a % 2, e : e + 1].to_broadcast([P, P]), ident[:])
             dst = xs_all[:, 2 * P * a : 2 * P * (a + 1)].rearrange("m (p e) -> m p e", e=2)
             src = spread[:].rearrange("m e p -> m p e")
-            if a < 2:
+            if a < XS_PARTS // 2:
                 nc.vector.tensor_copy(out=dst, in_=src)
             else:
                 nc.scalar.activation(out=dst, in_=src, func=ACT.Copy)
@@ -145,7 +151,7 @@ def tile_mppi_control_update_s13_kernel(tc, x_bytes, x_scale, w, base, ratio, ep
                 in_=w_grouped[q][:, cols, :].rearrange("p c j -> p (c j)"),
             )
 
-        x_scaled, x_turned, x_grouped, x_codes, x_scales = {}, {}, {}, {}, {}
+        x_scaled, x_ordered, x_turned, x_grouped, x_codes, x_scales = {}, {}, {}, {}, {}, {}
 
         def scale_x(j, a, parts=1):
             g, t = divmod(2 * j + a, NT)
@@ -168,8 +174,6 @@ def tile_mppi_control_update_s13_kernel(tc, x_bytes, x_scale, w, base, ratio, ep
                     else:
                         src = words[:, first + u : first + 256 : 2]
                     nc.tensor.transpose(x_turned[j, a, qs][:, n, u, :], src, ident[:])
-
-        x_ordered = {}
 
         def order_x(j, a):
             x_ordered[j, a] = buf("x_ordered", 2, [P, NQ, 2, P], F32)
@@ -197,7 +201,7 @@ def tile_mppi_control_update_s13_kernel(tc, x_bytes, x_scale, w, base, ratio, ep
 
         by_goal, by_rollout, expo, kept, diff, scaled, turned, grouped_m = {}, {}, {}, {}, {}, {}, {}, {}
         m_codes = [buf("m_codes", NC, [P, NG * P], U32) for ct in range(NC)]
-        m_scales = [buf("m_scales", NC, [P, NG * P], U8) for ct in range(NC)]
+        m_scales = [shifted("m_scales", NC, NG * P, M_SCALES_START) for ct in range(NC)]
 
         def cost_group(dst, still, moving):
             for q in range(NQ):
@@ -226,14 +230,14 @@ def tile_mppi_control_update_s13_kernel(tc, x_bytes, x_scale, w, base, ratio, ep
             for ct in range(2):
                 cost_group(by_goal[j][:, ct, :], w_cols(P * ct, P), x_cols(j, 0, UNIT))
 
-        def exponentials(j, cts=(0, 1)):
+        def exponentials(j):
             g, h = divmod(j, 2)
             cost = by_goal[j]
-            for ct in cts:
+            for ct in range(2):
                 if h == 0:
                     expo[g, ct] = buf("expo", 3 * NG, [P, KP], F32)
                 dst, src = expo[g, ct][:, UNIT * h : UNIT * (h + 1)], cost[:, ct, :]
-                if ct or g:
+                if (g, ct) != (0, 0):
                     dst, src = dst.rearrange("p (r a) -> p r a", a=2), src.rearrange("p (a r) -> p r a", a=2)
                 nc.scalar.activation(
                     out=dst,
@@ -264,9 +268,9 @@ def tile_mppi_control_update_s13_kernel(tc, x_bytes, x_scale, w, base, ratio, ep
                 op=ALU.mult,
             )
 
-        def turn_m(gs, ct, number, newest_first=True):
+        def turn_m(gs, ct, number):
             turned[gs, ct] = bank(number, [P, len(gs), 2, P])
-            for n in reversed(range(len(gs))) if newest_first else range(len(gs)):
+            for n in reversed(range(len(gs))):
                 for u in range(2):
                     nc.tensor.transpose(turned[gs, ct][:, n, u, :], scaled[gs[n], ct][:, u, :].bitcast(F32), ident[:])
 
@@ -277,21 +281,26 @@ def tile_mppi_control_update_s13_kernel(tc, x_bytes, x_scale, w, base, ratio, ep
                 in_=turned[gs, ct][:].rearrange("p n u m -> p n m u"),
             )
 
+        first_chunk = {}
+
         def turn_expo(number):
-            turned[0] = bank(number, [P, NT, P])
+            first_chunk["turned"] = bank(number, [P, NT, P])
             for t in range(NT):
-                nc.tensor.transpose(turned[0][:, t, :], expo[0, 0][:, P * t : P * (t + 1)], ident[:])
+                nc.tensor.transpose(first_chunk["turned"][:, t, :], expo[0, 0][:, P * t : P * (t + 1)], ident[:])
 
         def ratio_on_scalar():
-            scaled[0, 0] = buf("planes", 1, [P, NT, P], BF16)
+            first_chunk["planes"] = buf("planes", 1, [P, NT, P], BF16)
             for t in range(NT):
                 nc.scalar.activation(
-                    out=scaled[0, 0][:, t, :], in_=turned[0][:, t, :], func=ACT.Copy, scale=ratio_f32[:, t : t + 1]
+                    out=first_chunk["planes"][:, t, :],
+                    in_=first_chunk["turned"][:, t, :],
+                    func=ACT.Copy,
+                    scale=ratio_f32[:, t : t + 1],
                 )
 
         def group_on_scalar():
             grouped_m[(0,), 0] = buf("grouped_m", 4, [P, P, 4], BF16)
-            nc.scalar.copy(out=grouped_m[(0,), 0][:], in_=scaled[0, 0][:].rearrange("p t m -> p m t"))
+            nc.scalar.copy(out=grouped_m[(0,), 0][:], in_=first_chunk["planes"][:].rearrange("p t m -> p m t"))
 
         def minus_base(g, ct):
             e = ct - 2
@@ -331,16 +340,14 @@ def tile_mppi_control_update_s13_kernel(tc, x_bytes, x_scale, w, base, ratio, ep
                 in_=grouped_m[gs, ct][:, P * first : P * (first + count), :].rearrange("p c j -> p (c j)"),
             )
 
-        acc, done = {}, {}
+        acc = {}
         wide = [slice(NB * dt, NB * (dt + 1)) for dt in range(ND)]
         narrow = [slice(D - NB + P * n, D - NB + P * (n + 1)) for n in range(NB // P)]
         out_rows = out.rearrange("(h p e) d -> h e p d", p=P, e=2)
 
         def product2(ct, ds, g, number):
-            key = (ct, ds.start)
-            done[key] = done.get(key, 0) + 1
-            if done[key] == 1:
-                acc[key] = bank(number, [P, ds.stop - ds.start])
+            if g == 0:
+                acc[ct, ds.start] = bank(number, [P, ds.stop - ds.start])
             cols = slice(P * g, P * (g + 1))
             nc.tensor.matmul_mx(
                 out=acc[ct, ds.start][:],
@@ -348,8 +355,8 @@ def tile_mppi_control_update_s13_kernel(tc, x_bytes, x_scale, w, base, ratio, ep
                 lhsT_scale=m_scales[ct][:, cols],
                 rhs=e_words[g][:, 2 * ds.start : 2 * ds.stop].bitcast(FP4X4),
                 rhs_scale=e_scales[:, g, ds],
-                start=(done[key] == 1),
-                stop=(done[key] == NG),
+                start=(g == 0),
+                stop=(g == NG - 1),
             )
 
         def finish(ct, ds, engine, parts=1):
@@ -379,97 +386,95 @@ def tile_mppi_control_update_s13_kernel(tc, x_bytes, x_scale, w, base, ratio, ep
         quantise_w(0, slice(0, C))
         quantise_w(1, slice(0, PAIR))
         quantise_x(0)
-        costs_by_goal(0, 2)
+        costs_by_goal(0, COST_BANKS[0])
         exponentials(0)
         scale_x(2, 0)
         quantise_w(1, slice(PAIR, C))
-        costs_by_rollout(0, 3)
+        costs_by_rollout(0, COST_BANKS[1])
         keep_costs(0)
         ratio_f32 = buf("ratio_f32", 1, [P, NT], F32)
         nc.scalar.copy(out=ratio_f32[:], in_=ratio_own[:, 0, :])
+
         for j in range(2, end):
             g, odd = divmod(j, 2)
             scale_x(j, 1)
             if j == 3:
-                turn_expo(HELD_BANK + 3)
+                turn_expo(HELD_BANK + ND - 1)
                 ratio_on_scalar()
             turn_x(j, 0)
             turn_x(j, 1)
             empty_x(j, 0)
             if j == 3:
                 group_on_scalar()
-            if odd and j > 3:
-                times_ratio(g - 1, 0)
-                turn_m((g - 1,), 0, 3)
-                empty_m((g - 1,), 0)
-            if j in (4,):
-                quantise_m((g - 2,), 0)
-                held_passes(g - 2, (0, 1))
+            if j == 5:
+                times_ratio(1, 0)
+                turn_m((1,), 0, COST_BANKS[1])
+                empty_m((1,), 0)
+            if j == 4:
+                quantise_m((0,), 0)
+                held_passes(0, (0, 1))
             quantise_x(j - 1)
             empty_x(j, 1)
             scale_x(j + 1, 0)
-            if odd:
-                if j + 1 not in (4,):
-                    quantise_m((g - 1,), 0)
-                if g >= 2:
-                    held_passes(g - 2, (3,))
-            costs_by_goal(j - 1, 2 if odd else 3)
             if j == 5:
-                order_x(6, 0)
+                quantise_m((1,), 0)
+                held_passes(0, (3,))
+            costs_by_goal(j - 1, COST_BANKS[1 - odd])
+            if j + 1 == ORDERED_UNIT:
+                order_x(j + 1, 0)
             exponentials(j - 1)
-            costs_by_rollout(j - 1, 3 if odd else 2)
+            costs_by_rollout(j - 1, COST_BANKS[odd])
             keep_costs(j - 1)
-            if odd:
-                if j + 1 not in (4,):
-                    held_passes(g - 1, (0, 1))
-            elif g >= 2:
+            if j == 5:
+                held_passes(1, (0, 1))
+            if j in (4, 6):
                 held_passes(g - 2, (2,))
 
         scale_x(end, 1, NQ)
         turn_x(end, 0)
         empty_x(end, 0)
-        for q in range(NQ):
-            turn_x(end, 1, (q,), 1 + 2 * q)
+        for q, number in enumerate((X_BANKS[1], COST_BANKS[1])):
+            turn_x(end, 1, (q,), number)
             empty_x(end, 1, (q,))
         times_ratio(2, 0)
-        turn_m((2,), 0, 2)
+        turn_m((2,), 0, COST_BANKS[0])
         empty_m((2,), 0)
         quantise_x(end - 1)
         held_passes(1, (3,))
-        costs_by_goal(end - 1, 0)
+        costs_by_goal(end - 1, X_BANKS[0])
         exponentials(end - 1)
-        costs_by_rollout(end - 1, 1)
+        costs_by_rollout(end - 1, X_BANKS[1])
         keep_costs(end - 1)
+
         early, late = (0, 1), (2, last)
-        end = 2 * NG - 1
         times_ratio(0, 1)
-        quantise_x(end, 0, UNIT)
-        quantise_x(end, UNIT, UNIT)
-        quantise_m((last - 1,), 0)
+        for q in range(NQ):
+            quantise_x(end, UNIT * q, UNIT)
+        quantise_m((2,), 0)
         times_ratio(1, 1)
         times_ratio(2, 1)
-        costs_by_goal(end, 3)
+        costs_by_goal(end, COST_BANKS[1])
         exponentials(end)
-        costs_by_rollout(end, 2)
-        turn_m(early, 1, 0)
+        costs_by_rollout(end, COST_BANKS[0])
+        turn_m(early, 1, X_BANKS[0])
         empty_m(early, 1)
         keep_costs(end)
-        held_passes(last - 1, range(ND))
+        held_passes(2, range(ND))
         minus_base(0, 2)
         times_ratio(last, 0)
         times_ratio(last, 1)
         quantise_m(early, 1)
         minus_base(1, 2)
 
-        banks = (2, 0, 1, 3, 5, 4, 7, 6, 2, 0, 1)
+        banks = {1: (2, 0, 1, 3), 2: (5, 4, 7, 6), 3: (2, 0, 1)}
 
         def passes(ct, dts, gs):
             for dt in dts:
                 for g in gs:
-                    product2(ct, wide[dt], g, banks[ND * (ct - 1) + dt])
+                    product2(ct, wide[dt], g, banks[ct][dt])
 
-        turn_m((last,), 0, 1)
-        turn_m(late, 1, 3)
+        turn_m((last,), 0, X_BANKS[1])
+        turn_m(late, 1, COST_BANKS[1])
         late_exponential(0, 2)
         empty_m((last,), 0)
         empty_m(late, 1)
@@ -483,10 +488,9 @@ def tile_mppi_control_update_s13_kernel(tc, x_bytes, x_scale, w, base, ratio, ep
         passes(1, (0, 1), late)
         passes(1, (2, 3), range(NG))
 
-        finish(0, wide[0], "scalar")
-        late_exponential(2, 2)
-        finish(0, wide[1], "scalar")
-        late_exponential(last, 2)
+        for n in range(2):
+            finish(0, wide[n], "scalar")
+            late_exponential(late[n], 2)
         for n in range(2):
             late_ratio(early, n, 2)
         late_ratio(late, 0, 2)

@@ -30,7 +30,7 @@ X_BANKS = (0, 1)
 COST_BANKS = (2, 3)
 HELD_BANK = 4
 M_SCALES_START, E_WORDS_START, E_SCALES_START = 64, 128, 192
-ORDERED_UNIT = 6
+ORD = (6,)
 
 FLOPS = 2 * S * F * C + 2 * C * S * D
 
@@ -63,10 +63,10 @@ def tile_mppi_control_update_s13_kernel(tc, x_bytes, x_scale, w, base, ratio, ep
 
         ident = buf("ident", 1, [P, P], F32)
         make_identity(nc, ident[:])
-        ident_bf = buf("ident_bf", 1, [P, P], BF16)
-        nc.vector.tensor_copy(out=ident_bf[:], in_=ident[:])
         e_plane = shifted("e_scales", 1, NG * D, E_SCALES_START)
         nc.vector.memset(e_plane.bitcast(I32), 0)
+        ident_bf = buf("ident_bf", 1, [P, P], BF16)
+        nc.vector.tensor_copy(out=ident_bf[:], in_=ident[:])
         e_scales = e_plane.rearrange("p (g n) -> p g n", g=NG)
 
         x_rows = x_bytes.rearrange("(g p t) k -> g p t k", p=P, t=NT)
@@ -115,14 +115,16 @@ def tile_mppi_control_update_s13_kernel(tc, x_bytes, x_scale, w, base, ratio, ep
         xs_all = buf("xs_all", 1, [P, F], F32)
         for a in range(XS_PARTS):
             spread = bank(HELD_BANK + a, [P, 2, P])
+            repeated = xs[a // 2][:, a % 2, :].rearrange("p (e o) -> p e o", o=1).to_broadcast([P, 2, P])
+            if a > 0:
+                written = buf("repeated", XS_PARTS - 1, [P, 2, P], F32)
+                nc.vector.tensor_copy(out=written[:], in_=repeated)
+                repeated = written
             for e in range(2):
-                nc.tensor.transpose(spread[:, e, :], xs[a // 2][:, a % 2, e : e + 1].to_broadcast([P, P]), ident[:])
+                nc.tensor.transpose(spread[:, e, :], repeated[:, e, :], ident[:])
             dst = xs_all[:, 2 * P * a : 2 * P * (a + 1)].rearrange("m (p e) -> m p e", e=2)
             src = spread[:].rearrange("m e p -> m p e")
-            if a < XS_PARTS // 2:
-                nc.vector.tensor_copy(out=dst, in_=src)
-            else:
-                nc.scalar.activation(out=dst, in_=src, func=ACT.Copy)
+            nc.scalar.activation(out=dst, in_=src, func=ACT.Copy)
 
         w_grouped = [buf("w_grouped", NQ, [P, C, 4], BF16) for q in range(NQ)]
         w_codes = [buf("w_codes", NQ, [P, C], U32) for q in range(NQ)]
@@ -136,8 +138,8 @@ def tile_mppi_control_update_s13_kernel(tc, x_bytes, x_scale, w, base, ratio, ep
             for e in range(2):
                 nc.tensor.matmul(grouped[:, e, :], lhsT=ident_bf[:], rhs=w_by_tile(q)[:, pair, e], start=True, stop=True)
             nc.scalar.copy(
-                out=w_grouped[q][:, PAIR * pair : PAIR * (pair + 1), :].rearrange("p c j -> p (c j)"),
-                in_=grouped[:].rearrange("p e n -> p (e n)"),
+                out=w_grouped[q][:, PAIR * pair : PAIR * (pair + 1), :].rearrange("p c j -> p (c j)").bitcast(F32),
+                in_=grouped[:].rearrange("p e n -> p (e n)").bitcast(F32),
             )
 
         def group_w_on_scalar(q, pair):
@@ -420,7 +422,7 @@ def tile_mppi_control_update_s13_kernel(tc, x_bytes, x_scale, w, base, ratio, ep
                 quantise_m((1,), 0)
                 held_passes(0, (3,))
             costs_by_goal(j - 1, COST_BANKS[1 - odd])
-            if j + 1 == ORDERED_UNIT:
+            if j + 1 in ORD:
                 order_x(j + 1, 0)
             exponentials(j - 1)
             costs_by_rollout(j - 1, COST_BANKS[odd])

@@ -30,7 +30,7 @@ X_BANKS = (0, 1)
 COST_BANKS = (2, 3)
 HELD_BANK = 4
 M_SCALES_START, E_WORDS_START, E_SCALES_START = 64, 128, 192
-ORD = (6,)
+ORDERED_UNITS = (6,)
 
 FLOPS = 2 * S * F * C + 2 * C * S * D
 
@@ -62,11 +62,12 @@ def tile_mppi_control_update_s13_kernel(tc, x_bytes, x_scale, w, base, ratio, ep
         nc.sync.dma_start(out=xs[0][:], in_=xs_parts[:, : XS_PARTS // 2])
 
         ident = buf("ident", 1, [P, P], F32)
-        make_identity(nc, ident[:])
-        e_plane = shifted("e_scales", 1, NG * D, E_SCALES_START)
-        nc.vector.memset(e_plane.bitcast(I32), 0)
+        nc.vector.memset(ident[:], 0.0)
+        make_identity(nc, ident[:], nomemset=True)
         ident_bf = buf("ident_bf", 1, [P, P], BF16)
         nc.vector.tensor_copy(out=ident_bf[:], in_=ident[:])
+        e_plane = shifted("e_scales", 1, NG * D, E_SCALES_START)
+        nc.vector.memset(e_plane[:, : (NG - 1) * D].bitcast(I32), 0)
         e_scales = e_plane.rearrange("p (g n) -> p g n", g=NG)
 
         x_rows = x_bytes.rearrange("(g p t) k -> g p t k", p=P, t=NT)
@@ -105,12 +106,6 @@ def tile_mppi_control_update_s13_kernel(tc, x_bytes, x_scale, w, base, ratio, ep
         nc.sync.dma_start(out=e_words[0], in_=eps_words[0])
         nc.sync.dma_start(out=x_rest[2][:], in_=x_rows[3])
         spread_ratio(0)
-        load_e_scales(slice(1, NG))
-        nc.sync.dma_start(out=e_words[1], in_=eps_words[1])
-        spread_ratio(1)
-        nc.sync.dma_start(out=base_all[:], in_=base[PAIR:].partition_broadcast(P))
-        for g in range(2, NG):
-            nc.sync.dma_start(out=e_words[g], in_=eps_words[g])
 
         xs_all = buf("xs_all", 1, [P, F], F32)
         for a in range(XS_PARTS):
@@ -125,6 +120,14 @@ def tile_mppi_control_update_s13_kernel(tc, x_bytes, x_scale, w, base, ratio, ep
             dst = xs_all[:, 2 * P * a : 2 * P * (a + 1)].rearrange("m (p e) -> m p e", e=2)
             src = spread[:].rearrange("m e p -> m p e")
             nc.scalar.activation(out=dst, in_=src, func=ACT.Copy)
+
+        nc.vector.memset(e_plane[:, (NG - 1) * D :].bitcast(I32), 0)
+        load_e_scales(slice(1, NG))
+        nc.sync.dma_start(out=e_words[1], in_=eps_words[1])
+        spread_ratio(1)
+        nc.sync.dma_start(out=base_all[:], in_=base[PAIR:].partition_broadcast(P))
+        for g in range(2, NG):
+            nc.sync.dma_start(out=e_words[g], in_=eps_words[g])
 
         w_grouped = [buf("w_grouped", NQ, [P, C, 4], BF16) for q in range(NQ)]
         w_codes = [buf("w_codes", NQ, [P, C], U32) for q in range(NQ)]
@@ -422,7 +425,7 @@ def tile_mppi_control_update_s13_kernel(tc, x_bytes, x_scale, w, base, ratio, ep
                 quantise_m((1,), 0)
                 held_passes(0, (3,))
             costs_by_goal(j - 1, COST_BANKS[1 - odd])
-            if j + 1 in ORD:
+            if j + 1 in ORDERED_UNITS:
                 order_x(j + 1, 0)
             exponentials(j - 1)
             costs_by_rollout(j - 1, COST_BANKS[odd])

@@ -61,6 +61,15 @@ def tile_mppi_control_update_s13_kernel(tc, x_bytes, x_scale, w, base, ratio, ep
         xs = [buf("xs", 2, [P, XS_PARTS // 2, 2], F32) for half in range(2)]
         nc.sync.dma_start(out=xs[0][:], in_=xs_parts[:, : XS_PARTS // 2])
 
+        idle = buf("idle", 1, [P, NB], BF16)
+        nc.vector.memset(idle[:].bitcast(I32), 0)
+
+        def warm_up(count):
+            unread = bank(COST_BANKS[1], [P, NB])
+            for n in range(count):
+                nc.tensor.matmul(unread[:], lhsT=idle[:, :P], rhs=idle[:], start=True, stop=True)
+
+        warm_up(3)
         ident = buf("ident", 1, [P, P], F32)
         nc.vector.memset(ident[:], 0.0)
         make_identity(nc, ident[:], nomemset=True)
@@ -128,6 +137,8 @@ def tile_mppi_control_update_s13_kernel(tc, x_bytes, x_scale, w, base, ratio, ep
         nc.sync.dma_start(out=base_all[:], in_=base[PAIR:].partition_broadcast(P))
         for g in range(2, NG):
             nc.sync.dma_start(out=e_words[g], in_=eps_words[g])
+
+        warm_up(2)
 
         w_grouped = [buf("w_grouped", NQ, [P, C, 4], BF16) for q in range(NQ)]
         w_codes = [buf("w_codes", NQ, [P, C], U32) for q in range(NQ)]

@@ -64,12 +64,12 @@ def tile_mppi_control_update_s13_kernel(tc, x_bytes, x_scale, w, base, ratio, ep
         idle = buf("idle", 1, [P, NB], BF16)
         nc.vector.memset(idle[:].bitcast(I32), 0)
 
-        def warm_up(count):
-            unread = bank(COST_BANKS[1], [P, NB])
+        def warm_up(count, number):
+            unread = bank(number, [P, NB])
             for n in range(count):
                 nc.tensor.matmul(unread[:], lhsT=idle[:, :P], rhs=idle[:], start=True, stop=True)
 
-        warm_up(3)
+        warm_up(3, COST_BANKS[1])
         ident = buf("ident", 1, [P, P], F32)
         nc.vector.memset(ident[:], 0.0)
         make_identity(nc, ident[:], nomemset=True)
@@ -138,7 +138,7 @@ def tile_mppi_control_update_s13_kernel(tc, x_bytes, x_scale, w, base, ratio, ep
         for g in range(2, NG):
             nc.sync.dma_start(out=e_words[g], in_=eps_words[g])
 
-        warm_up(2)
+        warm_up(2, COST_BANKS[1])
 
         w_grouped = [buf("w_grouped", NQ, [P, C, 4], BF16) for q in range(NQ)]
         w_codes = [buf("w_codes", NQ, [P, C], U32) for q in range(NQ)]
@@ -147,18 +147,27 @@ def tile_mppi_control_update_s13_kernel(tc, x_bytes, x_scale, w, base, ratio, ep
         def w_by_tile(q):
             return w_raw[q][:].rearrange("p j (h m e) -> p h e m j", m=P, e=2)
 
-        def group_w_on_tensor(q, pair, number):
+        w_banks = {}
+
+        def group_w_on_tensor(q, pair, number, later=False):
             grouped = bank(number, [P, 2, KP], BF16)
             for e in range(2):
                 nc.tensor.matmul(grouped[:, e, :], lhsT=ident_bf[:], rhs=w_by_tile(q)[:, pair, e], start=True, stop=True)
+            w_banks[q, pair] = grouped
+            if not later:
+                empty_w(q, pair)
+
+        def empty_w(q, pair):
+            grouped = w_banks[q, pair]
             nc.scalar.copy(
                 out=w_grouped[q][:, PAIR * pair : PAIR * (pair + 1), :].rearrange("p c j -> p (c j)").bitcast(F32),
                 in_=grouped[:].rearrange("p e n -> p (e n)").bitcast(F32),
             )
 
         def group_w_on_scalar(q, pair):
-            dst = w_grouped[q][:].rearrange("p (h e m) j -> p h e m j", m=P, e=2)
-            nc.scalar.copy(out=dst[:, pair], in_=w_by_tile(q)[:, pair])
+            dst = w_grouped[q][:].rearrange("p (h e b i) j -> p h b j i e", h=2, e=2, i=2)
+            src = w_raw[q][:].rearrange("p j (h b i e) -> p h b j i e", h=2, e=2, i=2)
+            nc.scalar.copy(out=dst[:, pair], in_=src[:, pair])
 
         def quantise_w(q, cols):
             nc.vector.quantize_mx(
@@ -316,7 +325,10 @@ def tile_mppi_control_update_s13_kernel(tc, x_bytes, x_scale, w, base, ratio, ep
 
         def group_on_scalar():
             grouped_m[(0,), 0] = buf("grouped_m", 4, [P, P, 4], BF16)
-            nc.scalar.copy(out=grouped_m[(0,), 0][:], in_=first_chunk["planes"][:].rearrange("p t m -> p m t"))
+            nc.scalar.copy(
+                out=grouped_m[(0,), 0][:].rearrange("p (b i) t -> p b t i", i=4),
+                in_=first_chunk["planes"][:].rearrange("p t (b i) -> p b t i", i=4),
+            )
 
         def minus_base(g, ct):
             e = ct - 2
@@ -417,8 +429,8 @@ def tile_mppi_control_update_s13_kernel(tc, x_bytes, x_scale, w, base, ratio, ep
             if j == 3:
                 turn_expo(HELD_BANK + ND - 1)
                 ratio_on_scalar()
-            turn_x(j, 0)
-            turn_x(j, 1)
+            for a in range(2):
+                turn_x(j, a, number=HELD_BANK + 1 + a if j == 3 else None)
             empty_x(j, 0)
             if j == 3:
                 group_on_scalar()
@@ -495,8 +507,8 @@ def tile_mppi_control_update_s13_kernel(tc, x_bytes, x_scale, w, base, ratio, ep
         empty_m((last,), 0)
         empty_m(late, 1)
         passes(1, (0, 1), early)
-        quantise_m((last,), 0)
         minus_base(2, 2)
+        quantise_m((last,), 0)
         quantise_m(late, 1)
         minus_base(last, 2)
         late_exponential(1, 2)
@@ -522,9 +534,9 @@ def tile_mppi_control_update_s13_kernel(tc, x_bytes, x_scale, w, base, ratio, ep
             finish(1, wide[dt], "scalar")
         for g in early:
             late_exponential(g, 3)
+        late_exponential(2, 3)
         finish(1, wide[2], "scalar")
-        for g in late:
-            late_exponential(g, 3)
+        late_exponential(last, 3)
         finish(1, wide[3], "scalar")
         passes(2, (0, 1), early)
         passes(2, (0, 1), late)

from contextlib import ExitStack

import concourse.mybir as mybir
from concourse.masks import make_identity

F32 = mybir.dt.float32
BF16 = mybir.dt.bfloat16
U32 = mybir.dt.uint32
I32 = mybir.dt.int32
U8 = mybir.dt.uint8
FP8 = mybir.dt.float8_e4m3fn
FP8X4 = mybir.dt.float8_e4m3fn_x4
FP4X4 = mybir.dt.float4_e2m1fn_x4
ALU = mybir.AluOpType
ACT = mybir.ActivationFunctionType

P = 128
S, F, C, D = 2048, 1024, 512, 2048
KP = 512
NG = S // KP
NQ = F // KP
NT = 4
NC = C // P
NB = 512
ND = D // NB
UNIT = KP // 2
PAIR = C // 2
XS_PARTS = 4
X_BANKS = (0, 1)
COST_BANKS = (2, 3)
HELD_BANK = 4
M_SCALES_START, E_WORDS_START, E_SCALES_START = 64, 128, 192
ORDERED_UNITS = (6,)

FLOPS = 2 * S * F * C + 2 * C * S * D


def tile_mppi_control_update_s13_kernel(tc, x_bytes, x_scale, w, base, ratio, eps_words, eps_scales, out):
    nc = tc.nc
    with ExitStack() as ctx:
        sb = ctx.enter_context(tc.tile_pool(name="sb", bufs=1))
        psum = ctx.enter_context(tc.psum_pool(name="psum", bufs=1))
        ctx.enter_context(tc.manual_schedule())

        def buf(tag, bufs, shape, dtype):
            return sb.tile(shape, dtype, name=tag, tag=tag, bufs=bufs, align_bytes=256)

        def shifted(tag, bufs, width, start):
            return buf(tag, bufs, [P, start + width], U8)[:, start:]

        def bank(number, shape, dtype=F32):
            return psum.tile(shape, dtype, name="bank%d" % number, tag="bank%d" % number)

        def copy_on(engine, dst, src):
            if engine == "vector":
                nc.vector.tensor_copy(out=dst, in_=src)
            else:
                nc.scalar.copy(out=dst, in_=src)

        xs_parts = x_scale.rearrange("o (a p e) -> p (o a) e", p=P, e=2)
        xs = [buf("xs", 2, [P, XS_PARTS // 2, 2], F32) for half in range(2)]
        nc.sync.dma_start(out=xs[0][:], in_=xs_parts[:, : XS_PARTS // 2])

        idle = buf("idle", 1, [P, NB], BF16)
        nc.vector.memset(idle[:].bitcast(I32), 0)

        def warm_up(count, number):
            unread = bank(number, [P, NB])
            for n in range(count):
                nc.tensor.matmul(unread[:], lhsT=idle[:, :P], rhs=idle[:], start=True, stop=True)

        warm_up(3, COST_BANKS[1])
        ident = buf("ident", 1, [P, P], F32)
        nc.vector.memset(ident[:], 0.0)
        make_identity(nc, ident[:], nomemset=True)
        ident_bf = buf("ident_bf", 1, [P, P], BF16)
        nc.vector.tensor_copy(out=ident_bf[:], in_=ident[:])
        e_plane = shifted("e_scales", 1, NG * D, E_SCALES_START)
        nc.vector.memset(e_plane[:, : (NG - 1) * D].bitcast(I32), 0)
        e_scales = e_plane.rearrange("p (g n) -> p g n", g=NG)

        x_rows = x_bytes.rearrange("(g p t) k -> g p t k", p=P, t=NT)
        w_rows = w.rearrange("(q p j) c -> q p j c", p=P, j=4)
        x_first = [buf("x_first", NT, [P, F], U8) for t in range(NT)]
        x_rest = [buf("x_rest", NG - 1, [P, NT, F], U8) for g in range(1, NG)]
        w_raw = [buf("w_raw", NQ, [P, 4, C], BF16) for q in range(NQ)]
        for t in range(NT):
            nc.sync.dma_start(out=x_first[t][:], in_=x_rows[0][:, t, :])
            if t == 0:
                nc.sync.dma_start(out=xs[1][:], in_=xs_parts[:, XS_PARTS // 2 :])
            if t % 2 == 0:
                nc.sync.dma_start(out=w_raw[t // 2][:], in_=w_rows[t // 2])
        base_own = buf("base_own", 1, [P, 2], BF16)
        nc.sync.dma_start(out=base_own[:], in_=base[:PAIR].rearrange("(p e) -> p e", e=2))
        ratio_own = buf("ratio_own", 1, [P, NG, NT], BF16)
        base_all = buf("base_all", 1, [P, PAIR], BF16)
        ratio_all = [buf("ratio_all", 2, [P, 2 * KP], BF16) for half in range(2)]

        def spread_ratio(half):
            nc.sync.dma_start(out=ratio_all[half][:], in_=ratio[2 * KP * half : 2 * KP * (half + 1)].partition_broadcast(P))

        e_rows = eps_scales.bitcast(I32).rearrange("g q n -> q g n")
        e_words = [shifted("e_words", NG, 2 * D, E_WORDS_START) for g in range(NG)]

        def load_e_scales(gs):
            for quad in range(4):
                nc.sync.dma_start(
                    out=e_scales[32 * quad : 32 * quad + 4, gs, :].bitcast(I32), in_=e_rows[4 * quad : 4 * quad + 4, gs]
                )

        nc.sync.dma_start(out=x_rest[0][:], in_=x_rows[1])
        nc.sync.dma_start(out=ratio_own[:], in_=ratio.rearrange("(g p t) -> p g t", p=P, t=NT))
        nc.sync.dma_start(out=x_rest[1][:], in_=x_rows[2])
        load_e_scales(slice(0, 1))
        nc.sync.dma_start(out=e_words[0], in_=eps_words[0])
        nc.sync.dma_start(out=x_rest[2][:], in_=x_rows[3])
        spread_ratio(0)

        xs_all = buf("xs_all", 1, [P, F], F32)
        for a in range(XS_PARTS):
            spread = bank(HELD_BANK + a, [P, 2, P])
            repeated = xs[a // 2][:, a % 2, :].rearrange("p (e o) -> p e o", o=1).to_broadcast([P, 2, P])
            if a > 0:
                written = buf("repeated", XS_PARTS - 1, [P, 2, P], F32)
                nc.vector.tensor_copy(out=written[:], in_=repeated)
                repeated = written
            for e in range(2):
                nc.tensor.transpose(spread[:, e, :], repeated[:, e, :], ident[:])
            dst = xs_all[:, 2 * P * a : 2 * P * (a + 1)].rearrange("m (p e) -> m p e", e=2)
            src = spread[:].rearrange("m e p -> m p e")
            nc.scalar.activation(out=dst, in_=src, func=ACT.Copy)

        nc.vector.memset(e_plane[:, (NG - 1) * D :].bitcast(I32), 0)
        load_e_scales(slice(1, NG))
        nc.sync.dma_start(out=e_words[1], in_=eps_words[1])
        spread_ratio(1)
        nc.sync.dma_start(out=base_all[:], in_=base[PAIR:].partition_broadcast(P))
        for g in range(2, NG):
            nc.sync.dma_start(out=e_words[g], in_=eps_words[g])

        warm_up(2, COST_BANKS[1])

        w_grouped = [buf("w_grouped", NQ, [P, C, 4], BF16) for q in range(NQ)]
        w_codes = [buf("w_codes", NQ, [P, C], U32) for q in range(NQ)]
        w_scales = [buf("w_scales", NQ, [P, C], U8) for q in range(NQ)]

        def w_by_tile(q):
            return w_raw[q][:].rearrange("p j (h m e) -> p h e m j", m=P, e=2)

        w_banks = {}

        def group_w_on_tensor(q, pair, number, later=False):
            grouped = bank(number, [P, 2, KP], BF16)
            for e in range(2):
                nc.tensor.matmul(grouped[:, e, :], lhsT=ident_bf[:], rhs=w_by_tile(q)[:, pair, e], start=True, stop=True)
            w_banks[q, pair] = grouped
            if not later:
                empty_w(q, pair)

        def empty_w(q, pair):
            grouped = w_banks[q, pair]
            nc.scalar.copy(
                out=w_grouped[q][:, PAIR * pair : PAIR * (pair + 1), :].rearrange("p c j -> p (c j)").bitcast(F32),
                in_=grouped[:].rearrange("p e n -> p (e n)").bitcast(F32),
            )

        def group_w_on_scalar(q, pair):
            dst = w_grouped[q][:].rearrange("p (h e b i) j -> p h b j i e", h=2, e=2, i=2)
            src = w_raw[q][:].rearrange("p j (h b i e) -> p h b j i e", h=2, e=2, i=2)
            nc.scalar.copy(out=dst[:, pair], in_=src[:, pair])

        def quantise_w(q, cols):
            nc.vector.quantize_mx(
                out=w_codes[q][:, cols].bitcast(FP8X4),
                scales=w_scales[q][:, cols],
                in_=w_grouped[q][:, cols, :].rearrange("p c j -> p (c j)"),
            )

        x_scaled, x_ordered, x_turned, x_grouped, x_codes, x_scales = {}, {}, {}, {}, {}, {}

        def scale_x(j, a, parts=1):
            g, t = divmod(2 * j + a, NT)
            x_scaled[j, a] = buf("x_scaled", 4, [P, F], BF16)
            src = x_first[t][:] if g == 0 else x_rest[g - 1][:, t, :]
            for part in range(parts):
                ks = slice(F // parts * part, F // parts * (part + 1))
                nc.vector.tensor_tensor(
                    out=x_scaled[j, a][:, ks], in0=src[:, ks].bitcast(FP8), in1=xs_all[:, ks], op=ALU.mult
                )

        def turn_x(j, a, qs=(0, 1), number=None):
            x_turned[j, a, qs] = bank(X_BANKS[a] if number is None else number, [P, len(qs), 2, P])
            words = x_scaled[j, a][:].bitcast(F32)
            for n in range(len(qs)):
                for u in range(2):
                    first = 256 * qs[n]
                    if (j, a) in x_ordered:
                        src = x_ordered[j, a][:, qs[n], u, :]
                    else:
                        src = words[:, first + u : first + 256 : 2]
                    nc.tensor.transpose(x_turned[j, a, qs][:, n, u, :], src, ident[:])

        def order_x(j, a):
            x_ordered[j, a] = buf("x_ordered", 2, [P, NQ, 2, P], F32)
            nc.scalar.copy(
                out=x_ordered[j, a][:], in_=x_scaled[j, a][:].bitcast(F32).rearrange("p (q i u) -> p q u i", q=NQ, u=2)
            )

        def empty_x(j, a, qs=(0, 1)):
            if j not in x_grouped:
                x_grouped[j] = buf("x_grouped", 3, [P, NQ, UNIT, 4], BF16)
            nc.scalar.copy(
                out=x_grouped[j][:, qs[0] : qs[-1] + 1, P * a : P * (a + 1), :].bitcast(F32),
                in_=x_turned[j, a, qs][:].rearrange("p q u r -> p q r u"),
            )

        def quantise_x(j, first=0, count=NQ * UNIT):
            if first == 0:
                x_codes[j] = buf("x_codes", 3, [P, NQ * UNIT], U32)
                x_scales[j] = buf("x_scales", 3, [P, NQ * UNIT], U8)
            nc.vector.quantize_mx(
                out=x_codes[j][:, first : first + count].bitcast(FP8X4),
                scales=x_scales[j][:, first : first + count],
                in_=x_grouped[j][:].rearrange("p q r j -> p (q r j)")[:, 4 * first : 4 * (first + count)],
            )

        by_goal, by_rollout, expo, kept, diff, scaled, turned, grouped_m = {}, {}, {}, {}, {}, {}, {}, {}
        m_codes = [buf("m_codes", NC, [P, NG * P], U32) for ct in range(NC)]
        m_scales = [shifted("m_scales", NC, NG * P, M_SCALES_START) for ct in range(NC)]

        def cost_group(dst, still, moving):
            for q in range(NQ):
                nc.tensor.matmul_mx(
                    out=dst,
                    lhsT=still(q)[0].bitcast(FP8X4),
                    lhsT_scale=still(q)[1],
                    rhs=moving(q)[0].bitcast(FP8X4),
                    rhs_scale=moving(q)[1],
                    start=(q == 0),
                    stop=(q == NQ - 1),
                )

        def w_cols(first, n):
            return lambda q: (w_codes[q][:, first : first + n], w_scales[q][:, first : first + n])

        def x_cols(j, first, n):
            def cols(q):
                rows = slice(UNIT * q + first, UNIT * q + first + n)
                return x_codes[j][:, rows], x_scales[j][:, rows]

            return cols

        def costs_by_goal(j, number):
            by_goal[j] = bank(number, [P, 2, UNIT])
            for ct in range(2):
                cost_group(by_goal[j][:, ct, :], w_cols(P * ct, P), x_cols(j, 0, UNIT))

        def exponentials(j):
            g, h = divmod(j, 2)
            cost = by_goal[j]
            for ct in range(2):
                if h == 0:
                    expo[g, ct] = buf("expo", 3 * NG, [P, KP], F32)
                dst, src = expo[g, ct][:, UNIT * h : UNIT * (h + 1)], cost[:, ct, :]
                if (g, ct) != (0, 0):
                    dst, src = dst.rearrange("p (r a) -> p r a", a=2), src.rearrange("p (a r) -> p r a", a=2)
                nc.scalar.activation(
                    out=dst,
                    in_=src,
                    func=ACT.Exp,
                    bias=base_own[:, ct : ct + 1],
                    scale=-1.0,
                )

        def costs_by_rollout(j, number):
            by_rollout[j] = bank(number, [P, 2, PAIR])
            for a in range(2):
                cost_group(by_rollout[j][:, a, :], x_cols(j, P * a, P), w_cols(PAIR, PAIR))

        def keep_costs(j):
            g, h = divmod(j, 2)
            cost = by_rollout[j]
            if h == 0:
                kept[g] = buf("kept", NG, [P, 2, PAIR, 2], F32)
            nc.scalar.copy(out=kept[g][:, h], in_=cost[:].rearrange("p a c -> p c a"))

        def times_ratio(g, ct):
            scaled[g, ct] = buf("scaled", 6, [P, 2, UNIT], BF16)
            nc.vector.tensor_tensor(
                out=scaled[g, ct][:].rearrange("p u (i e) -> p u i e", e=2),
                in0=expo[g, ct][:].rearrange("p (u i e) -> p u i e", u=2, e=2),
                in1=ratio_all[g // 2][:, KP * (g % 2) : KP * (g % 2 + 1)].rearrange("p (i u e) -> p u i e", u=2, e=2),
                op=ALU.mult,
            )

        def turn_m(gs, ct, number):
            turned[gs, ct] = bank(number, [P, len(gs), 2, P])
            for n in reversed(range(len(gs))):
                for u in range(2):
                    nc.tensor.transpose(turned[gs, ct][:, n, u, :], scaled[gs[n], ct][:, u, :].bitcast(F32), ident[:])

        def empty_m(gs, ct):
            grouped_m[gs, ct] = buf("grouped_m", 4, [P, len(gs) * P, 4], BF16)
            nc.scalar.copy(
                out=grouped_m[gs, ct][:].bitcast(F32).rearrange("p (n m) u -> p n m u", n=len(gs)),
                in_=turned[gs, ct][:].rearrange("p n u m -> p n m u"),
            )

        first_chunk = {}

        def turn_expo(number):
            first_chunk["turned"] = bank(number, [P, NT, P])
            for t in range(NT):
                nc.tensor.transpose(first_chunk["turned"][:, t, :], expo[0, 0][:, P * t : P * (t + 1)], ident[:])

        def ratio_on_scalar():
            first_chunk["planes"] = buf("planes", 1, [P, NT, P], BF16)
            for t in range(NT):
                nc.scalar.activation(
                    out=first_chunk["planes"][:, t, :],
                    in_=first_chunk["turned"][:, t, :],
                    func=ACT.Copy,
                    scale=ratio_f32[:, t : t + 1],
                )

        def group_on_scalar():
            grouped_m[(0,), 0] = buf("grouped_m", 4, [P, P, 4], BF16)
            nc.scalar.copy(
                out=grouped_m[(0,), 0][:].rearrange("p (b i) t -> p b t i", i=4),
                in_=first_chunk["planes"][:].rearrange("p t (b i) -> p b t i", i=4),
            )

        def minus_base(g, ct):
            e = ct - 2
            diff[g, ct] = buf("diff", 6, [P, 2, P, 2], F32)
            nc.vector.tensor_tensor(
                out=diff[g, ct][:],
                in0=kept[g][:, :, P * e : P * (e + 1), :],
                in1=base_all[:].rearrange("p (m e a) -> p e m a", e=2, a=1)[:, e : e + 1].to_broadcast([P, 2, P, 2]),
                op=ALU.subtract,
            )

        def late_exponential(g, ct):
            expo[g, ct] = buf("expo", 3 * NG, [P, KP], F32)
            nc.scalar.activation(
                out=expo[g, ct][:].rearrange("p (m h a) -> p m h a", h=2, a=2),
                in_=diff[g, ct][:].rearrange("p h m a -> p m h a"),
                func=ACT.Exp,
                scale=-1.0,
            )

        def late_ratio(gs, n, ct):
            if n == 0:
                grouped_m[gs, ct] = buf("grouped_m", 4, [P, 2 * P, 4], BF16)
            nc.vector.tensor_tensor(
                out=grouped_m[gs, ct][:, P * n : P * (n + 1), :],
                in0=expo[gs[n], ct][:].rearrange("p (m t) -> p m t", t=NT),
                in1=ratio_own[:, gs[n] : gs[n] + 1, :].to_broadcast([P, P, NT]),
                op=ALU.mult,
            )

        def quantise_m(gs, ct, only=None):
            first, count = (0, len(gs)) if only is None else (only, 1)
            cols = slice(P * gs[first], P * (gs[first] + count))
            nc.vector.quantize_mx(
                out=m_codes[ct][:, cols].bitcast(FP8X4),
                scales=m_scales[ct][:, cols],
                in_=grouped_m[gs, ct][:, P * first : P * (first + count), :].rearrange("p c j -> p (c j)"),
            )

        acc = {}
        wide = [slice(NB * dt, NB * (dt + 1)) for dt in range(ND)]
        narrow = [slice(D - NB + P * n, D - NB + P * (n + 1)) for n in range(NB // P)]
        out_rows = out.rearrange("(h p e) d -> h e p d", p=P, e=2)

        def product2(ct, ds, g, number):
            if g == 0:
                acc[ct, ds.start] = bank(number, [P, ds.stop - ds.start])
            cols = slice(P * g, P * (g + 1))
            nc.tensor.matmul_mx(
                out=acc[ct, ds.start][:],
                lhsT=m_codes[ct][:, cols].bitcast(FP8X4),
                lhsT_scale=m_scales[ct][:, cols],
                rhs=e_words[g][:, 2 * ds.start : 2 * ds.stop].bitcast(FP4X4),
                rhs_scale=e_scales[:, g, ds],
                start=(g == 0),
                stop=(g == NG - 1),
            )

        def finish(ct, ds, engine, parts=1):
            width = (ds.stop - ds.start) // parts
            for part in range(parts):
                res = buf("res", NC * ND + 4, [P, width], F32)
                copy_on(engine, res[:], acc[ct, ds.start][:, width * part : width * (part + 1)])
                first = ds.start + width * part
                nc.sync.dma_start(out=out_rows[ct // 2, ct % 2][:, first : first + width], in_=res[:])

        def held_passes(g, dts):
            for dt in dts:
                product2(0, wide[dt], g, HELD_BANK + dt)

        last = NG - 1
        end = 2 * NG - 1
        group_w_on_scalar(0, 1)
        group_w_on_tensor(0, 0, COST_BANKS[0])
        for j in range(2):
            scale_x(j, 0, XS_PARTS if j == 0 else 1)
            scale_x(j, 1)
            turn_x(j, 0)
            empty_x(j, 0)
            group_w_on_tensor(1, j, HELD_BANK + j)
            turn_x(j, 1)
            empty_x(j, 1)
        quantise_w(0, slice(0, C))
        quantise_w(1, slice(0, PAIR))
        quantise_x(0)
        costs_by_goal(0, COST_BANKS[0])
        exponentials(0)
        scale_x(2, 0)
        quantise_w(1, slice(PAIR, C))
        costs_by_rollout(0, COST_BANKS[1])
        keep_costs(0)
        ratio_f32 = buf("ratio_f32", 1, [P, NT], F32)
        nc.scalar.copy(out=ratio_f32[:], in_=ratio_own[:, 0, :])

        for j in range(2, end):
            g, odd = divmod(j, 2)
            scale_x(j, 1)
            if j == 3:
                turn_expo(HELD_BANK + ND - 1)
                ratio_on_scalar()
            for a in range(2):
                turn_x(j, a, number=HELD_BANK + 1 + a if j == 3 else None)
            empty_x(j, 0)
            if j == 3:
                group_on_scalar()
            if j == 5:
                times_ratio(1, 0)
                turn_m((1,), 0, COST_BANKS[1])
                empty_m((1,), 0)
            if j == 4:
                quantise_m((0,), 0)
                held_passes(0, (0, 1))
            quantise_x(j - 1)
            empty_x(j, 1)
            scale_x(j + 1, 0)
            if j == 5:
                quantise_m((1,), 0)
                held_passes(0, (3,))
            costs_by_goal(j - 1, COST_BANKS[1 - odd])
            if j + 1 in ORDERED_UNITS:
                order_x(j + 1, 0)
            exponentials(j - 1)
            costs_by_rollout(j - 1, COST_BANKS[odd])
            keep_costs(j - 1)
            if j == 5:
                held_passes(1, (0, 1))
            if j in (4, 6):
                held_passes(g - 2, (2,))

        scale_x(end, 1, NQ)
        turn_x(end, 0)
        empty_x(end, 0)
        for q, number in enumerate((X_BANKS[1], COST_BANKS[1])):
            turn_x(end, 1, (q,), number)
            empty_x(end, 1, (q,))
        times_ratio(2, 0)
        turn_m((2,), 0, COST_BANKS[0])
        empty_m((2,), 0)
        quantise_x(end - 1)
        held_passes(1, (3,))
        costs_by_goal(end - 1, X_BANKS[0])
        exponentials(end - 1)
        costs_by_rollout(end - 1, X_BANKS[1])
        keep_costs(end - 1)

        early, late = (0, 1), (2, last)
        times_ratio(0, 1)
        for q in range(NQ):
            quantise_x(end, UNIT * q, UNIT)
        quantise_m((2,), 0)
        times_ratio(1, 1)
        times_ratio(2, 1)
        costs_by_goal(end, COST_BANKS[1])
        exponentials(end)
        costs_by_rollout(end, COST_BANKS[0])
        turn_m(early, 1, X_BANKS[0])
        empty_m(early, 1)
        keep_costs(end)
        held_passes(2, range(ND))
        minus_base(0, 2)
        times_ratio(last, 0)
        times_ratio(last, 1)
        quantise_m(early, 1)
        minus_base(1, 2)

        banks = {1: (2, 0, 1, 3), 2: (5, 4, 7, 6), 3: (2, 0, 1)}

        def passes(ct, dts, gs):
            for dt in dts:
                for g in gs:
                    product2(ct, wide[dt], g, banks[ct][dt])

        turn_m((last,), 0, X_BANKS[1])
        turn_m(late, 1, COST_BANKS[1])
        late_exponential(0, 2)
        empty_m((last,), 0)
        empty_m(late, 1)
        passes(1, (0, 1), early)
        minus_base(2, 2)
        quantise_m((last,), 0)
        quantise_m(late, 1)
        minus_base(last, 2)
        late_exponential(1, 2)
        held_passes(last, range(ND))
        passes(1, (0, 1), late)
        passes(1, (2, 3), range(NG))

        for n in range(2):
            finish(0, wide[n], "scalar")
            late_exponential(late[n], 2)
        for n in range(2):
            late_ratio(early, n, 2)
        late_ratio(late, 0, 2)
        quantise_m(early, 2)
        late_ratio(late, 1, 2)
        minus_base(0, 3)
        quantise_m(late, 2)
        for g in range(1, NG):
            minus_base(g, 3)
        for dt in range(2, ND):
            finish(0, wide[dt], "scalar")
        for dt in range(2):
            finish(1, wide[dt], "scalar")
        for g in early:
            late_exponential(g, 3)
        late_exponential(2, 3)
        finish(1, wide[2], "scalar")
        late_exponential(last, 3)
        finish(1, wide[3], "scalar")
        passes(2, (0, 1), early)
        passes(2, (0, 1), late)
        passes(2, (2, 3), range(NG))
        for n in range(2):
            late_ratio(early, n, 3)
        late_ratio(late, 0, 3)
        quantise_m(early, 3)
        late_ratio(late, 1, 3)
        for n in range(2):
            quantise_m(late, 3, n)
        for dt in range(ND):
            finish(2, wide[dt], "scalar" if dt < ND - 1 else "vector")
        passes(3, (0, 1), early)
        for g in late:
            passes(3, (0, 1), (g,))
        finish(3, wide[0], "scalar")
        finish(3, wide[1], "vector")
        passes(3, (2,), range(NG))
        finish(3, wide[2], "scalar", 2)
        for n in range(NB // P):
            for g in range(NG):
                product2(3, narrow[n], g, HELD_BANK + n)
            finish(3, narrow[n], "vector" if n % 2 == 0 else "scalar")
